import numpy as np, ml_dtypes
CORES = [16,18,20,22]
N = 4
BF = ml_dtypes.bfloat16
def gentries(a):
    return np.ascontiguousarray(a.reshape(8, 16, -1).transpose(0, 2, 1)).reshape(8, -1)
def gtable(e):
    e = np.asarray(e); return np.ascontiguousarray(e.reshape(8, -1, 16).transpose(0, 2, 1)).reshape(128, -1).astype(np.int32)
def f(rng, *shape):
    return (rng.standard_normal(shape, dtype=np.float32) * np.exp2(rng.integers(-2, 3, shape[:-1] + (1,)))).astype(BF)
def wide(rng, *shape):
    v = f(rng, *shape).astype(np.float32); k = shape[:-2] + (1, shape[-1])
    return (v * np.exp2(rng.integers(-6, 7, k)) * (rng.random(k) > 0.0625)).astype(BF)
V, H, M, RO, QN = 4096, 4096, 512, 4, 7
NO = V - 1
BIG = 2.0 ** 40
def grow(rng, par, lab, keep, nn, nm):
    B, q = nm.shape[0], nm.shape[2]; b = np.arange(B); C = np.full((B, M, 16), NO, np.int64)
    for i in range(M):
        up = C[b, par[:, i]]
        cand = np.concatenate([up, nm[:, i]], axis=1)
        use = np.concatenate([(rng.random((B, 16)) < keep[:, i, None]) & (up != NO), np.arange(q)[None, :] < nn[:, i, None]], axis=1)
        o = np.argsort(np.where(use, rng.random(use.shape), 2.0), axis=1)[:, :16]
        e = np.where(np.take_along_axis(use, o, 1), np.take_along_axis(cand, o, 1), NO)
        C[:, i] = np.take_along_axis(e, np.argsort(rng.random((B, 16)), axis=1), 1)
    D = np.empty_like(C); p = np.empty((B, M), np.int64)
    D[b[:, None], lab] = C; p[b[:, None], lab] = np.take_along_axis(lab, par, 1)
    return D, p
def fresh(rng):
    return np.argsort(rng.random((8 * N, V - 1)), axis=1)[:, :M * QN].reshape(8 * N, M, QN)
def shape(rng):
    B = 8 * N; n = np.arange(M)[None, :]; u = rng.random((B, M)); kind = rng.integers(0, 4, (B, 1))
    par = np.where(kind == 0, (u * n).astype(np.int64), np.where(kind == 1, n - 1 - (u * 8).astype(np.int64), np.where(kind == 2, (u * np.minimum(n, 12)).astype(np.int64), np.where(u > 0.7, n - 2, n - 1))))
    return np.maximum(par, 0), np.argsort(rng.random((B, M)), axis=1)
def trees(rng):
    par, lab = shape(rng); B = 8 * N
    keep = rng.choice(np.array([0.4, 0.7, 0.9, 1.0]), (B, M)); nn = np.where(rng.random((B, M)) < 0.15, 0, rng.integers(0, QN + 1, (B, M))); nn[:, 0] = QN
    return grow(rng, par, lab, keep, nn, fresh(rng))
def floats(rng):
    sc = np.exp2(rng.integers(-2, 3, (N, 128, 1))).astype(np.float32)
    x = (rng.standard_normal((N, 128, V), dtype=np.float32) * sc).astype(BF)
    col = np.repeat(1.5 * np.exp2(rng.integers(-3, 3, (N, 8, H))), 16, axis=1).astype(np.float32)
    return x, (np.abs(rng.standard_normal((N, 128, H), dtype=np.float32)) * sc * col).astype(BF)
def pack(x, l, C, p, th):
    C = C.reshape(N, 8, M * 16); p = p.reshape(N, 8, M)
    return {"xs": x, "lim": l, "cq": np.stack([gtable(a) for a in C]), "pt": np.stack([gtable(a) for a in p]), "th": np.asarray(th).astype(np.int32)}
def setup_inputs(rng):
    C, p = trees(rng); x, l = floats(rng)
    return pack(x, l, C, p, rng.integers(4, 17, (N, 8, 2)))
def setup_inputs_corners(rng):
    B = 8 * N; n = np.arange(M); par, lab = shape(rng); g = np.arange(B) & 7; k = (g + np.arange(B) // 8) & 7
    par[k < 2] = np.maximum(n - 1, 0); par[(k == 2) | (k == 3)] = 0; par[k == 4] = np.maximum(n - 1, 0) // 2
    lab[(k == 0) | (k == 2) | (k == 4)] = n; lab[(k == 1) | (k == 3)] = M - 1 - n
    mode = rng.integers(0, 6, (B, M)); mode[g == 5] = 2; mode[g == 6] = 3
    keep = np.array([0.0, 0.0, 1.0, 1.0, 0.93, 0.5])[mode]; nn = np.array([0, QN, 0, QN, 1, QN])[mode]; nn[:, 0] = QN; nn[g == 7, 0] = 0
    C, p = grow(rng, par, lab, keep, nn, fresh(rng)); x, l = floats(rng)
    th = rng.choice(np.array([0, 1, 8, 15, 16]), (N, 8, 2)); th[:, 0, 0] = 0; th[:, 1, 0] = 16; th[:, 5, 1] = 8
    return pack(x, l, C, p, th)
def setup_inputs_hubs(rng):
    B = 8 * N; n = np.arange(M); h = M // 2; k = ((np.arange(B) & 7) + np.arange(B) // 8) & 7
    hub = np.where(n > 1, 1, 0); star = np.zeros_like(n); teeth = np.where(n > h, n - h + 1, 0)
    low = n.copy(); low[0] = 1; low[1] = 0
    high = (n - 2) % M; swap = high.copy(); swap[0] = M - 1; swap[1] = M - 2
    comb = np.where(n > h, 2 * (n - h) - 1, 2 * (n - 1)); comb[0] = M - 1
    par = np.stack([hub, hub, hub, hub, star, star, hub, teeth])[k]; lab = np.stack([low, swap, low, high, M - 1 - n, n, low, comb])[k]
    mode = rng.integers(0, 6, (B, M))
    keep = np.array([0.0, 0.0, 1.0, 1.0, 0.93, 0.5])[mode]; nn = np.array([0, QN, 0, QN, 1, QN])[mode]
    a = (k == 0) | (k == 1); keep[a, 2:] = 0.0; keep[a, 1] = 1.0; nn[a, 1] = QN; keep[a, M - 1] = 1.0; nn[a, M - 1] = 0
    a = k == 6; keep[a, 2:] = np.where((n[2:] >= 3 * M // 4) & (rng.random((N, M - 2)) < 0.125), 0.5, 0.0); keep[a, 1] = 1.0; nn[a, 1] = QN
    a = (k == 2) | (k == 3); keep[a, 1] = 1.0; nn[a, 1] = 0
    a = (k == 4) | (k == 5); keep[a] = 1.0; nn[a] = 0
    a = k == 7; keep[a, 1:h + 1] = 1.0; nn[a, 1:h + 1] = 0
    nn[:, 0] = QN
    C, p = grow(rng, par, lab, keep, nn, fresh(rng)); x, l = floats(rng)
    th = np.stack([rng.choice(np.array([8, 12, 16]), (N, 8)), rng.choice(np.array([0, 8, 16]), (N, 8))], axis=2)
    return pack(x, l, C, p, th)
def setup_inputs_ends(rng):
    B = 8 * N; side = rng.integers(0, 2, (B, 1)); i = np.arange(V - 1)
    lab = np.concatenate([side * (M - 1), (1 - side) * (M - 1), 1 + np.argsort(rng.random((B, M - 2)), axis=1)], axis=1)
    par = rng.integers(0, 2, (B, M)); par[:, :2] = 0
    seq = np.where(i & 1 == 1, i // 2, V - 2 - i // 2); nm = np.full((B, M, QN), NO, np.int64)
    nm[:, 0] = seq[:QN]; nm[:, 1] = seq[QN:2 * QN]; nm[:, 2:, :2] = seq[2 * QN:2 * QN + 2 * (M - 2)].reshape(M - 2, 2)
    keep = np.full((B, M), 0.35); keep[:, 1] = 0.6; nn = rng.integers(0, 3, (B, M)); nn[:, :2] = QN
    C, p = grow(rng, par, lab, keep, nn, nm)
    for c in (0, M - 1):
        C[:, c] = np.sort(C[:, c], axis=1); C[3::4, c] = C[3::4, c, ::-1].copy()
    th = 16 * (np.argsort(rng.random((N, 8, 2)), axis=1) & 1)
    def signs(n, lows):
        kind = rng.integers(0, 2 + lows, (N, 8, 1, n)); kind[..., -2:] = 0
        s = np.where(kind == 0, 1, np.where(kind == 2, -1, 2 * rng.integers(0, 2, (N, 8, 16, n)) - 1))
        return (s * BIG).reshape(N, 128, n).astype(BF)
    return pack(signs(V, 0), signs(H, 1), C, p, th)
def setup_inputs_spread(rng):
    C, p = trees(rng); x = wide(rng, N, 128, V)
    l = np.abs(wide(rng, N, 128, H).astype(np.float32)) * np.where(rng.random((N, 1, H)) < 0.125, -1.0, 1.0)
    return pack(x, l.astype(BF), C, p, rng.integers(0, 17, (N, 8, 2)))
def setup_inputs_ties(rng):
    C, p = trees(rng)
    px = rng.choice(np.array([0.0, 0.75, 1.0, 256.0, -0.25, -1.5 * 2.0 ** -17]), (N, 8, 16, 6)); pl = rng.choice(np.array([0.0, 0.25, 1.0, 255.0, 256.0, 258.0, -1.0]), (N, 8, 16, 8))
    x = np.take_along_axis(px, rng.integers(0, 6, (N, 8, 1, V)), 3); l = np.take_along_axis(pl, rng.integers(0, 8, (N, 8, 1, H)), 3)
    return pack(x.reshape(N, 128, V).astype(BF), l.reshape(N, 128, H).astype(BF), C, p, rng.integers(5, 14, (N, 8, 2)))
def check_inputs(d):
    bad = []
    for k, hi in (("cq", NO), ("pt", M - 1), ("th", 16)):
        if np.min(d[k]) < 0 or np.max(d[k]) > hi: bad.append("range of " + k)
    for k in ("xs", "lim"):
        if not np.all(np.abs(np.asarray(d[k]).astype(np.float32)) <= BIG): bad.append("size of " + k)
    if "range of cq" in bad or "range of pt" in bad: return bad
    g = np.arange(8)[:, None]; own = np.arange(M)[None, :]
    for a in range(N):
        C = gentries(np.asarray(d["cq"][a])).astype(np.int64).reshape(8, M, 16); p = gentries(np.asarray(d["pt"][a])).astype(np.int64)
        e = np.sort(np.where(C == NO, -1 - np.arange(16), C), axis=2)
        if np.any(e[..., 1:] == e[..., :-1]) and "a name twice in a clique of cq" not in bad: bad.append("a name twice in a clique of cq")
        r = p
        for i in range(10): r = np.take_along_axis(r, r, 1)
        if (np.any(r != r[:, :1]) or np.any(np.take_along_axis(p, r, 1) != r)) and "pt not a tree" not in bad: bad.append("pt not a tree")
        inp = np.any(C[:, :, :, None] == C[g, p][:, :, None, :], axis=3)
        top = (C != NO) & (~inp | (p == own)[..., None])
        if np.max(np.bincount((C + V * np.arange(8)[:, None, None])[top], minlength=1)) > 1 and "cliques of a name not connected" not in bad: bad.append("cliques of a name not connected")
    return bad
def reference(xs, lim, cq, pt, th):
    C = np.stack([gentries(a) for a in cq]).astype(np.int64).reshape(N, 8, M, 16); P = np.stack([gentries(a) for a in pt]).astype(np.int64)
    X = xs.astype(np.float32).reshape(N, 8, 16, V); LM = lim.astype(np.float32).reshape(N, 8, 16, H); T = th.astype(np.int64)
    g = np.arange(8)[:, None]; own = np.arange(M)[None, :]; odd = [0] * N
    for t in range(RO):
        c = np.arange(t & 1, M, 2); m = len(c)
        for a in range(N):
            q = (a + t) % N; D = C[a]; pa = P[a]; full = D != NO
            up = D[g, pa]
            same = (D[:, :, :, None] == up[:, :, None, :]) & full[..., None]
            mark = np.any(same, axis=2) & (pa != own)[..., None]
            kids = np.zeros((8, M, 16), np.int64); np.add.at(kids, (g, pa), mark.astype(np.int64))
            e = D[:, c]; Q = up[:, c]; E = same[:, c]; pc = pa[:, c]; act = (pc & 1) != (t & 1)
            outside = full[:, c] & ~np.any(E, axis=3); has = np.any(outside, axis=2)
            y = np.where(has, np.take_along_axis(e, np.argmax(outside, axis=2)[..., None], 2)[..., 0], Q[..., 0])
            h = (((y[..., None] * Q) >> 5) + y[..., None] + 37 * Q) & (H - 1)
            XQ = np.take_along_axis(X[q], Q.reshape(8, 1, -1), 2).reshape(8, 16, m, 16)
            Xy = np.take_along_axis(X[q], y[:, None, :], 2)[..., None]
            LH = np.take_along_axis(LM[q], h.reshape(8, 1, -1), 2).reshape(8, 16, m, 16)
            s = np.add.reduce((np.abs(XQ - Xy) <= LH).astype(np.int64), axis=1)
            inC = np.any(E, axis=2); held = np.any(E & (kids[:, c] > 0)[..., None], axis=2); room = ~full[:, c]
            key = np.where((Q != NO) & ~inC, s, -1); j = np.argmax(key, axis=2); best = np.max(key, axis=2)
            join = act & has & (best >= 0) & (best >= T[q][:, :1] + odd[a]) & np.any(room, axis=2)
            can = inC & ~held; w = np.argmin(np.where(can, s, 17), axis=2)
            leave = act & has & ~join & np.any(can, axis=2); gone = act & ~has
            new = e.copy()
            i, n = np.nonzero(join); new[i, n, np.argmax(room[i, n], axis=1)] = Q[i, n, j[i, n]]
            i, n = np.nonzero(leave); new[i, n, np.argmax(E[i, n, :, w[i, n]], axis=1)] = NO
            i, n = np.nonzero(gone); new[i, n] = np.where(s[i, n] <= T[q][i, 1][:, None], Q[i, n], NO)
            A = np.broadcast_to(own, (8, M)).copy(); A[:, c] = np.where(gone, pc, c[None, :])
            D[:, c] = new; P[a] = np.take_along_axis(A, pa, 1); odd[a] = int(np.count_nonzero(join)) & 1
    return {"yc": np.stack([gtable(a.reshape(8, -1)) for a in C]).astype(np.float32), "yp": np.stack([gtable(a) for a in P]).astype(np.float32)}

@@ -1,0 +1,737 @@
+import math
+from concourse.mybir import AluOpType, ActivationFunctionType
+
+A = AluOpType
+F = ActivationFunctionType
+LN2 = math.log(2.0)
+XW = 8208
+XO = 520
+K = 64.0
+BIG = 8192.0
+RND = 1.5 * 2.0 ** 23
+
+SCRATCH = {}
+
+
+def _sb(name, cols, dtype):
+    SCRATCH[name] = ("sbuf", [128, cols], dtype)
+
+
+for _i in range(4):
+    _sb("XL%d" % _i, XW, "bfloat16")
+    _sb("PR%d" % _i, 512, "bfloat16")
+_sb("LU", 288, "uint16")
+_sb("PU", 160, "uint16")
+_sb("PF", 128, "float32")
+_sb("PW", 256, "bfloat16")
+_sb("AB", 64, "float32")
+for _i in range(8):
+    SCRATCH["B%d" % _i] = ("psum", [128, 512], "float32")
+for _n, _c, _d in [
+    ("cqs", 512, "int32"), ("pts", 32, "int32"), ("ths", 8, "int32"), ("thb", 8, "bfloat16"),
+    ("NX", 1040, "float32"), ("WF", 1024, "bfloat16"), ("FI", 528, "bfloat16"),
+    ("IC", 512, "bfloat16"), ("NAT", 512, "bfloat16"), ("STP", 1024, "bfloat16"),
+    ("AW0", 512, "bfloat16"), ("AW1", 512, "bfloat16"), ("AW3", 512, "bfloat16"),
+    ("pci", 8, "int32"), ("pcf", 16, "float32"), ("IG", 128, "float32"), ("IJ", 128, "float32"),
+    ("I144", 144, "float32"), ("IL", 32, "float32"), ("I128", 128, "bfloat16"),
+    ("EQ", 16, "bfloat16"), ("B0b", 144, "bfloat16"), ("CE", 768, "float16"), ("HX", 32, "float32"),
+    ("OBm", 128, "bfloat16"),
+    ("OBf", 128, "float32"), ("OBb", 128, "bfloat16"), ("OBp", 128, "bfloat16"),
+    ("OBn", 128, "bfloat16"), ("ONf", 128, "float32"), ("ONb", 128, "bfloat16"),
+    ("Ih", 128, "float16"), ("Ib", 128, "bfloat16"), ("In", 128, "bfloat16"), ("Ihalf", 128, "bfloat16"),
+    ("D1", 128, "bfloat16"), ("D3", 128, "bfloat16"), ("DJ", 128, "bfloat16"),
+    ("L1", 128, "float16"), ("L2", 128, "float16"), ("BT", 2048, "float16"), ("BM", 144, "bfloat16"),
+    ("B0h", 144, "float16"), ("EX", 2048, "bfloat16"), ("FST", 128, "bfloat16"), ("TRI", 128, "bfloat16"),
+    ("PK", 128, "bfloat16"), ("PK32", 128, "bfloat16"), ("c1", 128, "bfloat16"),
+    ("CST", 1024, "bfloat16"), ("S8", 128, "bfloat16"),
+    ("NC", 512, "float16"), ("QN", 512, "float16"), ("E", 2048, "bfloat16"), ("i5", 256, "int32"),
+    ("b5", 512, "bfloat16"), ("t5", 512, "bfloat16"), ("f5", 512, "float32"), ("LT", 528, "float32"),
+    ("HL", 32, "float32"), ("tl", 192, "float32"), ("ti", 96, "int32"), ("PN", 512, "bfloat16"),
+    ("QU", 256, "uint16"), ("QH", 256, "float16"), ("YH", 256, "float16"), ("YU", 16, "uint16"),
+    ("XY", 256, "bfloat16"), ("XT", 256, "bfloat16"), ("hm", 256, "float32"), ("hi", 256, "int32"),
+    ("HU", 256, "uint16"), ("XQ", 4096, "bfloat16"), ("AD", 2048, "float32"), ("CM", 4096, "bfloat16"),
+    ("FWq", 512, "bfloat16"), ("FIq", 512, "bfloat16"), ("Ns", 256, "float32"), ("DG", 2048, "bfloat16"),
+    ("Ws", 512, "bfloat16"), ("fl", 1280, "bfloat16"), ("thr", 512, "float32"), ("MT", 512, "bfloat16"),
+    ("mi", 512, "float32"), ("OH", 4096, "bfloat16"), ("ki", 128, "float32"), ("nh", 256, "bfloat16"),
+    ("cw", 256, "bfloat16"), ("zi", 768, "int32"), ("pj", 256, "bfloat16"), ("sg", 256, "bfloat16"),
+    ("NJ", 256, "float32"), ("SW", 256, "bfloat16"), ("u", 256, "float32"), ("w", 256, "bfloat16"),
+    ("Np", 256, "float32"), ("Wp", 256, "bfloat16"), ("a", 256, "float32"), ("b", 256, "bfloat16"),
+    ("t", 256, "float32"), ("tw", 256, "bfloat16"), ("sc", 8, "float32"), ("si", 8, "int32"),
+    ("OC", 512, "float32"), ("OP", 32, "float32"),
+]:
+    _sb(_n, _c, _d)
+
+SEMAPHORES = ["sV", "sS", "sP", "sG", "dcq", "dpt", "dth", "dxs", "dlim", "dout", "sent", "arr1", "arr2", "arr3"]
+
+CY = 0.83 * 1.25
+PCY = 0.42 * 1.25
+GA = 1.6
+CUTS = (128, 256)
+MIS = True
+NS2 = 0
+
+
+def build(g, T):
+    ops = []
+    V, S, P = g.vector, g.scalar, g.tensor
+
+    def op(eng, ns, rd, wr, fn):
+        ops.append({"e": eng, "c": ns, "r": rd, "w": wr, "f": fn})
+
+    def vc(n, f):
+        return 30 + max(64.0, n * f) * CY
+
+    def ts(out, in0, s1, s2, o0, o1, n, rd, wr, f=1.0):
+        if s2 is None:
+            op("V", vc(n, f), rd, wr, lambda: V.tensor_scalar(out, in0, s1, None, o0))
+        else:
+            op("V", vc(n, f), rd, wr, lambda: V.tensor_scalar(out, in0, s1, s2, o0, o1))
+
+    def tt(out, in0, in1, o, n, rd, wr, f=1.0):
+        op("V", vc(n, f), rd, wr, lambda: V.tensor_tensor(out, in0, in1, o))
+
+    def cp(out, in_, n, rd, wr, f=1.0):
+        op("V", vc(n, f), rd, wr, lambda: V.tensor_copy(out, in_))
+
+    def ms(out, val, n, wr):
+        op("V", vc(n, 0.5), [], wr, lambda: V.memset(out, val))
+
+    def act(out, in_, func, n, rd, wr, f=1.0, bias=None, scale=None, acc=None):
+        kw = {}
+        if bias is not None:
+            kw["bias"] = bias
+        if scale is not None:
+            kw["scale"] = scale
+        if acc is not None:
+            kw["accum_out"] = acc
+        op("S", 60 + max(64.0, n * f) * CY, rd, wr, lambda: S.activation(out, in_, func, **kw))
+
+    def mm(items, rd, wr):
+        c = 40 + sum(max(64, it[5]) * (it[6] if len(it) > 6 else 1) for it in items) * PCY
+
+        def fn():
+            last = None
+            for it in items:
+                last = P.matmul(it[0], it[1], it[2], it[3], it[4])
+            return last
+        op("P", c, rd, wr, fn)
+
+    def io(out, pat, base, ch, n, wr, flt=True):
+        if flt:
+            op("G", 130 + 2 * n * CY, [], wr, lambda: g.iota(out, pat, base, ch, allow_small_or_imprecise_dtypes=True))
+        else:
+            op("G", 130 + 2 * n * CY, [], wr, lambda: g.iota(out, pat, base, ch))
+
+    def sel(out, in_, pat, cmp, fill, base, ch, n, rd, wr):
+        op("G", 170 + 2 * n * CY, rd, wr, lambda: g.affine_select(out, in_, pat, cmp, fill, base, ch))
+
+    B = [T["B%d" % i] for i in range(8)]
+    pcf = T.pcf
+    pcol, gcol, kcol, g16, k1, k40 = [pcf[:, i:i + 1] for i in range(6)]
+
+    io(T.pci[:, 0:1], [[0, 1]], 0, 1, 1, ["pci0"], False)
+    io(T.IG[:], [[1, 8], [0, 16]], 0, 0, 128, ["IG"])
+    io(T.I144[:], [[1, 144]], -15, 0, 144, ["I144"])
+    io(T.IJ[:], [[0, 8], [1, 16]], 0, 0, 128, ["IJ"])
+    io(T.IC[:], [[1, 512]], -256, 0, 512, ["IC"])
+    io(T.IL[:], [[16, 32]], 0, 0, 32, ["IL0"])
+    io(T.NAT[:], [[1, 2], [2, 256]], -256, 0, 512, ["NAT"])
+    io(T.STP[:, 0:512], [[0, 512]], 0, 0, 512, ["STP"])
+    io(T.STP[:, 512:1024], [[0, 512]], 1, 0, 512, ["STP1"])
+    io(T.ONf[:], [[0, 128]], 1, 0, 128, ["ONf"])
+    io(T.ONb[:], [[0, 128]], 1, 0, 128, ["ONb"])
+    io(T.NX[:, 512:520], [[0, 8]], 0, 0, 8, ["NXz"])
+    io(T.NX[:, XO + 256:1040], [[0, 264]], 0, 0, 264, ["X1"])
+    io(T.FI[:, 512:528], [[0, 16]], 0, 0, 16, ["FIz"])
+    io(T.LT[:, 512:528], [[0, 16]], 0, 0, 16, ["LTz"])
+    io(T.XL0[:, 8192:XW], [[0, 16]], 0, 0, 16, ["XLt0"])
+    io(T.I128[:], [[1, 128]], 0, 0, 128, ["I128"])
+    io(T.AW0[:, 256:512], [[1, 256]], 0, 0, 256, ["AW0s"])
+    io(T.AW1[:, 0:256], [[1, 256]], -256, 0, 256, ["AW1s"])
+    io(T.AW3[:, 0:256], [[2, 256]], -256, 0, 256, ["AW3s"])
+    for q in range(4):
+        sel(T.EX[:, 512 * q:512 * q + 512], T.STP[:, 512:1024], [[-1, 32], [0, 16]], A.is_equal, 0.0, -32 * q, 1, 512,
+            ["STP1"], ["EX%d" % q])
+    ts(T.pci[:, 1:2], T.pci[:, 0:1], 4, None, A.arith_shift_right, None, 1, ["pci0"], ["pci1"])
+    ts(T.pci[:, 2:3], T.pci[:, 0:1], 15, None, A.bitwise_and, None, 1, ["pci0"], ["pci2"])
+    cp(pcf[:, 0:3], T.pci[:, 0:3], 3, ["pci0", "pci1", "pci2"], ["pc"])
+    ts(g16, gcol, 16.0, None, A.mult, None, 1, ["pc"], ["g16"])
+    ts(k1, kcol, -1.0, 1.0, A.mult, A.add, 1, ["pc"], ["k1"])
+    ts(k40, kcol, -1.0, -40.0, A.mult, A.add, 1, ["pc"], ["k40"])
+    I128f = T.I144[:, 15:143]
+    ts(T.OBf[:], T.IG[:], gcol, None, A.is_equal, None, 128, ["IG", "pc"], ["OBf"])
+    ts(T.OBb[:], T.IG[:], gcol, None, A.is_equal, None, 128, ["IG", "pc"], ["OBb"])
+    ts(T.EQ[:], T.IJ[:, 0:16], kcol, None, A.is_equal, None, 16, ["IJ", "pc"], ["EQ"])
+    ts(T.Ih[:], I128f, pcol, None, A.is_equal, None, 128, ["I144", "pc"], ["Ih"])
+    ts(T.Ib[:], I128f, pcol, None, A.is_equal, None, 128, ["I144", "pc"], ["Ib"])
+    for j in range(16):
+        ts(T.BT[:, 128 * j:128 * j + 128], T.OBb[:], T.EQ[:, j:j + 1], None, A.mult, None, 128, ["OBb", "EQ"], ["BT%d" % j], 0.5)
+    for nm, v in (("In", -1.0), ("Ihalf", -0.5), ("D1", -25.5 * K * K), ("D3", -20.0 * K)):
+        act(T[nm][:], T.Ib[:], F.Copy, 128, ["Ib"], [nm], scale=v)
+    for nm, v in (("OBm", -1.0), ("OBp", K), ("OBn", -K)):
+        act(T[nm][:], T.OBf[:], F.Copy, 128, ["OBf"], [nm], scale=v)
+    ts(T.L1[:], T.BT[:, 0:128], 2080.0, None, A.mult, None, 128, ["BT0"], ["L1"], 0.5)
+    ts(T.L2[:], T.Ih[:], 3232.0, None, A.mult, None, 128, ["Ih"], ["L2"], 0.5)
+    ts(T.BM[:], T.I144[:], g16, K, A.is_equal, A.mult, 144, ["I144", "g16"], ["BM"])
+    ts(pcf[:, 6:7], kcol, 0.0, None, A.is_equal, None, 1, ["pc"], ["k0"])
+    ts(T.B0h[:], T.I144[:], pcol, pcf[:, 6:7], A.is_equal, A.mult, 144, ["I144", "pc", "k0"], ["B0h"])
+    ts(T.B0b[:], T.I144[:], pcol, pcf[:, 6:7], A.is_equal, A.mult, 144, ["I144", "pc", "k0"], ["B0b"])
+    sel(T.c1[:], T.OBb[:], [[1, 128]], A.is_gt, 0.0, 0, -1, 128, ["OBb"], ["c1"])
+    sel(T.FST[:], T.c1[:], [[1, 128]], A.not_equal, -16.0, 0, -1, 128, ["c1"], ["FST"])
+    act(T.c1[:], T.c1[:], F.Identity, 128, ["c1"], ["c1"], bias=1.0 / 32, scale=47.0 / 32)
+    sel(T.c1[:], T.c1[:], [[1, 128]], A.not_equal, -1.0, 0, -1, 128, ["c1"], ["c1"])
+    act(T.PK[:], T.IJ[:], F.Exp, 128, ["IJ"], ["PK"], scale=-LN2, bias=-LN2)
+    ops[-1]["c"] += 1300
+    for nm, src in (("TRI", "c1"), ("PK", "PK")):
+        sel(T[nm][:], T[src][:], [[-16, 8], [0, 16]], A.is_ge, 0.0, 0, 1, 128, [src], [nm])
+        sel(T[nm][:], T[nm][:], [[16, 8], [0, 16]], A.is_ge, 0.0, 15, -1, 128, [nm], [nm])
+    act(T.PK32[:], T.PK[:], F.Copy, 128, ["PK"], ["PK32"], scale=1.0 / 32)
+    cA, cB, cC, cD = [T.CST[:, 256 * i:256 * i + 256] for i in range(4)]
+    ms(cA, -4.5 * K / 16, 256, ["cA"])
+    ms(cB, 1.0 / 32, 256, ["cB"])
+    ms(cC, 2.5 / 16, 256, ["cC"])
+    cE = T.fl[:, 512:768]
+    io(cE, [[0, 256]], 4096, 0, 256, ["cE"])
+    ts(T.IL[:], T.IL[:], kcol, None, A.add, None, 32, ["IL0", "pc"], ["IL0", "IL"])
+    ts(T.S8[0:8, :], T.IG[0:8, :], pcf[0:8, 0:1], None, A.is_equal, None, 128, ["IG", "pc"], ["S8"])
+    cp(T.thb[0:8, 0:2], T.ths[0:8, 0:2], 2, ["xth"], ["thb"])
+    mm([(B[7][:, 0:2], T.S8[0:8, :], T.thb[0:8, 0:2], True, True, 2)], ["S8", "thb"], ["B7"])
+    cp(T.XL0[:, 8192:8194], B[7][:, 0:2], 2, ["B7", "XLt0"], ["XLt0"])
+
+    NW = ["N0", "N1", "NXz"]
+    for h in range(2):
+        ts(T.NX[:, 256 * h:256 * h + 256], T.cqs[:, h::2], -1.0, 4095.0, A.mult, A.add, 256, ["xcq"], ["N%d" % h])
+    ts(T.ti[:, 0:32], T.pts[:], 1, None, A.arith_shift_right, None, 32, ["xpt"], ["ti0"])
+    ts(T.ti[:, 32:64], T.pts[:], 1, None, A.bitwise_and, None, 32, ["xpt"], ["ti1"])
+    ts(T.tl[:, 0:32], T.ti[:, 32:64], 256.0, None, A.mult, None, 32, ["ti1"], ["tl0"])
+    tt(T.tl[:, 0:32], T.tl[:, 0:32], T.ti[:, 0:32], A.add, 32, ["tl0", "ti0"], ["tl0"])
+    PUn = T.PU[:, 128:160]
+    cp(PUn, T.tl[:, 0:32], 32, ["tl0"], ["PUn"])
+    ts(T.QN[:], T.NX[:, 0:512].indirect(PUn), -1.0, 2047.0, A.mult, A.add, 512, NW + ["PUn"], ["QN"], GA)
+    act(T.b5[:], T.NX[:, 0:512], F.Sign, 512, ["N0", "N1"], ["b5"])
+    act(B[4][:], T.NX[:, 0:512], F.Identity, 512, ["N0", "N1"], ["B4"], bias=-2048.0)
+    tt(T.NC[:], B[4][:], T.b5[:], A.add, 512, ["B4", "b5"], ["NC"])
+    ts(T.CE[:, 0:256], T.NC[:, 0:256], -1.0, None, A.mult, None, 256, ["NC"], ["CE0"], 0.5)
+    ts(T.CE[:, 256:768], T.NC[:], -1.0, None, A.mult, None, 512, ["NC"], ["CE1"], 0.5)
+    act(T.PN[:], T.IC[:].indirect(PUn), F.Copy, 512, ["IC", "PUn"], ["PN"], GA)
+    for h in range(2):
+        act(T.PR0[:, 256 * h:256 * h + 256], T.PN[:, h::2], F.Copy, 256, ["PN"], ["PR0"])
+
+    def lists(t):
+        PR = T["PR%d" % t]
+        mm([(B[6][:, 0:32], T.B0b[:, 15 - w:143 - w], PR[:, w::16], w == 0, w == 15, 32) for w in range(16)],
+           ["B0b", "PR%d" % t], ["B6"])
+        ts(T.PU[:, 32 * t:32 * t + 32], B[6][:, 0:32], 256.0, None, A.add, None, 32, ["B6"], ["PU%d" % t])
+        act(T.PF[:, 32 * t:32 * t + 32], B[6][:, 0:32], F.Identity, 32, ["B6"], ["PF%d" % t], bias=256.0)
+        mm([(B[7][:, 8 * k:8 * k + 8], PR[:, 128 * k:128 * k + 128], T.B0b[:, 15:143:16], True, True, 8) for k in range(4)],
+           ["B0b", "PR%d" % t], ["B7"])
+        ts(T.ti[:, 0:32], B[7][:, 0:32], 256.0, None, A.add, None, 32, ["B7"], ["ti0"])
+        ts(T.ti[:, 32:64], T.ti[:, 0:32], 383, None, A.bitwise_and, None, 32, ["ti0"], ["ti1"])
+        ts(T.ti[:, 64:96], T.ti[:, 0:32], 128, None, A.bitwise_and, None, 32, ["ti0"], ["ti2"])
+        ts(T.PW[:, 64 * t:64 * t + 32], T.ti[:, 32:64], float(-256 * (t & 1)), None, A.add, None, 32, ["ti1"], ["PWa%d" % t])
+        ts(T.PW[:, 64 * t + 32:64 * t + 64], T.ti[:, 64:96], 1023.0 / 128, 1.0, A.mult, A.add, 32, ["ti2"], ["PWb%d" % t])
+
+    def compare(h):
+        c = slice(256 * h, 256 * h + 256)
+        sb = 3 + 2 * h
+        for n in range(8):
+            bk, eb = (n % 2, n % 2) if h == 0 else (2 + 2 * (n % 2), 2 + n % 2)
+            its = []
+            for i in range(2):
+                o, j = B[bk][:, 256 * i:256 * i + 256], 2 * n + i
+                if h:
+                    its.append((o, T.Ih[:], T.NC[:, c], True, False, 256))
+                its.append((o, T.BT[:, 128 * j:128 * j + 128], T.QN[:, h::2], h == 0, True, 256))
+            mm(its, ["Ih", "NC", "QN", "BT%d" % (2 * n), "BT%d" % (2 * n + 1)], ["B%d" % bk])
+            e = T.E[:, 512 * eb:512 * eb + 512]
+            if h:
+                act(e, B[bk][:], F.Sign, 512, ["B%d" % bk], ["E%d" % eb])
+            else:
+                tt(e, B[bk][:], T.CE[:, 0:512], A.is_equal, 512, ["B%d" % bk, "CE0", "CE1"], ["E%d" % eb])
+            mm([(B[sb][:, 0:256], T.Ib[:], T.E[:, 512 * eb + 256 * i:512 * eb + 256 * i + 256], n + i == 0, n + i == 8, 256)
+                for i in range(2)], ["Ib", "E%d" % eb], ["B%d" % sb])
+        if h:
+            cp(T.i5[:], B[sb][:, 0:256], 256, ["B5"], ["i5"])
+            ts(T.i5[:], T.i5[:], 1, None, A.bitwise_and, None, 256, ["i5"], ["i5"])
+            tt(T.t5[:, c], T.b5[:, c], T.i5[:], A.is_gt, 256, ["b5", "i5"], ["t51"], 2)
+        else:
+            tt(T.t5[:, c], B[sb][:, 0:256], T.b5[:, c], A.is_lt, 256, ["B3", "b5"], ["t50"])
+
+    def tops(h):
+        c = slice(256 * h, 256 * h + 256)
+        tp = "t5%d" % h
+        mm([(B[6][:, 0:16], T.BM[:, 15 - w:143 - w], T.t5[:, 256 * h + w:256 * h + 256:16], w == 0, w == 15, 16) for w in range(16)],
+           ["BM", tp], ["B6"])
+        s = slice(16 * h, 16 * h + 16)
+        ts(T.HL[:, s], B[6][:, 0:16], 0.0, None, A.is_gt, None, 16, ["B6"], ["HL%d" % h])
+        ts(T.HX[:, s], T.IL[:, s], float(XO), None, A.add, None, 16, ["IL"], ["HX%d" % h])
+        tt(T.HX[:, s], T.HX[:, s], T.HL[:, s], A.mult, 16, ["HX%d" % h, "HL%d" % h], ["HX%d" % h])
+        mm([(B[7][:, 0:256], T.FST[:], T.t5[:, c], True, True, 256)], ["FST", tp], ["B7"])
+        act(B[7][:, 0:256], B[7][:, 0:256], F.Relu, 256, ["B7"], ["B7"], bias=-15.0, scale=-1.0)
+        tt(T.f5[:, c], B[7][:, 0:256], T.NX[:, c], A.mult, 256, ["B7", "N%d" % h], ["f5%d" % h])
+        mm([(B[7][:, 0:256], T.OBf[:], T.f5[:, c], True, True, 256, 4)], ["OBf", "f5%d" % h], ["B7"])
+        act(T.NX[:, XO + 256 * h:XO + 256 * h + 256], B[7][:, 0:256], F.Copy, 256, ["B7"], ["X%d" % h])
+
+    def chain(t):
+        par = t & 1
+        s = slice(16 * par, 16 * par + 16)
+        PF, ab = T.PF[:, 32 * t + 16 * par:32 * t + 16 * par + 16], T.AB[:, 16 * t:16 * t + 16]
+        hl, il = T.HL[:, s], T.IL[:, s]
+        x0, x1 = T.tl[:, 32:48], T.tl[:, 48:64]
+        ly, lf, ln, lw = [T.tl[:, 64 + 16 * i:80 + 16 * i] for i in range(4)]
+        pf, lu, hn = "PF%d" % t, "LU%d" % t, "HL%d" % par
+        tt(ly, PF, T.HX[:, s], A.max, 16, [pf, "HX%d" % par], ["ly"])
+        cp(T.LU[:, 64 * t:64 * t + 16], ly, 16, ["ly"], [lu + "y"])
+        ts(x0, PF, 256.0, None, A.is_lt if par else A.is_ge, None, 16, [pf], ["x0"])
+        tt(ab, x0, hl, A.is_gt, 16, ["x0", hn], ["AB%d" % t])
+        tt(x1, PF, il, A.subtract, 16, [pf, "IL"], ["x1"])
+        tt(x1, x1, ab, A.mult, 16, ["x1", "AB%d" % t], ["x1"])
+        tt(ln, x1, il, A.add, 16, ["x1", "IL"], ["ln"])
+        cp(T.LU[:, 64 * t + 32:64 * t + 48], ln, 16, ["ln"], [lu + "N"])
+        act(x1, ab, F.Copy, 16, ["AB%d" % t], ["x1"], scale=512.0)
+        tt(lw, x1, ln, A.add, 16, ["x1", "ln"], ["lw"])
+        tt(x0, x0, hl, A.mult, 16, ["x0", hn], ["x0"])
+        act(x0, x0, F.Identity, 16, ["x0"], ["x0"], scale=-512.0, bias=512.0)
+        tt(lf, x0, PF, A.max, 16, ["x0", pf], ["lf"])
+        cp(T.LU[:, 64 * t + 16:64 * t + 32], lf, 16, ["lf"], [lu + "F"])
+        cp(T.LU[:, 64 * t + 48:64 * t + 64], lw, 16, ["lw"], [lu + "W"])
+        aw = "AW3" if t == 3 else "AW%d" % par
+        src = "NAT" if t == 3 else "IC"
+        h = slice(256 * par, 256 * par + 256)
+        act(T[aw][:, h], T[src][:].indirect(T.LU[:, 64 * t + 32:64 * t + 48]), F.Copy, 256, [src, lu + "N"], [aw], GA)
+        nx = "PN" if t == 3 else "PR%d" % (t + 1)
+        act(T[nx][:], T[aw][:].indirect(T.PU[:, 32 * t:32 * t + 32]), F.Copy, 512, [aw, aw + "s", "PU%d" % t], [nx], GA)
+
+    def parents_out():
+        mm([(B[6][:, 0:32], T.B0b[:, 15 - w:143 - w], T.PN[:, 256 * (w & 1) + (w >> 1):256 * (w & 1) + 256:8],
+             w == 0, w == 15, 32) for w in range(16)], ["B0b", "PN"], ["B6"])
+        act(T.OP[:], B[6][:, 0:32], F.Identity, 32, ["B6"], ["OP"], bias=256.0)
+
+    def frames():
+        ts(T.QN[:], T.NX[:, 0:512].indirect(T.PU[:, 96:128]), -1.0, 2047.0, A.mult, A.add, 512, NW + ["PU3"], ["QN"], GA)
+        for n in range(16):
+            bk = 4 + n % 3
+            bn = "B%d" % bk
+            e = T.E[:, 512 * (n % 4):512 * (n % 4) + 512]
+            bt = T.BT[:, 128 * n:128 * n + 128]
+            if (n * NS2) // 16 != ((n + 1) * NS2) // 16:
+                mm([(B[bk][:], T.Ih[:], T.NC[:], True, False, 512), (B[bk][:], bt, T.QN[:], False, True, 512)],
+                   ["Ih", "NC", "QN", "BT%d" % n], [bn])
+                act(B[bk][:], B[bk][:], F.Abs, 512, [bn], [bn])
+                act(e, B[bk][:], F.Relu, 512, [bn], ["E%d" % (n % 4)], bias=float(n + 40), scale=-float(n + 40))
+                dg, dn = T.Ib[:], "Ib"
+            else:
+                mm([(B[bk][:], bt, T.QN[:], True, True, 512)], ["QN", "BT%d" % n], [bn])
+                tt(e, B[bk][:], T.CE[:, 256:768], A.is_equal, 512, [bn, "CE1"], ["E%d" % (n % 4)])
+                dg, dn = T.DG[:, 128 * n:128 * n + 128], "DG%d" % n
+                act(dg, T.Ib[:], F.Copy, 128, ["Ib"], [dn], scale=float(n + 40))
+            mm([(B[7][:], dg, e, n == 0, n == 15, 512)], [dn, "E%d" % (n % 4)], ["B7"])
+        act(T.WF[:, 0:512], B[7][:], F.Exp, 512, ["B7"], ["WA0", "WA1"], scale=LN2, bias=-40.0 * LN2)
+        act(T.LT[:, 0:512], B[7][:], F.Identity, 512, ["B7", "k40"], ["LT"], bias=k40)
+        tt(T.tl[:, 128:144], T.AB[:, 0:16], T.AB[:, 32:48], A.max, 16, ["AB0", "AB2"], ["x3"])
+        cp(T.tl[:, 144:160], T.AB[:, 16:32], 16, ["AB1"], ["x4"])
+        ts(T.tl[:, 0:32], T.IL[:], -512.0, None, A.add, None, 32, ["IL"], ["tl0"])
+        tt(T.tl[:, 0:32], T.tl[:, 0:32], T.tl[:, 128:160], A.mult, 32, ["tl0", "x3", "x4"], ["tl0"])
+        ts(T.LU[:, 256:288], T.tl[:, 0:32], 512.0, None, A.add, None, 32, ["tl0"], ["La"])
+        f5 = ["f50", "f51"]
+        act(T.f5[:], T.LT[:].indirect(T.LU[:, 256:288]), F.Identity, 512, ["LT", "LTz", "La", "pc"], f5, GA, bias=kcol)
+        act(T.WF[:, 512:1024], T.f5[:], F.Exp, 512, f5, ["FW"], scale=LN2)
+        act(T.f5[:], T.f5[:], F.Abs, 512, f5, f5)
+        act(T.FI[:, 0:512], T.f5[:], F.Exp, 512, f5, ["FI"], scale=-LN2)
+
+    def onehot(t):
+        for q in range(8):
+            for k in range(4):
+                i = 8 * k + q
+                ts(T.OH[:, 128 * i:128 * i + 128], T.I128[:], T.PW[:, 64 * t + i:64 * t + i + 1],
+                   T.PW[:, 64 * t + 32 + i:64 * t + 33 + i], A.is_equal, A.mult,
+                   128, ["I128", "PWa%d" % t, "PWb%d" % t], ["OH%d" % i], 0.5)
+
+    def head(t):
+        XL = T["XL%d" % t]
+        lu, xs, pu = "LU%d" % t, "xxs%d" % t, "PU%d" % t
+        p0 = 32 * t + 16 * (t & 1)
+        for h in range(2):
+            ts(T.QU[:, 128 * h:128 * h + 128], T.NX[:, 0:512].indirect(T.PU[:, p0 + 8 * h:p0 + 8 * h + 8]), -1.0, 4095.0,
+               A.mult, A.add, 128, NW + [pu], ["QU%d" % h], GA)
+        ts(T.YH[:], T.NX[:].indirect(T.LU[:, 64 * t:64 * t + 16]), -1.0, 2047.0, A.mult, A.add, 256,
+           NW + ["X0", "X1", lu + "y"], ["YH"], GA)
+        mm([(B[6][:, 0:16], T.B0h[:, 15 - w:143 - w], T.YH[:, w::16], w == 0, w == 15, 16) for w in range(16)],
+           ["B0h", "YH"], ["B6"])
+        ts(T.YU[:], B[6][:, 0:16], 2048.0, None, A.add, None, 16, ["B6"], ["YU"])
+        ts(T.QH[:], T.QU[:], -2048.0, None, A.add, None, 256, ["QU0", "QU1"], ["QH"], 0.5)
+        mm([(B[5][:, 0:256], T.BT[:, 0:128], T.YH[:], True, True, 256),
+            (B[5][:, 256:512], T.L1[:], T.YH[:], True, False, 256),
+            (B[5][:, 256:512], T.L2[:], T.QH[:], False, True, 256)], ["BT0", "L1", "L2", "YH", "QH"], ["B5"])
+        tt(T.hm[:], B[5][:, 0:256], T.QH[:], A.mult, 256, ["B5", "QH"], ["hm"])
+        tt(T.hi[:], B[5][:, 256:512], T.hm[:], A.add, 256, ["B5", "hm"], ["hi"])
+        ts(T.hi[:], T.hi[:], 5, 4095, A.arith_shift_right, A.bitwise_and, 256, ["hi"], ["hi"])
+        cp(T.HU[:], T.hi[:], 256, ["hi"], ["HU"])
+        act(T.XY[:], XL[:, 0:4096].indirect(T.YU[:, 0:16]), F.Copy, 256, [xs, "YU"], ["XY"], GA)
+        mm([(B[6][:, 128 * h:128 * h + 128], T.XY[:, 128 * h:128 * h + 128], T.In[:], True, True, 128) for h in range(2)],
+           ["XY", "In"], ["B6"])
+        act(T.XT[:], B[6][:, 0:256], F.Copy, 256, ["B6"], ["XT"])
+
+    def scores(t):
+        XL = T["XL%d" % t]
+        xs, lm = "xxs%d" % t, "xlim%d" % t
+        for n in range(8):
+            c = slice(512 * n, 512 * n + 512)
+            act(T.XQ[:, c], XL[:, 0:4096].indirect(T.QU[:, 32 * n:32 * n + 32]), F.Copy, 512, [xs, "QU%d" % (n // 4)], ["XQ%d" % n], GA)
+            bk = n % 2 if len(CUTS) > 1 else n % 3
+            mm([(B[bk][:], T.Ib[:], T.XQ[:, c], True, False, 512),
+                (B[bk][:], T.XT[:, 128 * (n // 4):128 * (n // 4) + 128], T.EX[:, 512 * (n % 4):512 * (n % 4) + 512], False, True, 512)],
+               ["Ib", "XQ%d" % n, "XT", "EX%d" % (n % 4)], ["B%d" % bk])
+            ad = T.AD[:, 512 * (n % 4):512 * (n % 4) + 512]
+            act(ad, B[bk][:], F.Abs, 512, ["B%d" % bk], ["AD%d" % (n % 4)])
+            tt(T.CM[:, c], XL[:, 4096:8192].indirect(T.HU[:, 32 * n:32 * n + 32]), ad, A.is_ge, 512,
+               [lm, "HU", "AD%d" % (n % 4)], ["CM%d" % n], GA)
+
+    def bits(t, src, nm, bk, z, zn):
+        p = str(t & 1)
+        c = slice(256 * (t & 1), 256 * (t & 1) + 256)
+        o = B[bk][:, 0:256]
+        if nm == "cw":
+            its = [(o, T.OBb[:], cB, True, False, 256), (o, T.Ihalf[:], T.FWq[:, c], False, False, 256), (o, T.OBb[:], src, False, True, 256)]
+        else:
+            its = [(o, T.OBb[:], cE, True, False, 256), (o, T.OBm[:], cB, False, False, 256),
+                   (o, T.Ihalf[:], T.FWq[:, c], False, False, 256), (o, T.OBm[:], src, False, True, 256)]
+        mm(its, ["OBb", "OBm", "cB", "cE", "Ihalf", "FWq" + p, nm], ["B%d" % bk])
+        tt(z, o, T.FIq[:, c], A.mult, 256, ["B%d" % bk, "FIq" + p], [zn])
+        ts(z, z, 1, None, A.bitwise_and, None, 256, [zn], [zn])
+
+    def early(t):
+        par = t & 1
+        p = str(par)
+        c = slice(256 * par, 256 * par + 256)
+        XL = T["XL%d" % t]
+        Lf, Lw = T.LU[:, 64 * t + 16:64 * t + 32], T.LU[:, 64 * t + 48:64 * t + 64]
+        lu, pu, th = "LU%d" % t, "PU%d" % t, ("XLt0" if t == 0 else "xxs%d" % t)
+        p0 = 32 * t + 16 * par
+        ne = T.fl[:, 0:256]
+        act(ne, T.NX[:, c], F.Sign, 256, ["N" + p], ["ne"])
+        act(T.Ws[:, c], T.WF[:].indirect(Lw), F.Copy, 256, ["WA0", "WA1", "FW", lu + "W"], ["Ws" + p], GA)
+        act(T.FWq[:, c], T.WF[:, 512:1024].indirect(T.PU[:, p0:p0 + 16]), F.Copy, 256, ["FW", pu], ["FWq" + p], GA)
+        act(T.FIq[:, c], T.FI[:].indirect(Lf), F.Copy, 256, ["FI", "FIz", lu + "F"], ["FIq" + p], GA)
+        act(T.sc[:, 0:1], XL[:, 8193:8194], F.Identity, 1, [th], ["sc0"], scale=K, bias=-50.0 * K - BIG)
+        act(T.thr[:, c], T.STP[:].indirect(Lw), F.Identity, 256, ["STP", "STP1", lu + "W", "sc0"], ["thr" + p], GA,
+            bias=BIG, scale=T.sc[:, 0:1])
+        b1, b2 = (1, 0) if t else (5, 7)
+        mm([(B[b2][:, 0:256], T.FST[:], ne, True, True, 256)], ["FST", "ne"], ["B%d" % b2])
+        act(T.fl[:, 768 + 256 * par:1024 + 256 * par], B[b2][:, 0:256], F.Relu, 256, ["B%d" % b2, "k1"], ["first" + p], bias=k1)
+        bits(t, T.Ws[:, c], "Ws" + p, b1, T.zi[:, c], "zi" + p)
+
+    def masks(t):
+        par = t & 1
+        p = str(par)
+        XL = T["XL%d" % t]
+        Ly, Lf, Ln, Lw = [T.LU[:, 64 * t + 16 * i:64 * t + 16 * i + 16] for i in range(4)]
+        lu, pu, th = "LU%d" % t, "PU%d" % t, ("XLt0" if t == 0 else "xxs%d" % t)
+        p0 = 32 * t + 16 * par
+        PL = T.PU[:, p0:p0 + 16]
+        qne, first = T.fl[:, 256:512], T.fl[:, 768 + 256 * par:1024 + 256 * par]
+        cc = slice(256 * par, 256 * par + 256)
+        act(qne, T.NX[:, 0:512].indirect(PL), F.Sign, 256, NW + [pu], ["qne"], GA)
+        act(T.Ns[:], T.NX[:, 0:512].indirect(Ln), F.Copy, 256, NW + [lu + "N"], ["Ns"], GA)
+        for h in ((0, 1) if t == 0 else (1 - par,)):
+            its = []
+            for k in (2 * h, 2 * h + 1):
+                o = B[7][:, 128 * (k & 1):128 * (k & 1) + 128]
+                its += [(o, T.WF[:, 128 * k:128 * k + 128], T.PK[:], True, False, 128), (o, T.ONb[:], T.PK32[:], False, True, 128)]
+            mm(its, ["WA%d" % h, "PK", "PK32", "ONb"], ["B7"])
+            c = slice(256 * h, 256 * h + 256)
+            if MIS:
+                act(T.mi[:, c], B[7][:, 0:256], F.Identity, 256, ["B7"], ["mi%d" % h], bias=RND)
+                act(T.mi[:, c], T.mi[:, c], F.Identity, 256, ["mi%d" % h], ["mi%d" % h], bias=-RND)
+            else:
+                ts(T.mi[:, c], B[7][:, 0:256], RND, -RND, A.add, A.add, 256, ["B7"], ["mi%d" % h])
+            tt(T.MT[:, c], T.mi[:, c], B[7][:, 0:256], A.is_gt, 256, ["B7", "mi%d" % h], ["MT%d" % h])
+        for q in range(8):
+            mm([(B[6][:, 16 * q:16 * q + 16], T.OH[:, 128 * (8 * k + q):128 * (8 * k + q) + 128],
+                 T.MT[:, 128 * k + 16 * q:128 * k + 16 * q + 16], k == 0, k == 3, 16) for k in range(4)],
+               ["MT0", "MT1"] + ["OH%d" % (8 * k + q) for k in range(4)], ["B6"])
+        act(T.ki[:], B[6][:, 0:128], F.Identity, 128, ["B6"], ["ki"], scale=1.0 / 1024, bias=RND)
+        act(T.ki[:], T.ki[:], F.Identity, 128, ["ki"], ["ki"], scale=1024.0, bias=-1024.0 * RND)
+        act(T.nh[:, 128:256], T.ki[:], F.Relu, 128, ["ki"], ["nh1"], scale=-1.0, bias=1.0)
+        tt(T.nh[:, 0:128], B[6][:, 0:128], T.ki[:], A.is_equal, 128, ["B6", "ki"], ["nh0"])
+        mm([(B[7][:, 128 * f:128 * f + 128], T.nh[:, 128 * f:128 * f + 128], T.Ib[:], True, True, 128) for f in range(2)],
+           ["nh0", "nh1", "Ib"], ["B7"])
+        tt(T.cw[:], B[7][:, 0:256], T.Ws[:, cc], A.mult, 256, ["B7", "Ws" + p], ["cw"])
+        bits(t, T.cw[:], "cw", 6, T.zi[:, 512:768], "zc")
+        o = B[5][:, 0:256]
+        mm([(o, T.OBb[:], cC, True, False, 256), (o, T.OBm[:], first, False, False, 256), (o, T.In[:], qne, False, True, 256)],
+           ["OBb", "OBm", "cC", "In", "qne", "first" + p], ["B5"])
+        tt(T.pj[:], o, T.zi[:, cc], A.is_lt, 256, ["B5", "zi" + p], ["pj"])
+        ts(T.sg[:], T.zi[:, 512:768], -2.0 / K, 1.0 / K, A.mult, A.add, 256, ["zc"], ["sg"])
+        tt(T.NJ[:], T.NX[:, 0:512].indirect(PL), T.pj[:], A.mult, 256, NW + ["pj", pu], ["NJ"], GA)
+        mm([(B[6][:, 0:256], T.Ib[:], T.FWq[:, cc], True, True, 256)], ["Ib", "FWq" + p], ["B6"])
+        tt(T.SW[:], B[6][:, 0:256], T.sg[:], A.mult, 256, ["B6", "sg"], ["SW"])
+        if t == 0:
+            act(T.sc[:, 1:2], XL[:, 8192:8193], F.Identity, 1, [th], ["sc1"], scale=-K, bias=50.0 * K)
+        else:
+            mm([(B[5][:, 0:1], T.ONf[:], T.sc[:, 4:5], True, True, 1, 4)], ["ONf", "cnt"], ["B5"])
+            cp(T.si[:, 0:1], B[5][:, 0:1], 1, ["B5"], ["si"])
+            ts(T.si[:, 0:1], T.si[:, 0:1], 1, None, A.bitwise_and, None, 1, ["si"], ["si"])
+            tt(T.sc[:, 2:3], T.si[:, 0:1], XL[:, 8192:8193], A.add, 1, ["si", th], ["sc2"])
+            act(T.sc[:, 1:2], T.sc[:, 2:3], F.Identity, 1, ["sc2"], ["sc1"], scale=-K, bias=50.0 * K)
+        act(T.DJ[:], T.Ib[:], F.Copy, 128, ["Ib", "sc1"], ["DJ"], scale=T.sc[:, 1:2])
+
+    def back(t):
+        par = t & 1
+        lo = 0
+        for hi in CUTS:
+            piece(t, lo, hi)
+            lo = hi
+        c = slice(256 * par, 256 * par + 256)
+        if t < 3:
+            act(T.w[:], T.t[:], F.Sign, 256, ["t%d" % x for x in CUTS], ["w%d" % x for x in CUTS] + ["cnt"], acc=T.sc[:, 4:5])
+        if t == 2:
+            act(T.OC[:, 0::2], T.NX[:, c], F.Identity, 256, ["N0"], ["OC0"], bias=4095.0, scale=-1.0)
+
+    def piece(t, lo, hi):
+        par = t & 1
+        p, s, n = str(par), str(hi), hi - lo
+        c = slice(lo, hi)
+        d = slice(256 * par + lo, 256 * par + hi)
+        first = T.fl[:, 768 + 256 * par + lo:768 + 256 * par + hi]
+        sb = 3 if lo == 0 else 2
+        sn = "B%d" % sb
+        for q in range(lo // 64, hi // 64):
+            e = slice(64 * q, 64 * q + 64)
+            o = B[sb][:, e]
+            its = [(o, T.OBb[:], T.CST[:, e], True, False, 64), (o, T.D3[:], T.fl[:, 256 + 64 * q:320 + 64 * q], False, False, 64),
+                   (o, T.DJ[:], T.pj[:, e], False, False, 64), (o, T.D1[:], T.sg[:, e], False, False, 64)]
+            its += [(o, T.BM[:, 15 - j:143 - j], T.CM[:, 1024 * q + j:1024 * q + 1024:16], False, j == 15, 64) for j in range(16)]
+            mm(its, ["OBb", "cA", "D3", "qne", "DJ", "pj", "D1", "sg", "BM", "CM%d" % (2 * q), "CM%d" % (2 * q + 1)], [sn])
+        Sp, H0, H1 = B[sb][:, c], B[4][:, c], B[4][:, 256 + lo:256 + hi]
+        h0, h1 = "H0" + s, "H1" + s
+        tt(T.u[:, c], Sp, T.sg[:, c], A.mult, n, [sn, "sg"], ["u" + s])
+        tt(T.u[:, c], Sp, T.u[:, c], A.min, n, [sn, "u" + s], ["u" + s])
+        act(T.w[:, c], T.u[:, c], F.Exp, n, ["u" + s], ["w" + s], scale=6 * LN2)
+        tt(H0, Sp, T.thr[:, d], A.is_le, n, [sn, "thr" + p, "B4"], [h0])
+        tt(T.Np[:, c], H0, T.Ns[:, c], A.mult, n, [h0, "Ns"], ["Np" + s])
+        if t < 3:
+            tt(T.Wp[:, c], H0, T.Ws[:, d], A.mult, n, [h0, "Ws" + p], ["Wp" + s])
+        mm([(B[5][:, c], T.TRI[:], T.w[:, c], True, True, n)], ["TRI", "w" + s], ["B5"])
+        ts(H1, B[5][:, c], 0.0, None, A.is_lt, None, n, ["B5"], [h1])
+        tt(T.b[:, c], H1, T.SW[:, c], A.mult, n, [h1, "SW"], ["b" + s])
+        tt(T.a[:, c], H1, T.NJ[:, c], A.mult, n, [h1, "NJ"], ["a" + s])
+        its = [(B[7][:, c], T.OBn[:], T.b[:, c], True, True, n)]
+        if t < 3:
+            its.append((B[7][:, 256 + lo:256 + hi], T.OBp[:], T.b[:, c], True, True, n))
+        mm(its, ["OBn", "OBp", "b" + s], ["B7"])
+        mm([(B[6][:, c], T.OBf[:], T.a[:, c], True, True, n, 4)], ["OBf", "a" + s], ["B6"])
+        tt(H0, B[7][:, c], T.Ws[:, d], A.not_equal, n, ["B7", "Ws" + p], [h0])
+        tt(H1, H0, T.Np[:, c], A.mult, n, [h0, "Np" + s], [h1])
+        tt(T.t[:, c], B[6][:, c], first, A.mult, n, ["B6", "first" + p], ["t" + s])
+        if t < 3:
+            tt(T.NX[:, d], H1, T.t[:, c], A.add, n, [h1, "t" + s], ["N" + p])
+            tt(T.tw[:, c], B[7][:, 256 + lo:256 + hi], first, A.mult, n, ["B7", "first" + p], ["tw" + s])
+            tt(H0, H0, T.Wp[:, c], A.mult, n, [h0, "Wp" + s], [h0])
+            tt(T.WF[:, d], H0, T.tw[:, c], A.max, n, [h0, "tw" + s], ["WA" + p])
+        else:
+            tt(H1, H1, T.t[:, c], A.add, n, [h1, "t" + s], [h1])
+            ts(T.OC[:, 2 * lo + 1:2 * hi:2], H1, -1.0, 4095.0, A.mult, A.add, n, [h1], ["OC1"])
+
+
+    lists(0)
+    compare(0)
+    compare(1)
+    tops(0)
+    chain(0)
+    head(0)
+    tops(1)
+    scores(0)
+    lists(1)
+    chain(1)
+    lists(2)
+    chain(2)
+    lists(3)
+    frames()
+    onehot(0)
+    early(0)
+    masks(0)
+    chain(3)
+    parents_out()
+    for t in range(4):
+        if t > 0:
+            head(t)
+            scores(t)
+            masks(t)
+        if t < 3:
+            onehot(t + 1)
+            early(t + 1)
+        back(t)
+    return ops
+
+
+EXT = {"xcq": ("dcq", 2600), "xpt": ("dpt", 2300), "xth": ("dth", 2400), "xxs0": ("dxs", 7000), "xlim0": ("dlim", 11000),
+       "xxs1": ("arr1", 22000), "xlim1": ("arr1", 22000), "xxs2": ("arr2", 34000), "xlim2": ("arr2", 34000),
+       "xxs3": ("arr3", 46000), "xlim3": ("arr3", 46000)}
+
+
+def schedule(ops):
+    n = len(ops)
+    lastw, readers = {}, {}
+    deps = [set() for _ in range(n)]
+    for i, o in enumerate(ops):
+        rd, wr = list(o["r"]), list(o["w"])
+        for r in rd:
+            if r in lastw:
+                deps[i].add(lastw[r])
+            if r[0] == "B" and r[1:].isdigit():
+                deps[i].update(x for x in readers.get(r, []) if ops[x]["e"] != o["e"])
+        for r in wr:
+            if r in lastw:
+                deps[i].add(lastw[r])
+            deps[i].update(readers.get(r, []))
+        for r in rd:
+            readers.setdefault(r, []).append(i)
+        for r in wr:
+            lastw[r] = i
+            readers[r] = []
+        deps[i].discard(i)
+    succ = [[] for _ in range(n)]
+    for i in range(n):
+        for d in deps[i]:
+            succ[d].append(i)
+    if "start" not in CACHE:
+        CACHE["start"] = arrange(ops, deps, succ)
+    start = CACHE["start"]
+    for i in range(n):
+        ops[i]["t"] = start[i]
+    return sorted(range(n), key=lambda i: (start[i], i)), deps, succ, max(start[i] + ops[i]["c"] for i in range(n))
+
+
+CACHE = {}
+LAT = 130.0
+ROUNDS = 1500
+
+
+def place(seq, pre, eng, cost, rel):
+    line = {"V": [], "S": [], "P": [], "G": []}
+    st = [0.0] * len(seq)
+    for i in seq:
+        e, c, t = eng[i], cost[i], rel[i]
+        for d in pre[i]:
+            w = 0.0 if e == "P" and eng[d] == "P" else (0.5 * LAT if eng[d] == e else LAT)
+            t = max(t, st[d] + cost[d] + w)
+        ln = line[e]
+        lo, hi = 0, len(ln)
+        while lo < hi:
+            m = (lo + hi) // 2
+            if ln[m][1] <= t:
+                lo = m + 1
+            else:
+                hi = m
+        while lo < len(ln) and ln[lo][0] < t + c:
+            t = max(t, ln[lo][1])
+            lo += 1
+        ln.insert(lo, (t, t + c))
+        st[i] = t
+    return st
+
+
+def arrange(ops, deps, succ):
+    n = len(ops)
+    eng, cost = [o["e"] for o in ops], [o["c"] for o in ops]
+    rel = [max([EXT[r][1] for r in o["r"] if r in EXT] + [0.0]) for o in ops]
+    way = [0.0] * n
+    for i in range(n - 1, -1, -1):
+        way[i] = cost[i] + max([way[s] + LAT for s in succ[i]] + [0.0])
+    best, span, rnd = None, 1e18, 12345
+    for k in range(ROUNDS):
+        if best is None:
+            seq = sorted(range(n), key=lambda i: (-way[i], i))
+        else:
+            key = list(best)
+            rnd = (rnd * 1103515245 + 12345) % 2147483648
+            t0, amp = rnd / 2147483648.0 * span, (500.0, 1500.0, 4000.0)[k % 3]
+            for i in range(n):
+                if abs(best[i] - t0) < 9000:
+                    rnd = (rnd * 1103515245 + 12345) % 2147483648
+                    key[i] += rnd / 2147483648.0 * amp
+                for d in deps[i]:
+                    key[i] = max(key[i], key[d] + 1e-3)
+            seq = sorted(range(n), key=lambda i: (key[i], i))
+        st = place(seq, deps, eng, cost, rel)
+        for _r in range(6 if best is None else 1):
+            back = place(sorted(range(n), key=lambda i: (-st[i] - cost[i], -i)), succ, eng, cost, [0.0] * n)
+            st = place(sorted(range(n), key=lambda i: (-back[i] - cost[i], i)), deps, eng, cost, rel)
+            sp = max(st[i] + cost[i] for i in range(n))
+            if sp <= span:
+                best, span = st, sp
+    return best
+
+
+def rank_program(g, core, T, topo):
+    rank = T.rank_of(core)
+    if rank is None:
+        return
+    n = len(T.cores)
+    sem = T.sem
+    g.sync.dma_start(T.cqs[:], T.cq[:]).then_inc(sem.dcq, 16)
+    g.scalar.dma_start(T.pts[:], T.pt[:]).then_inc(sem.dpt, 16)
+    g.scalar.dma_start(T.ths[0:8, 0:2], T.th[:]).then_inc(sem.dth, 16)
+    g.sync.dma_start(T.XL0[:, 0:4096], T.xs[:]).then_inc(sem.dxs, 16)
+    g.sync.dma_start(T.XL0[:, 4096:8192], T.lim[:]).then_inc(sem.dlim, 16)
+
+    ops = build(g, T)
+    order, deps, succ, _ = schedule(ops)
+    Q = {"V": g.vector, "S": g.scalar, "P": g.tensor, "G": g}
+    SM = {"V": sem.sV, "S": sem.sS, "P": sem.sP, "G": sem.sG}
+    arrive = {}
+    for t in range(1, n):
+        arrive["arr%d" % t] = len(topo.engines(T.cores[(rank + t) % n], core))
+    count = {"V": 0, "S": 0, "P": 0, "G": 0}
+    seen = {}
+    mark = {}
+    outs = ("OP", "OC0", "OC1", "XLt0")
+    last = {}
+
+    def wait(e, name, s, v):
+        if seen.get((e, name), 0) < v:
+            Q[e].wait_ge(s, v)
+            seen[(e, name)] = v
+
+    for i in order:
+        o = ops[i]
+        e = o["e"]
+        for r in o["r"]:
+            if r in EXT:
+                wait(e, EXT[r][0], sem[EXT[r][0]], arrive.get(EXT[r][0], 16))
+        need = {}
+        for d in deps[i]:
+            de = ops[d]["e"]
+            if de == "P" and e == "P":
+                continue
+            need[de] = max(need.get(de, 0), mark[d])
+        for de in need:
+            wait(e, de, SM[de], need[de])
+        ins = o["f"]()
+        count[e] += 1
+        ins.then_inc(SM[e], 1)
+        mark[i] = count[e]
+        for r in o["w"]:
+            if r in outs:
+                last[r] = (e, count[e])
+
+    g.wait_ge(sem.dxs, 16)
+    g.wait_ge(sem.dlim, 16)
+    g.wait_ge(SM[last["XLt0"][0]], last["XLt0"][1])
+    sent = 0
+    for t in range(1, n):
+        dst = T.cores[(rank - t) % n]
+        rid, pid, _ = topo.addr(dst)
+        g.remote_dma(T["XL%d" % t][:], T.XL0[:], sem["arr%d" % t], sem.sent, pid, rid, topo.mask(core, dst))
+        sent += len(topo.engines(core, dst))
+        g.wait_ge(sem.sent, sent)
+
+    g.sync.wait_ge(SM[last["OP"][0]], last["OP"][1])
+    g.sync.dma_start(T.yp[:], T.OP[:]).then_inc(sem.dout, 16)
+    for r in ("OC0", "OC1"):
+        g.sync.wait_ge(SM[last[r][0]], last[r][1])
+    g.sync.dma_start(T.yc[:], T.OC[:]).then_inc(sem.dout, 16)
+    g.sync.wait_ge(sem.dout, 32)
+    for e in count:
+        g.sync.wait_ge(SM[e], count[e])

@@ -34,10 +34,10 @@ for _n, _c, _d in [
     ("AW0", 512, "bfloat16"), ("AW1", 512, "bfloat16"), ("AW3", 512, "bfloat16"),
     ("pci", 8, "int32"), ("pcf", 16, "float32"), ("IG", 128, "float32"), ("IJ", 128, "float32"),
     ("I144", 144, "float32"), ("IL", 32, "float32"), ("I128", 128, "bfloat16"),
-    ("EQ", 16, "bfloat16"), ("B0b", 144, "bfloat16"), ("CE", 768, "float16"), ("HX", 32, "float32"),
+    ("EQ", 16, "bfloat16"), ("B0b", 144, "bfloat16"), ("CE", 1024, "float16"), ("HX", 32, "float32"),
     ("OBm", 128, "bfloat16"),
-    ("OBf", 128, "float32"), ("OBb", 128, "bfloat16"), ("OBp", 128, "bfloat16"),
-    ("OBn", 128, "bfloat16"), ("ONf", 128, "float32"), ("ONb", 128, "bfloat16"),
+    ("OBf", 128, "float32"), ("OBb", 128, "bfloat16"), ("oc", 96, "float32"),
+    ("ox", 256, "bfloat16"), ("ONf", 128, "float32"), ("ONb", 128, "bfloat16"),
     ("Ih", 128, "float16"), ("Ib", 128, "bfloat16"), ("In", 128, "bfloat16"), ("Ihalf", 128, "bfloat16"),
     ("D1", 128, "bfloat16"), ("D3", 128, "bfloat16"), ("DJ", 128, "bfloat16"),
     ("L1", 128, "float16"), ("L2", 128, "float16"), ("BT", 2048, "float16"), ("BM", 144, "bfloat16"),
@@ -46,16 +46,16 @@ for _n, _c, _d in [
     ("CST", 1024, "bfloat16"), ("S8", 128, "bfloat16"),
     ("NC", 512, "float16"), ("QN", 512, "float16"), ("E", 2048, "bfloat16"), ("i5", 256, "int32"),
     ("b5", 512, "bfloat16"), ("t5", 512, "bfloat16"), ("f5", 512, "float32"), ("LT", 528, "float32"),
-    ("HL", 32, "float32"), ("tl", 192, "float32"), ("ti", 96, "int32"), ("PN", 512, "bfloat16"),
+    ("HL", 32, "float32"), ("tl", 192, "float32"), ("ti", 128, "int32"), ("PN", 512, "bfloat16"),
     ("QU", 256, "uint16"), ("QH", 256, "float16"), ("YH", 256, "float16"), ("YU", 16, "uint16"),
     ("XY", 256, "bfloat16"), ("XT", 256, "bfloat16"), ("hm", 256, "float32"), ("hi", 256, "int32"),
     ("HU", 256, "uint16"), ("XQ", 4096, "bfloat16"), ("AD", 2048, "float32"), ("CM", 4096, "bfloat16"),
     ("FWq", 512, "bfloat16"), ("FIq", 512, "bfloat16"), ("Ns", 256, "float32"), ("DG", 2048, "bfloat16"),
     ("Ws", 512, "bfloat16"), ("fl", 1280, "bfloat16"), ("thr", 512, "float32"), ("MT", 512, "bfloat16"),
-    ("mi", 512, "float32"), ("OH", 4096, "bfloat16"), ("ki", 128, "float32"), ("nh", 256, "bfloat16"),
+    ("mi", 512, "int32"), ("OH", 4096, "bfloat16"), ("ki", 128, "float32"), ("nh", 256, "bfloat16"),
     ("cw", 256, "bfloat16"), ("zi", 768, "int32"), ("pj", 256, "bfloat16"), ("sg", 256, "bfloat16"),
-    ("NJ", 256, "float32"), ("SW", 256, "bfloat16"), ("u", 256, "float32"), ("w", 256, "bfloat16"),
-    ("Np", 256, "float32"), ("Wp", 256, "bfloat16"), ("a", 256, "float32"), ("b", 256, "bfloat16"),
+    ("NJ", 256, "float32"), ("u", 256, "float32"), ("w", 256, "bfloat16"),
+    ("Wp", 256, "bfloat16"), ("a", 256, "float32"), ("b", 256, "bfloat16"),
     ("t", 256, "float32"), ("tw", 256, "bfloat16"), ("sc", 8, "float32"), ("si", 8, "int32"),
     ("OC", 512, "float32"), ("OP", 32, "float32"),
 ]:
@@ -63,11 +63,13 @@ for _n, _c, _d in [
 
 SEMAPHORES = ["sV", "sS", "sP", "sG", "dcq", "dpt", "dth", "dxs", "dlim", "dout", "sent", "arr1", "arr2", "arr3"]
 
-CY = 0.83 * 1.25
-PCY = 0.42 * 1.25
+CY = 0.83 * 1.1
+PCY = 0.42 * 1.1
 GA = 1.6
 CUTS = (128, 256)
-MIS = True
+PWC = (0, 2, 1, 3)
+NOH = (0, 0, 0, 0)
+NS1 = 0
 NS2 = 0
 
 
@@ -168,8 +170,7 @@ def build(g, T):
         ts(T.BT[:, 128 * j:128 * j + 128], T.OBb[:], T.EQ[:, j:j + 1], None, A.mult, None, 128, ["OBb", "EQ"], ["BT%d" % j], 0.5)
     for nm, v in (("In", -1.0), ("Ihalf", -0.5), ("D1", -25.5 * K * K), ("D3", -20.0 * K)):
         act(T[nm][:], T.Ib[:], F.Copy, 128, ["Ib"], [nm], scale=v)
-    for nm, v in (("OBm", -1.0), ("OBp", K), ("OBn", -K)):
-        act(T[nm][:], T.OBf[:], F.Copy, 128, ["OBf"], [nm], scale=v)
+    act(T.OBm[:], T.OBb[:], F.Copy, 128, ["OBb"], ["OBm"], scale=-1.0)
     ts(T.L1[:], T.BT[:, 0:128], 2080.0, None, A.mult, None, 128, ["BT0"], ["L1"], 0.5)
     ts(T.L2[:], T.Ih[:], 3232.0, None, A.mult, None, 128, ["Ih"], ["L2"], 0.5)
     ts(T.BM[:], T.I144[:], g16, K, A.is_equal, A.mult, 144, ["I144", "g16"], ["BM"])
@@ -213,23 +214,31 @@ def build(g, T):
     tt(T.NC[:], B[4][:], T.b5[:], A.add, 512, ["B4", "b5"], ["NC"])
     ts(T.CE[:, 0:256], T.NC[:, 0:256], -1.0, None, A.mult, None, 256, ["NC"], ["CE0"], 0.5)
     ts(T.CE[:, 256:768], T.NC[:], -1.0, None, A.mult, None, 512, ["NC"], ["CE1"], 0.5)
+    if NS1 < 8:
+        ts(T.CE[:, 768:1024], T.NC[:, 256:512], -1.0, None, A.mult, None, 256, ["NC"], ["CE2"], 0.5)
     act(T.PN[:], T.IC[:].indirect(PUn), F.Copy, 512, ["IC", "PUn"], ["PN"], GA)
     for h in range(2):
         act(T.PR0[:, 256 * h:256 * h + 256], T.PN[:, h::2], F.Copy, 256, ["PN"], ["PR0"])
 
     def lists(t):
         PR = T["PR%d" % t]
-        mm([(B[6][:, 0:32], T.B0b[:, 15 - w:143 - w], PR[:, w::16], w == 0, w == 15, 32) for w in range(16)],
-           ["B0b", "PR%d" % t], ["B6"])
-        ts(T.PU[:, 32 * t:32 * t + 32], B[6][:, 0:32], 256.0, None, A.add, None, 32, ["B6"], ["PU%d" % t])
-        act(T.PF[:, 32 * t:32 * t + 32], B[6][:, 0:32], F.Identity, 32, ["B6"], ["PF%d" % t], bias=256.0)
-        mm([(B[7][:, 8 * k:8 * k + 8], PR[:, 128 * k:128 * k + 128], T.B0b[:, 15:143:16], True, True, 8) for k in range(4)],
-           ["B0b", "PR%d" % t], ["B7"])
-        ts(T.ti[:, 0:32], B[7][:, 0:32], 256.0, None, A.add, None, 32, ["B7"], ["ti0"])
-        ts(T.ti[:, 32:64], T.ti[:, 0:32], 383, None, A.bitwise_and, None, 32, ["ti0"], ["ti1"])
-        ts(T.ti[:, 64:96], T.ti[:, 0:32], 128, None, A.bitwise_and, None, 32, ["ti0"], ["ti2"])
-        ts(T.PW[:, 64 * t:64 * t + 32], T.ti[:, 32:64], float(-256 * (t & 1)), None, A.add, None, 32, ["ti1"], ["PWa%d" % t])
-        ts(T.PW[:, 64 * t + 32:64 * t + 64], T.ti[:, 64:96], 1023.0 / 128, 1.0, A.mult, A.add, 32, ["ti2"], ["PWb%d" % t])
+        bk = 3 if t else 6
+        bn = "B%d" % bk
+        mm([(B[bk][:, 0:32], T.B0b[:, 15 - w:143 - w], PR[:, w::16], w == 0, w == 15, 32) for w in range(16)],
+           ["B0b", "PR%d" % t], [bn])
+        ts(T.PF[:, 32 * t:32 * t + 32], B[bk][:, 0:32], 256.0, None, A.add, None, 32, [bn], ["PF%d" % t])
+        ts(T.PU[:, 32 * t:32 * t + 32], B[bk][:, 0:32], 256.0, None, A.add, None, 32, [bn], ["PU%d" % t])
+
+    def columns(tt_):
+        par, m = tt_[0] & 1, 32 * len(tt_)
+        mm([(B[7][:, 32 * i + 8 * k:32 * i + 8 * k + 8], T["PR%d" % t][:, 128 * k:128 * k + 128], T.B0b[:, 15:143:16], True, True, 8)
+            for i, t in enumerate(tt_) for k in range(4)], ["B0b"] + ["PR%d" % t for t in tt_], ["B7"])
+        a = 32 * PWC[tt_[0]]
+        ts(T.ti[:, 0:m], B[7][:, 0:m], 512.0 if par else 256.0, None, A.add, None, m, ["B7"], ["ti0", "ti1"])
+        ts(T.ti[:, 64:64 + m], T.ti[:, 0:m], 128, None, A.bitwise_and, None, m, ["ti0", "ti1"], ["ti2"])
+        ts(T.ti[:, 0:m], T.ti[:, 0:m], 383, None, A.bitwise_and, None, m, ["ti0", "ti1"], ["ti0", "ti1"])
+        cp(T.PW[:, a:a + m], T.ti[:, 0:m], m, ["ti0", "ti1"], ["PWa%d" % t for t in tt_])
+        ts(T.PW[:, 128 + a:128 + a + m], T.ti[:, 64:64 + m], 1023.0 / 128, 1.0, A.mult, A.add, m, ["ti2"], ["PWb%d" % t for t in tt_])
 
     def compare(h):
         c = slice(256 * h, 256 * h + 256)
@@ -237,25 +246,26 @@ def build(g, T):
         for n in range(8):
             bk, eb = (n % 2, n % 2) if h == 0 else (2 + 2 * (n % 2), 2 + n % 2)
             its = []
+            sgn = h and (n * NS1) // 8 != ((n + 1) * NS1) // 8
             for i in range(2):
                 o, j = B[bk][:, 256 * i:256 * i + 256], 2 * n + i
-                if h:
+                if sgn:
                     its.append((o, T.Ih[:], T.NC[:, c], True, False, 256))
-                its.append((o, T.BT[:, 128 * j:128 * j + 128], T.QN[:, h::2], h == 0, True, 256))
+                its.append((o, T.BT[:, 128 * j:128 * j + 128], T.QN[:, h::2], not sgn, True, 256))
             mm(its, ["Ih", "NC", "QN", "BT%d" % (2 * n), "BT%d" % (2 * n + 1)], ["B%d" % bk])
             e = T.E[:, 512 * eb:512 * eb + 512]
-            if h:
+            if sgn:
                 act(e, B[bk][:], F.Sign, 512, ["B%d" % bk], ["E%d" % eb])
             else:
-                tt(e, B[bk][:], T.CE[:, 0:512], A.is_equal, 512, ["B%d" % bk, "CE0", "CE1"], ["E%d" % eb])
+                tt(e, B[bk][:], T.CE[:, 512 * h:512 * h + 512], A.is_equal, 512, ["B%d" % bk, "CE1", "CE%d" % (2 * h)], ["E%d" % eb])
             mm([(B[sb][:, 0:256], T.Ib[:], T.E[:, 512 * eb + 256 * i:512 * eb + 256 * i + 256], n + i == 0, n + i == 8, 256)
                 for i in range(2)], ["Ib", "E%d" % eb], ["B%d" % sb])
-        if h:
+        if h and NS1:
             cp(T.i5[:], B[sb][:, 0:256], 256, ["B5"], ["i5"])
             ts(T.i5[:], T.i5[:], 1, None, A.bitwise_and, None, 256, ["i5"], ["i5"])
             tt(T.t5[:, c], T.b5[:, c], T.i5[:], A.is_gt, 256, ["b5", "i5"], ["t51"], 2)
         else:
-            tt(T.t5[:, c], B[sb][:, 0:256], T.b5[:, c], A.is_lt, 256, ["B3", "b5"], ["t50"])
+            tt(T.t5[:, c], B[sb][:, 0:256], T.b5[:, c], A.is_lt, 256, ["B%d" % sb, "b5"], ["t5%d" % h])
 
     def tops(h):
         c = slice(256 * h, 256 * h + 256)
@@ -340,11 +350,21 @@ def build(g, T):
         act(T.FI[:, 0:512], T.f5[:], F.Exp, 512, f5, ["FI"], scale=-LN2)
 
     def onehot(t):
+        a, ns = 32 * PWC[t], NOH[t]
+        if ns:
+            act(T.oc[:, 0:32], T.PW[:, a:a + 32], F.Copy, 32, ["PWa%d" % t], ["oc0"], scale=-1.0)
+            act(T.oc[:, 32:64], T.PW[:, 128 + a:160 + a], F.Copy, 32, ["PWb%d" % t], ["oc1"], scale=-1.0)
         for q in range(8):
             for k in range(4):
                 i = 8 * k + q
-                ts(T.OH[:, 128 * i:128 * i + 128], T.I128[:], T.PW[:, 64 * t + i:64 * t + i + 1],
-                   T.PW[:, 64 * t + 32 + i:64 * t + 33 + i], A.is_equal, A.mult,
+                if 4 * q + k < ns:
+                    x = T.ox[:, 128 * (k & 1):128 * (k & 1) + 128]
+                    act(x, T.I128[:], F.Abs, 128, ["I128", "oc0"], ["ox%d" % (k & 1)], bias=T.oc[:, i:i + 1])
+                    act(T.OH[:, 128 * i:128 * i + 128], x, F.Relu, 128, ["ox%d" % (k & 1), "oc1", "PWb%d" % t], ["OH%d" % i],
+                        scale=T.oc[:, 32 + i:33 + i], bias=T.PW[:, 128 + a + i:129 + a + i])
+                    continue
+                ts(T.OH[:, 128 * i:128 * i + 128], T.I128[:], T.PW[:, 32 * PWC[t] + i:32 * PWC[t] + i + 1],
+                   T.PW[:, 128 + 32 * PWC[t] + i:129 + 32 * PWC[t] + i], A.is_equal, A.mult,
                    128, ["I128", "PWa%d" % t, "PWb%d" % t], ["OH%d" % i], 0.5)
 
     def head(t):
@@ -416,7 +436,13 @@ def build(g, T):
         act(T.sc[:, 0:1], XL[:, 8193:8194], F.Identity, 1, [th], ["sc0"], scale=K, bias=-50.0 * K - BIG)
         act(T.thr[:, c], T.STP[:].indirect(Lw), F.Identity, 256, ["STP", "STP1", lu + "W", "sc0"], ["thr" + p], GA,
             bias=BIG, scale=T.sc[:, 0:1])
-        b1, b2 = (1, 0) if t else (5, 7)
+
+    def early2(t):
+        par = t & 1
+        p = str(par)
+        c = slice(256 * par, 256 * par + 256)
+        ne = T.fl[:, 0:256]
+        b1, b2 = (3, 3) if t else (5, 4)
         mm([(B[b2][:, 0:256], T.FST[:], ne, True, True, 256)], ["FST", "ne"], ["B%d" % b2])
         act(T.fl[:, 768 + 256 * par:1024 + 256 * par], B[b2][:, 0:256], F.Relu, 256, ["B%d" % b2, "k1"], ["first" + p], bias=k1)
         bits(t, T.Ws[:, c], "Ws" + p, b1, T.zi[:, c], "zi" + p)
@@ -435,25 +461,23 @@ def build(g, T):
         act(T.Ns[:], T.NX[:, 0:512].indirect(Ln), F.Copy, 256, NW + [lu + "N"], ["Ns"], GA)
         for h in ((0, 1) if t == 0 else (1 - par,)):
             its = []
+            bk = 6 if t == 0 and h else 7
+            bn = "B%d" % bk
             for k in (2 * h, 2 * h + 1):
-                o = B[7][:, 128 * (k & 1):128 * (k & 1) + 128]
+                o = B[bk][:, 128 * (k & 1):128 * (k & 1) + 128]
                 its += [(o, T.WF[:, 128 * k:128 * k + 128], T.PK[:], True, False, 128), (o, T.ONb[:], T.PK32[:], False, True, 128)]
-            mm(its, ["WA%d" % h, "PK", "PK32", "ONb"], ["B7"])
+            mm(its, ["WA%d" % h, "PK", "PK32", "ONb"], [bn])
             c = slice(256 * h, 256 * h + 256)
-            if MIS:
-                act(T.mi[:, c], B[7][:, 0:256], F.Identity, 256, ["B7"], ["mi%d" % h], bias=RND)
-                act(T.mi[:, c], T.mi[:, c], F.Identity, 256, ["mi%d" % h], ["mi%d" % h], bias=-RND)
-            else:
-                ts(T.mi[:, c], B[7][:, 0:256], RND, -RND, A.add, A.add, 256, ["B7"], ["mi%d" % h])
-            tt(T.MT[:, c], T.mi[:, c], B[7][:, 0:256], A.is_gt, 256, ["B7", "mi%d" % h], ["MT%d" % h])
+            cp(T.mi[:, c], B[bk][:, 0:256], 256, [bn], ["mi%d" % h])
+            tt(T.MT[:, c], T.mi[:, c], B[bk][:, 0:256], A.is_gt, 256, [bn, "mi%d" % h], ["MT%d" % h])
         for q in range(8):
-            mm([(B[6][:, 16 * q:16 * q + 16], T.OH[:, 128 * (8 * k + q):128 * (8 * k + q) + 128],
+            mm([(B[2][:, 16 * q:16 * q + 16], T.OH[:, 128 * (8 * k + q):128 * (8 * k + q) + 128],
                  T.MT[:, 128 * k + 16 * q:128 * k + 16 * q + 16], k == 0, k == 3, 16) for k in range(4)],
-               ["MT0", "MT1"] + ["OH%d" % (8 * k + q) for k in range(4)], ["B6"])
-        act(T.ki[:], B[6][:, 0:128], F.Identity, 128, ["B6"], ["ki"], scale=1.0 / 1024, bias=RND)
+               ["MT0", "MT1"] + ["OH%d" % (8 * k + q) for k in range(4)], ["B2"])
+        act(T.ki[:], B[2][:, 0:128], F.Identity, 128, ["B2"], ["ki"], scale=1.0 / 1024, bias=RND)
         act(T.ki[:], T.ki[:], F.Identity, 128, ["ki"], ["ki"], scale=1024.0, bias=-1024.0 * RND)
         act(T.nh[:, 128:256], T.ki[:], F.Relu, 128, ["ki"], ["nh1"], scale=-1.0, bias=1.0)
-        tt(T.nh[:, 0:128], B[6][:, 0:128], T.ki[:], A.is_equal, 128, ["B6", "ki"], ["nh0"])
+        tt(T.nh[:, 0:128], B[2][:, 0:128], T.ki[:], A.is_equal, 128, ["B2", "ki"], ["nh0"])
         mm([(B[7][:, 128 * f:128 * f + 128], T.nh[:, 128 * f:128 * f + 128], T.Ib[:], True, True, 128) for f in range(2)],
            ["nh0", "nh1", "Ib"], ["B7"])
         tt(T.cw[:], B[7][:, 0:256], T.Ws[:, cc], A.mult, 256, ["B7", "Ws" + p], ["cw"])
@@ -464,12 +488,11 @@ def build(g, T):
         tt(T.pj[:], o, T.zi[:, cc], A.is_lt, 256, ["B5", "zi" + p], ["pj"])
         ts(T.sg[:], T.zi[:, 512:768], -2.0 / K, 1.0 / K, A.mult, A.add, 256, ["zc"], ["sg"])
         tt(T.NJ[:], T.NX[:, 0:512].indirect(PL), T.pj[:], A.mult, 256, NW + ["pj", pu], ["NJ"], GA)
-        mm([(B[6][:, 0:256], T.Ib[:], T.FWq[:, cc], True, True, 256)], ["Ib", "FWq" + p], ["B6"])
-        tt(T.SW[:], B[6][:, 0:256], T.sg[:], A.mult, 256, ["B6", "sg"], ["SW"])
         if t == 0:
             act(T.sc[:, 1:2], XL[:, 8192:8193], F.Identity, 1, [th], ["sc1"], scale=-K, bias=50.0 * K)
         else:
-            mm([(B[5][:, 0:1], T.ONf[:], T.sc[:, 4:5], True, True, 1, 4)], ["ONf", "cnt"], ["B5"])
+            mm([(B[5][:, 0:1], T.ONf[:], T.sc[:, 4 + k:5 + k], k == 0, k == len(CUTS) - 1, 1, 4) for k in range(len(CUTS))],
+               ["ONf"] + ["cnt%d" % x for x in CUTS], ["B5"])
             cp(T.si[:, 0:1], B[5][:, 0:1], 1, ["B5"], ["si"])
             ts(T.si[:, 0:1], T.si[:, 0:1], 1, None, A.bitwise_and, None, 1, ["si"], ["si"])
             tt(T.sc[:, 2:3], T.si[:, 0:1], XL[:, 8192:8193], A.add, 1, ["si", th], ["sc2"])
@@ -481,10 +504,10 @@ def build(g, T):
         lo = 0
         for hi in CUTS:
             piece(t, lo, hi)
+            if lo == 0 and t < 3:
+                early2(t + 1)
             lo = hi
         c = slice(256 * par, 256 * par + 256)
-        if t < 3:
-            act(T.w[:], T.t[:], F.Sign, 256, ["t%d" % x for x in CUTS], ["w%d" % x for x in CUTS] + ["cnt"], acc=T.sc[:, 4:5])
         if t == 2:
             act(T.OC[:, 0::2], T.NX[:, c], F.Identity, 256, ["N0"], ["OC0"], bias=4095.0, scale=-1.0)
 
@@ -509,38 +532,38 @@ def build(g, T):
         tt(T.u[:, c], Sp, T.u[:, c], A.min, n, [sn, "u" + s], ["u" + s])
         act(T.w[:, c], T.u[:, c], F.Exp, n, ["u" + s], ["w" + s], scale=6 * LN2)
         tt(H0, Sp, T.thr[:, d], A.is_le, n, [sn, "thr" + p, "B4"], [h0])
-        tt(T.Np[:, c], H0, T.Ns[:, c], A.mult, n, [h0, "Ns"], ["Np" + s])
-        if t < 3:
-            tt(T.Wp[:, c], H0, T.Ws[:, d], A.mult, n, [h0, "Ws" + p], ["Wp" + s])
+        tt(T.Wp[:, c], H0, T.Ws[:, d], A.mult, n, [h0, "Ws" + p], ["Wp" + s])
         mm([(B[5][:, c], T.TRI[:], T.w[:, c], True, True, n)], ["TRI", "w" + s], ["B5"])
         ts(H1, B[5][:, c], 0.0, None, A.is_lt, None, n, ["B5"], [h1])
-        tt(T.b[:, c], H1, T.SW[:, c], A.mult, n, [h1, "SW"], ["b" + s])
+        tt(T.b[:, c], H1, T.FWq[:, d], A.mult, n, [h1, "FWq" + p], ["b" + s])
         tt(T.a[:, c], H1, T.NJ[:, c], A.mult, n, [h1, "NJ"], ["a" + s])
-        its = [(B[7][:, c], T.OBn[:], T.b[:, c], True, True, n)]
-        if t < 3:
-            its.append((B[7][:, 256 + lo:256 + hi], T.OBp[:], T.b[:, c], True, True, n))
-        mm(its, ["OBn", "OBp", "b" + s], ["B7"])
-        mm([(B[6][:, c], T.OBf[:], T.a[:, c], True, True, n, 4)], ["OBf", "a" + s], ["B6"])
-        tt(H0, B[7][:, c], T.Ws[:, d], A.not_equal, n, ["B7", "Ws" + p], [h0])
-        tt(H1, H0, T.Np[:, c], A.mult, n, [h0, "Np" + s], [h1])
-        tt(T.t[:, c], B[6][:, c], first, A.mult, n, ["B6", "first" + p], ["t" + s])
+        bw, bn = (7, 6) if lo == 0 else (0, 1)
+        wn, nn = "B%d" % bw, "B%d" % bn
+        mm([(B[bw][:, c], T.OBb[:], T.b[:, c], True, True, n)], ["OBb", "b" + s], [wn])
+        mm([(B[bn][:, c], T.OBf[:], T.a[:, c], True, True, n, 4)], ["OBf", "a" + s], [nn])
+        tt(H0, B[bw][:, c], T.Wp[:, c], A.not_equal, n, [wn, "Wp" + s], [h0])
+        tt(H1, H0, T.Ns[:, c], A.mult, n, [h0, "Ns"], [h1])
+        tt(T.t[:, c], B[bn][:, c], first, A.mult, n, [nn, "first" + p], ["t" + s])
         if t < 3:
             tt(T.NX[:, d], H1, T.t[:, c], A.add, n, [h1, "t" + s], ["N" + p])
-            tt(T.tw[:, c], B[7][:, 256 + lo:256 + hi], first, A.mult, n, ["B7", "first" + p], ["tw" + s])
+            k = 4 + CUTS.index(hi)
+            act(T.w[:, c], T.t[:, c], F.Sign, n, ["t" + s], ["w" + s, "cnt" + s], acc=T.sc[:, k:k + 1])
+            tt(T.tw[:, c], B[bw][:, c], T.w[:, c], A.mult, n, [wn, "w" + s], ["tw" + s])
             tt(H0, H0, T.Wp[:, c], A.mult, n, [h0, "Wp" + s], [h0])
             tt(T.WF[:, d], H0, T.tw[:, c], A.max, n, [h0, "tw" + s], ["WA" + p])
         else:
             tt(H1, H1, T.t[:, c], A.add, n, [h1, "t" + s], [h1])
-            ts(T.OC[:, 2 * lo + 1:2 * hi:2], H1, -1.0, 4095.0, A.mult, A.add, n, [h1], ["OC1"])
+            ts(T.OC[:, 2 * lo + 1:2 * hi:2], H1, -1.0, 4095.0, A.mult, A.add, n, [h1], ["OC" + s])
 
 
     lists(0)
+    columns((0,))
     compare(0)
     compare(1)
     tops(0)
+    tops(1)
     chain(0)
     head(0)
-    tops(1)
     scores(0)
     lists(1)
     chain(1)
@@ -550,7 +573,10 @@ def build(g, T):
     frames()
     onehot(0)
     early(0)
+    early2(0)
     masks(0)
+    columns((1, 3))
+    columns((2,))
     chain(3)
     parents_out()
     for t in range(4):
@@ -604,8 +630,8 @@ def schedule(ops):
 
 
 CACHE = {}
-LAT = 130.0
-ROUNDS = 1500
+LAT = 220.0
+ROUNDS = 4500
 
 
 def place(seq, pre, eng, cost, rel):
@@ -684,19 +710,41 @@ def rank_program(g, core, T, topo):
     for t in range(1, n):
         arrive["arr%d" % t] = len(topo.engines(T.cores[(rank + t) % n], core))
     count = {"V": 0, "S": 0, "P": 0, "G": 0}
-    seen = {}
     mark = {}
-    outs = ("OP", "OC0", "OC1", "XLt0")
+    outs = ["OP", "OC0", "XLt0"] + ["OC%d" % x for x in CUTS]
     last = {}
 
+    known = {e: {} for e in Q}
+    after = {}
+
     def wait(e, name, s, v):
-        if seen.get((e, name), 0) < v:
+        if known[e].get(name, 0) < v:
             Q[e].wait_ge(s, v)
-            seen[(e, name)] = v
+            known[e][name] = v
+            for k, x in after.get((name, v), {}).items():
+                known[e][k] = max(known[e].get(k, 0), x)
+
+    sent = [0, 0]
+
+    def send():
+        t = sent[0] + 1
+        if t == 1:
+            wait("G", "dxs", sem.dxs, 16)
+            wait("G", "dlim", sem.dlim, 16)
+            wait("G", last["XLt0"][0], SM[last["XLt0"][0]], last["XLt0"][1])
+        else:
+            g.wait_ge(sem.sent, sent[1])
+        dst = T.cores[(rank - t) % n]
+        rid, pid, _ = topo.addr(dst)
+        g.remote_dma(T["XL%d" % t][:], T.XL0[:], sem["arr%d" % t], sem.sent, pid, rid, topo.mask(core, dst))
+        sent[0] = t
+        sent[1] += len(topo.engines(core, dst))
 
     for i in order:
         o = ops[i]
         e = o["e"]
+        if e == "G" and sent[0] == 0 and o["t"] >= EXT["xlim0"][1] and last.get("XLt0", "G")[0] == "V":
+            send()
         for r in o["r"]:
             if r in EXT:
                 wait(e, EXT[r][0], sem[EXT[r][0]], arrive.get(EXT[r][0], 16))
@@ -706,32 +754,29 @@ def rank_program(g, core, T, topo):
             if de == "P" and e == "P":
                 continue
             need[de] = max(need.get(de, 0), mark[d])
-        for de in need:
+        for de in sorted(need, key=lambda x: x == e):
             wait(e, de, SM[de], need[de])
         ins = o["f"]()
         count[e] += 1
         ins.then_inc(SM[e], 1)
         mark[i] = count[e]
+        after[(e, count[e])] = dict(known[e])
         for r in o["w"]:
             if r in outs:
                 last[r] = (e, count[e])
-
-    g.wait_ge(sem.dxs, 16)
-    g.wait_ge(sem.dlim, 16)
-    g.wait_ge(SM[last["XLt0"][0]], last["XLt0"][1])
-    sent = 0
-    for t in range(1, n):
-        dst = T.cores[(rank - t) % n]
-        rid, pid, _ = topo.addr(dst)
-        g.remote_dma(T["XL%d" % t][:], T.XL0[:], sem["arr%d" % t], sem.sent, pid, rid, topo.mask(core, dst))
-        sent += len(topo.engines(core, dst))
-        g.wait_ge(sem.sent, sent)
+    while sent[0] < n - 1:
+        send()
+    g.wait_ge(sem.sent, sent[1])
 
     g.sync.wait_ge(SM[last["OP"][0]], last["OP"][1])
     g.sync.dma_start(T.yp[:], T.OP[:]).then_inc(sem.dout, 16)
-    for r in ("OC0", "OC1"):
-        g.sync.wait_ge(SM[last[r][0]], last[r][1])
-    g.sync.dma_start(T.yc[:], T.OC[:]).then_inc(sem.dout, 16)
-    g.sync.wait_ge(sem.dout, 32)
+    g.sync.wait_ge(SM[last["OC0"][0]], last["OC0"][1])
+    lo = 0
+    for hi in CUTS:
+        r = last["OC%d" % hi]
+        g.sync.wait_ge(SM[r[0]], r[1])
+        g.sync.dma_start(T.yc[:, 2 * lo:2 * hi], T.OC[:, 2 * lo:2 * hi]).then_inc(sem.dout, 16)
+        lo = hi
+    g.sync.wait_ge(sem.dout, 16 + 16 * len(CUTS))
     for e in count:
         g.sync.wait_ge(SM[e], count[e])

@@ -6,8 +6,7 @@ F = ActivationFunctionType
 LN2 = math.log(2.0)
 XW = 8208
 XO = 520
-K = 64.0
-BIG = 8192.0
+KL = 6 * LN2
 RND = 1.5 * 2.0 ** 23
 
 SCRATCH = {}
@@ -20,622 +19,553 @@ def _sb(name, cols, dtype):
 for _i in range(4):
     _sb("XL%d" % _i, XW, "bfloat16")
     _sb("PR%d" % _i, 512, "bfloat16")
-_sb("LU", 288, "uint16")
-_sb("PU", 160, "uint16")
-_sb("PF", 128, "float32")
-_sb("PW", 256, "bfloat16")
-_sb("AB", 64, "float32")
 for _i in range(8):
     SCRATCH["B%d" % _i] = ("psum", [128, 512], "float32")
 for _n, _c, _d in [
     ("cqs", 512, "int32"), ("pts", 32, "int32"), ("ths", 8, "int32"), ("thb", 8, "bfloat16"),
-    ("NX", 1040, "float32"), ("WF", 1024, "bfloat16"), ("FI", 528, "bfloat16"),
-    ("IC", 512, "bfloat16"), ("NAT", 512, "bfloat16"), ("STP", 1024, "bfloat16"),
+    ("LU", 192, "uint16"), ("PU", 160, "uint16"), ("PF", 128, "float32"), ("PW", 64, "bfloat16"),
+    ("NX", 1040, "float32"), ("WF", 528, "bfloat16"), ("TH", 768, "bfloat16"),
+    ("IC", 512, "bfloat16"), ("NAT", 512, "bfloat16"), ("PERM", 512, "bfloat16"),
     ("AW0", 512, "bfloat16"), ("AW1", 512, "bfloat16"), ("AW3", 512, "bfloat16"),
     ("pci", 8, "int32"), ("pcf", 16, "float32"), ("IG", 128, "float32"), ("IJ", 128, "float32"),
-    ("I144", 144, "float32"), ("IL", 32, "float32"), ("I128", 128, "bfloat16"),
+    ("I144", 144, "float32"), ("IL", 32, "float32"), ("I256", 256, "bfloat16"),
     ("EQ", 16, "bfloat16"), ("B0b", 144, "bfloat16"), ("CE", 1024, "float16"), ("HX", 32, "float32"),
-    ("OBm", 128, "bfloat16"),
-    ("OBf", 128, "float32"), ("OBb", 128, "bfloat16"), ("oc", 96, "float32"),
-    ("ox", 256, "bfloat16"), ("ONf", 128, "float32"), ("ONb", 128, "bfloat16"),
-    ("Ih", 128, "float16"), ("Ib", 128, "bfloat16"), ("In", 128, "bfloat16"), ("Ihalf", 128, "bfloat16"),
-    ("D1", 128, "bfloat16"), ("D3", 128, "bfloat16"), ("DJ", 128, "bfloat16"),
+    ("OBf", 128, "float32"), ("OBb", 128, "bfloat16"), ("OBh", 128, "float16"), ("Ifn", 128, "float32"),
+    ("ONE", 512, "bfloat16"), ("NEG", 256, "bfloat16"), ("RT", 256, "bfloat16"),
+    ("Ihn", 128, "float16"), ("In", 128, "bfloat16"), ("DG", 17 * 128, "bfloat16"),
+    ("N35", 128, "bfloat16"), ("D10", 128, "bfloat16"), ("N256", 128, "bfloat16"), ("N60", 128, "bfloat16"),
+    ("MJ", 128, "bfloat16"), ("O2k", 128, "bfloat16"), ("O6k", 128, "bfloat16"), ("O8k", 128, "bfloat16"),
+    ("PW2", 128, "bfloat16"),
     ("L1", 128, "float16"), ("L2", 128, "float16"), ("BT", 2048, "float16"), ("BM", 144, "bfloat16"),
     ("B0h", 144, "float16"), ("EX", 2048, "bfloat16"), ("FST", 128, "bfloat16"), ("TRI", 128, "bfloat16"),
-    ("PK", 128, "bfloat16"), ("PK32", 128, "bfloat16"), ("c1", 128, "bfloat16"),
-    ("CST", 1024, "bfloat16"), ("S8", 128, "bfloat16"),
-    ("NC", 512, "float16"), ("QN", 512, "float16"), ("E", 2048, "bfloat16"), ("i5", 256, "int32"),
-    ("b5", 512, "bfloat16"), ("t5", 512, "bfloat16"), ("f5", 512, "float32"), ("LT", 528, "float32"),
-    ("HL", 32, "float32"), ("tl", 192, "float32"), ("ti", 128, "int32"), ("PN", 512, "bfloat16"),
+    ("PK", 128, "bfloat16"), ("PKn", 128, "bfloat16"), ("PK32", 128, "bfloat16"), ("c1", 128, "bfloat16"),
+    ("S8", 128, "bfloat16"), ("QN", 512, "float16"), ("E", 2048, "bfloat16"),
+    ("ne", 512, "bfloat16"), ("t5", 512, "bfloat16"), ("f5", 512, "float32"),
+    ("HL", 64, "float32"), ("tl", 192, "float32"), ("ti", 128, "int32"), ("PN", 512, "bfloat16"),
+    ("CL", 64, "float16"), ("CD", 1024, "bfloat16"), ("first", 512, "bfloat16"),
     ("QU", 256, "uint16"), ("QH", 256, "float16"), ("YH", 256, "float16"), ("YU", 16, "uint16"),
     ("XY", 256, "bfloat16"), ("XT", 256, "bfloat16"), ("hm", 256, "float32"), ("hi", 256, "int32"),
     ("HU", 256, "uint16"), ("XQ", 4096, "bfloat16"), ("AD", 2048, "float32"), ("CM", 4096, "bfloat16"),
-    ("FWq", 512, "bfloat16"), ("FIq", 512, "bfloat16"), ("Ns", 256, "float32"), ("DG", 2048, "bfloat16"),
-    ("Ws", 512, "bfloat16"), ("fl", 1280, "bfloat16"), ("thr", 512, "float32"), ("MT", 512, "bfloat16"),
-    ("mi", 512, "int32"), ("OH", 4096, "bfloat16"), ("ki", 128, "float32"), ("nh", 256, "bfloat16"),
-    ("cw", 256, "bfloat16"), ("zi", 768, "int32"), ("pj", 256, "bfloat16"), ("sg", 256, "bfloat16"),
-    ("NJ", 256, "float32"), ("u", 256, "float32"), ("w", 256, "bfloat16"),
-    ("Wp", 256, "bfloat16"), ("a", 256, "float32"), ("b", 256, "bfloat16"),
-    ("t", 256, "float32"), ("tw", 256, "bfloat16"), ("sc", 8, "float32"), ("si", 8, "int32"),
-    ("OC", 512, "float32"), ("OP", 32, "float32"),
+    ("Ns", 256, "float32"), ("Nx", 256, "float32"), ("thr", 256, "float32"), ("MT", 512, "bfloat16"),
+    ("OH", 8192, "bfloat16"), ("ki", 128, "float32"), ("nh", 256, "bfloat16"), ("cw", 512, "bfloat16"),
+    ("cb", 256, "bfloat16"), ("b3", 256, "bfloat16"), ("q", 256, "bfloat16"), ("pj", 256, "bfloat16"),
+    ("wA", 256, "bfloat16"), ("wB", 256, "bfloat16"), ("H", 512, "bfloat16"),
+    ("KP", 256, "bfloat16"), ("p", 512, "float16"), ("AB", 256, "float32"),
+    ("sc", 16, "float32"), ("si", 8, "int32"), ("cn", 8, "bfloat16"), ("OC", 512, "float32"), ("OP", 32, "float32"),
 ]:
     _sb(_n, _c, _d)
 
 SEMAPHORES = ["sV", "sS", "sP", "sG", "dcq", "dpt", "dth", "dxs", "dlim", "dout", "sent", "arr1", "arr2", "arr3"]
 
-CY = 0.83 * 1.1
-PCY = 0.42 * 1.1
-GA = 1.6
-CUTS = (128, 256)
-PWC = (0, 2, 1, 3)
-NOH = (0, 0, 0, 0)
-NS1 = 0
-NS2 = 0
+CY = 0.83
+PCY = 0.42
+GA = 1.56
+VQ = ((), (1, 3), (1, 3), (1, 3))
+
+
+def r(name, lo=0, hi=None, st=1, p=None):
+    return (name, lo, SCRATCH[name][1][1] if hi is None else hi, st, p, None)
+
+
+def ind(win, off):
+    return win[:5] + (off,)
+
+
+def cols(x):
+    return 16 * cols(x[5]) if x[5] else (x[2] - x[1] + x[3] - 1) // x[3]
+
+
+def psum(x):
+    return SCRATCH[x[0]][0] == "psum"
+
+
+def narrow(x):
+    return SCRATCH[x[0]][2] in ("bfloat16", "float16", "uint16")
 
 
 def build(g, T):
     ops = []
     V, S, P = g.vector, g.scalar, g.tensor
 
+    def ap(x):
+        if not isinstance(x, tuple):
+            return x
+        c = slice(x[1], x[2], x[3]) if x[3] > 1 else slice(x[1], x[2])
+        a = T[x[0]][slice(x[4][0], x[4][1]) if x[4] else slice(None), c]
+        return a.indirect(ap(x[5])) if x[5] else a
+
     def op(eng, ns, rd, wr, fn):
-        ops.append({"e": eng, "c": ns, "r": rd, "w": wr, "f": fn})
+        rd = [x for x in rd if isinstance(x, tuple)]
+        ops.append({"e": eng, "c": ns, "r": rd + [x[5] for x in rd if x[5]], "w": wr, "f": fn})
 
-    def vc(n, f):
-        return 30 + max(64.0, n * f) * CY
+    def vc(out, in0, f):
+        if in0[5]:
+            return 50 + cols(out) * GA * CY
+        return 35 + max(64.0, cols(out) * f) * CY
 
-    def ts(out, in0, s1, s2, o0, o1, n, rd, wr, f=1.0):
+    def ts(out, in0, s1, s2, o0, o1=None):
+        c = vc(out, in0, 0.5 if narrow(out) and narrow(in0) else 1)
         if s2 is None:
-            op("V", vc(n, f), rd, wr, lambda: V.tensor_scalar(out, in0, s1, None, o0))
+            op("V", c, [in0, s1], [out], lambda: V.tensor_scalar(ap(out), ap(in0), ap(s1), None, o0))
         else:
-            op("V", vc(n, f), rd, wr, lambda: V.tensor_scalar(out, in0, s1, s2, o0, o1))
+            op("V", c, [in0, s1, s2], [out], lambda: V.tensor_scalar(ap(out), ap(in0), ap(s1), ap(s2), o0, o1))
 
-    def tt(out, in0, in1, o, n, rd, wr, f=1.0):
-        op("V", vc(n, f), rd, wr, lambda: V.tensor_tensor(out, in0, in1, o))
+    def tt(out, in0, in1, o):
+        op("V", vc(out, in0, 1 if psum(in0) or psum(in1) else 2), [in0, in1], [out],
+           lambda: V.tensor_tensor(ap(out), ap(in0), ap(in1), o))
 
-    def cp(out, in_, n, rd, wr, f=1.0):
-        op("V", vc(n, f), rd, wr, lambda: V.tensor_copy(out, in_))
+    def cp(out, in_):
+        op("V", vc(out, in_, 0.5 if narrow(out) and narrow(in_) else 1), [in_], [out], lambda: V.tensor_copy(ap(out), ap(in_)))
 
-    def ms(out, val, n, wr):
-        op("V", vc(n, 0.5), [], wr, lambda: V.memset(out, val))
+    def ms(out, val):
+        op("V", vc(out, out, 0.5 if narrow(out) else 1), [], [out], lambda: V.memset(ap(out), val))
 
-    def act(out, in_, func, n, rd, wr, f=1.0, bias=None, scale=None, acc=None):
+    def act(out, in_, func, bias=None, scale=None):
         kw = {}
         if bias is not None:
             kw["bias"] = bias
         if scale is not None:
             kw["scale"] = scale
-        if acc is not None:
-            kw["accum_out"] = acc
-        op("S", 60 + max(64.0, n * f) * CY, rd, wr, lambda: S.activation(out, in_, func, **kw))
+        op("S", 65 + max(64.0, cols(out) * (GA if in_[5] else 1)) * CY, [in_, bias, scale], [out],
+           lambda: S.activation(ap(out), ap(in_), func, **{k: ap(v) for k, v in kw.items()}))
 
-    def mm(items, rd, wr):
-        c = 40 + sum(max(64, it[5]) * (it[6] if len(it) > 6 else 1) for it in items) * PCY
+    def mm(items):
+        c = 40 + sum(max(64, cols(it[2])) * (1 if narrow(it[2]) else 4) for it in items) * PCY
 
         def fn():
             last = None
             for it in items:
-                last = P.matmul(it[0], it[1], it[2], it[3], it[4])
+                last = P.matmul(ap(it[0]), ap(it[1]), ap(it[2]), it[3], it[4])
             return last
-        op("P", c, rd, wr, fn)
+        op("P", c, [it[1] for it in items] + [it[2] for it in items], [it[0] for it in items], fn)
 
-    def io(out, pat, base, ch, n, wr, flt=True):
+    def acc(out, terms, start=True, stop=True):
+        return [(out, a, b, start and i == 0, stop and i == len(terms) - 1) for i, (a, b) in enumerate(terms)]
+
+    def io(out, pat, base, ch, flt=True):
         if flt:
-            op("G", 130 + 2 * n * CY, [], wr, lambda: g.iota(out, pat, base, ch, allow_small_or_imprecise_dtypes=True))
+            op("G", 130 + 2 * cols(out) * CY, [], [out], lambda: g.iota(ap(out), pat, base, ch, allow_small_or_imprecise_dtypes=True))
         else:
-            op("G", 130 + 2 * n * CY, [], wr, lambda: g.iota(out, pat, base, ch))
+            op("G", 130 + 2 * cols(out) * CY, [], [out], lambda: g.iota(ap(out), pat, base, ch))
 
-    def sel(out, in_, pat, cmp, fill, base, ch, n, rd, wr):
-        op("G", 170 + 2 * n * CY, rd, wr, lambda: g.affine_select(out, in_, pat, cmp, fill, base, ch))
+    def sel(out, in_, pat, cmp, fill, base, ch):
+        op("G", 170 + 2 * cols(out) * CY, [in_], [out], lambda: g.affine_select(ap(out), ap(in_), pat, cmp, fill, base, ch))
 
-    B = [T["B%d" % i] for i in range(8)]
-    pcf = T.pcf
-    pcol, gcol, kcol, g16, k1, k40 = [pcf[:, i:i + 1] for i in range(6)]
+    def B(k, lo=0, hi=512, st=1):
+        return r("B%d" % k, lo, hi, st)
 
-    io(T.pci[:, 0:1], [[0, 1]], 0, 1, 1, ["pci0"], False)
-    io(T.IG[:], [[1, 8], [0, 16]], 0, 0, 128, ["IG"])
-    io(T.I144[:], [[1, 144]], -15, 0, 144, ["I144"])
-    io(T.IJ[:], [[0, 8], [1, 16]], 0, 0, 128, ["IJ"])
-    io(T.IC[:], [[1, 512]], -256, 0, 512, ["IC"])
-    io(T.IL[:], [[16, 32]], 0, 0, 32, ["IL0"])
-    io(T.NAT[:], [[1, 2], [2, 256]], -256, 0, 512, ["NAT"])
-    io(T.STP[:, 0:512], [[0, 512]], 0, 0, 512, ["STP"])
-    io(T.STP[:, 512:1024], [[0, 512]], 1, 0, 512, ["STP1"])
-    io(T.ONf[:], [[0, 128]], 1, 0, 128, ["ONf"])
-    io(T.ONb[:], [[0, 128]], 1, 0, 128, ["ONb"])
-    io(T.NX[:, 512:520], [[0, 8]], 0, 0, 8, ["NXz"])
-    io(T.NX[:, XO + 256:1040], [[0, 264]], 0, 0, 264, ["X1"])
-    io(T.FI[:, 512:528], [[0, 16]], 0, 0, 16, ["FIz"])
-    io(T.LT[:, 512:528], [[0, 16]], 0, 0, 16, ["LTz"])
-    io(T.XL0[:, 8192:XW], [[0, 16]], 0, 0, 16, ["XLt0"])
-    io(T.I128[:], [[1, 128]], 0, 0, 128, ["I128"])
-    io(T.AW0[:, 256:512], [[1, 256]], 0, 0, 256, ["AW0s"])
-    io(T.AW1[:, 0:256], [[1, 256]], -256, 0, 256, ["AW1s"])
-    io(T.AW3[:, 0:256], [[2, 256]], -256, 0, 256, ["AW3s"])
+    def blk(name, i, w=128):
+        return r(name, w * i, w * i + w)
+
+    def DG(j):
+        return blk("DG", j)
+
+    pcol, gcol, kcol, g16, k1, k0, kln = [r("pcf", i, i + 1) for i in range(7)]
+    Ib, In, OBb, ONb = DG(0), r("In"), r("OBb"), r("ONE", 0, 128)
+
+    io(r("pci", 0, 1), [[0, 1]], 0, 1, False)
+    io(r("IG"), [[1, 8], [0, 16]], 0, 0)
+    io(r("I144"), [[1, 144]], -15, 0)
+    io(r("IJ"), [[0, 8], [1, 16]], 0, 0)
+    io(r("PERM"), [[1, 256], [256, 2]], -256, 0)
+    io(r("IC"), [[1, 512]], -256, 0)
+    io(r("IL"), [[16, 32]], 0, 0)
+    io(r("NAT"), [[1, 2], [2, 256]], -256, 0)
+    io(r("NX", 512, 520), [[0, 8]], 0, 0)
+    io(r("NX", XO + 256, 1040), [[0, 264]], 0, 0)
+    io(r("XL0", 8192, XW), [[0, 16]], 0, 0)
+    io(r("I256"), [[1, 256]], 0, 0)
+    io(r("AW0", 256, 512), [[1, 256]], 0, 0)
+    io(r("AW1", 0, 256), [[1, 256]], -256, 0)
+    io(r("AW3", 0, 256), [[2, 256]], -256, 0)
+    ms(r("ONE"), 1.0)
+    ms(r("NEG"), -1.0)
+    ms(r("RT"), RND)
     for q in range(4):
-        sel(T.EX[:, 512 * q:512 * q + 512], T.STP[:, 512:1024], [[-1, 32], [0, 16]], A.is_equal, 0.0, -32 * q, 1, 512,
-            ["STP1"], ["EX%d" % q])
-    ts(T.pci[:, 1:2], T.pci[:, 0:1], 4, None, A.arith_shift_right, None, 1, ["pci0"], ["pci1"])
-    ts(T.pci[:, 2:3], T.pci[:, 0:1], 15, None, A.bitwise_and, None, 1, ["pci0"], ["pci2"])
-    cp(pcf[:, 0:3], T.pci[:, 0:3], 3, ["pci0", "pci1", "pci2"], ["pc"])
-    ts(g16, gcol, 16.0, None, A.mult, None, 1, ["pc"], ["g16"])
-    ts(k1, kcol, -1.0, 1.0, A.mult, A.add, 1, ["pc"], ["k1"])
-    ts(k40, kcol, -1.0, -40.0, A.mult, A.add, 1, ["pc"], ["k40"])
-    I128f = T.I144[:, 15:143]
-    ts(T.OBf[:], T.IG[:], gcol, None, A.is_equal, None, 128, ["IG", "pc"], ["OBf"])
-    ts(T.OBb[:], T.IG[:], gcol, None, A.is_equal, None, 128, ["IG", "pc"], ["OBb"])
-    ts(T.EQ[:], T.IJ[:, 0:16], kcol, None, A.is_equal, None, 16, ["IJ", "pc"], ["EQ"])
-    ts(T.Ih[:], I128f, pcol, None, A.is_equal, None, 128, ["I144", "pc"], ["Ih"])
-    ts(T.Ib[:], I128f, pcol, None, A.is_equal, None, 128, ["I144", "pc"], ["Ib"])
+        sel(blk("EX", q, 512), r("ONE"), [[-1, 32], [0, 16]], A.is_equal, 0.0, -32 * q, 1)
+    ts(r("pci", 1, 2), r("pci", 0, 1), 4, None, A.arith_shift_right)
+    ts(r("pci", 2, 3), r("pci", 0, 1), 15, None, A.bitwise_and)
+    cp(r("pcf", 0, 3), r("pci", 0, 3))
+    act(g16, gcol, F.Copy, scale=16.0)
+    act(k1, kcol, F.Identity, scale=-1.0, bias=1.0)
+    act(k0, k1, F.Relu)
+    act(kln, kcol, F.Copy, scale=LN2)
+    I128f = r("I144", 15, 143)
+    ts(OBb, r("IG"), gcol, None, A.is_equal)
+    ts(r("EQ"), r("IJ", 0, 16), kcol, None, A.is_equal)
+    ts(Ib, I128f, pcol, None, A.is_equal)
     for j in range(16):
-        ts(T.BT[:, 128 * j:128 * j + 128], T.OBb[:], T.EQ[:, j:j + 1], None, A.mult, None, 128, ["OBb", "EQ"], ["BT%d" % j], 0.5)
-    for nm, v in (("In", -1.0), ("Ihalf", -0.5), ("D1", -25.5 * K * K), ("D3", -20.0 * K)):
-        act(T[nm][:], T.Ib[:], F.Copy, 128, ["Ib"], [nm], scale=v)
-    act(T.OBm[:], T.OBb[:], F.Copy, 128, ["OBb"], ["OBm"], scale=-1.0)
-    ts(T.L1[:], T.BT[:, 0:128], 2080.0, None, A.mult, None, 128, ["BT0"], ["L1"], 0.5)
-    ts(T.L2[:], T.Ih[:], 3232.0, None, A.mult, None, 128, ["Ih"], ["L2"], 0.5)
-    ts(T.BM[:], T.I144[:], g16, K, A.is_equal, A.mult, 144, ["I144", "g16"], ["BM"])
-    ts(pcf[:, 6:7], kcol, 0.0, None, A.is_equal, None, 1, ["pc"], ["k0"])
-    ts(T.B0h[:], T.I144[:], pcol, pcf[:, 6:7], A.is_equal, A.mult, 144, ["I144", "pc", "k0"], ["B0h"])
-    ts(T.B0b[:], T.I144[:], pcol, pcf[:, 6:7], A.is_equal, A.mult, 144, ["I144", "pc", "k0"], ["B0b"])
-    sel(T.c1[:], T.OBb[:], [[1, 128]], A.is_gt, 0.0, 0, -1, 128, ["OBb"], ["c1"])
-    sel(T.FST[:], T.c1[:], [[1, 128]], A.not_equal, -16.0, 0, -1, 128, ["c1"], ["FST"])
-    act(T.c1[:], T.c1[:], F.Identity, 128, ["c1"], ["c1"], bias=1.0 / 32, scale=47.0 / 32)
-    sel(T.c1[:], T.c1[:], [[1, 128]], A.not_equal, -1.0, 0, -1, 128, ["c1"], ["c1"])
-    act(T.PK[:], T.IJ[:], F.Exp, 128, ["IJ"], ["PK"], scale=-LN2, bias=-LN2)
+        ts(blk("BT", j), OBb, r("EQ", j, j + 1), None, A.mult)
+    for j in range(1, 17):
+        act(DG(j), Ib, F.Copy, scale=2.0 ** j)
+    for nm, v in (("In", -1.0), ("N35", -35.0), ("D10", 10.0), ("N256", -256.0), ("N60", -2.0 ** 60), ("Ifn", -1.0)):
+        act(r(nm), Ib, F.Copy, scale=v)
+    for nm, v in (("OBf", 1.0), ("O2k", 2048.0), ("O6k", 6144.0), ("O8k", 8192.0), ("MJ", 12.0)):
+        act(r(nm), OBb, F.Copy, scale=v)
+    sel(r("MJ"), r("MJ"), [[1, 128]], A.not_equal, 76.0, 0, -1)
+    cp(r("OBh"), OBb)
+    ts(r("Ihn"), Ib, -1.0, None, A.mult)
+    ts(r("L1"), blk("BT", 0), 2080.0, None, A.mult)
+    ts(r("L2"), Ib, 3232.0, None, A.mult)
+    ts(r("BM"), r("I144"), g16, None, A.is_equal)
+    ts(r("B0b"), r("I144"), pcol, k0, A.is_equal, A.mult)
+    cp(r("B0h"), r("B0b"))
+    sel(r("c1"), OBb, [[1, 128]], A.is_gt, 0.0, 0, -1)
+    sel(r("FST"), r("c1"), [[1, 128]], A.not_equal, -16.0, 0, -1)
+    act(r("c1"), r("c1"), F.Identity, bias=1.0 / 32, scale=47.0 / 32)
+    sel(r("c1"), r("c1"), [[1, 128]], A.not_equal, -1.0, 0, -1)
+    act(r("PK"), r("IJ"), F.Exp, scale=-LN2, bias=-LN2)
     ops[-1]["c"] += 1300
+    act(r("WF", 512, 528), r("IJ", 0, 16), F.Exp, scale=0.0, bias=kln)
     for nm, src in (("TRI", "c1"), ("PK", "PK")):
-        sel(T[nm][:], T[src][:], [[-16, 8], [0, 16]], A.is_ge, 0.0, 0, 1, 128, [src], [nm])
-        sel(T[nm][:], T[nm][:], [[16, 8], [0, 16]], A.is_ge, 0.0, 15, -1, 128, [nm], [nm])
-    act(T.PK32[:], T.PK[:], F.Copy, 128, ["PK"], ["PK32"], scale=1.0 / 32)
-    cA, cB, cC, cD = [T.CST[:, 256 * i:256 * i + 256] for i in range(4)]
-    ms(cA, -4.5 * K / 16, 256, ["cA"])
-    ms(cB, 1.0 / 32, 256, ["cB"])
-    ms(cC, 2.5 / 16, 256, ["cC"])
-    cE = T.fl[:, 512:768]
-    io(cE, [[0, 256]], 4096, 0, 256, ["cE"])
-    ts(T.IL[:], T.IL[:], kcol, None, A.add, None, 32, ["IL0", "pc"], ["IL0", "IL"])
-    ts(T.S8[0:8, :], T.IG[0:8, :], pcf[0:8, 0:1], None, A.is_equal, None, 128, ["IG", "pc"], ["S8"])
-    cp(T.thb[0:8, 0:2], T.ths[0:8, 0:2], 2, ["xth"], ["thb"])
-    mm([(B[7][:, 0:2], T.S8[0:8, :], T.thb[0:8, 0:2], True, True, 2)], ["S8", "thb"], ["B7"])
-    cp(T.XL0[:, 8192:8194], B[7][:, 0:2], 2, ["B7", "XLt0"], ["XLt0"])
+        sel(r(nm), r(src), [[-16, 8], [0, 16]], A.is_ge, 0.0, 0, 1)
+        sel(r(nm), r(nm), [[16, 8], [0, 16]], A.is_ge, 0.0, 15, -1)
+    act(r("PK32"), r("PK"), F.Copy, scale=1.0 / 32)
+    act(r("PKn"), r("PK"), F.Copy, scale=-1.0)
+    ts(r("PW2"), OBb, r("WF", 512, 513), None, A.mult)
+    act(r("IL"), r("IL"), F.Identity, bias=kcol)
+    ts(r("S8", p=(0, 8)), r("IG", p=(0, 8)), r("pcf", 0, 1, p=(0, 8)), None, A.is_equal)
+    cp(r("thb", 0, 2, p=(0, 8)), r("ths", 0, 2, p=(0, 8)))
+    mm([(B(7, 0, 2), r("S8", p=(0, 8)), r("thb", 0, 2, p=(0, 8)), True, True)])
+    act(r("XL0", 8192, 8194), B(7, 0, 2), F.Copy)
 
-    NW = ["N0", "N1", "NXz"]
+    made = [x for o in ops if o["e"] == "G" for x in o["w"]]
+    for t in range(1, 4):
+        op("D", SEND, made + [r("XL%d" % (t - 1), 4096, XW)], [r("XL%d" % t)], None)
+
+    NW = r("NX", 0, 512)
+    PUn = r("PU", 128, 160)
+    cp(PUn, r("pts"))
+    ts(r("QN"), ind(r("cqs"), PUn), -2048.0, None, A.add)
     for h in range(2):
-        ts(T.NX[:, 256 * h:256 * h + 256], T.cqs[:, h::2], -1.0, 4095.0, A.mult, A.add, 256, ["xcq"], ["N%d" % h])
-    ts(T.ti[:, 0:32], T.pts[:], 1, None, A.arith_shift_right, None, 32, ["xpt"], ["ti0"])
-    ts(T.ti[:, 32:64], T.pts[:], 1, None, A.bitwise_and, None, 32, ["xpt"], ["ti1"])
-    ts(T.tl[:, 0:32], T.ti[:, 32:64], 256.0, None, A.mult, None, 32, ["ti1"], ["tl0"])
-    tt(T.tl[:, 0:32], T.tl[:, 0:32], T.ti[:, 0:32], A.add, 32, ["tl0", "ti0"], ["tl0"])
-    PUn = T.PU[:, 128:160]
-    cp(PUn, T.tl[:, 0:32], 32, ["tl0"], ["PUn"])
-    ts(T.QN[:], T.NX[:, 0:512].indirect(PUn), -1.0, 2047.0, A.mult, A.add, 512, NW + ["PUn"], ["QN"], GA)
-    act(T.b5[:], T.NX[:, 0:512], F.Sign, 512, ["N0", "N1"], ["b5"])
-    act(B[4][:], T.NX[:, 0:512], F.Identity, 512, ["N0", "N1"], ["B4"], bias=-2048.0)
-    tt(T.NC[:], B[4][:], T.b5[:], A.add, 512, ["B4", "b5"], ["NC"])
-    ts(T.CE[:, 0:256], T.NC[:, 0:256], -1.0, None, A.mult, None, 256, ["NC"], ["CE0"], 0.5)
-    ts(T.CE[:, 256:768], T.NC[:], -1.0, None, A.mult, None, 512, ["NC"], ["CE1"], 0.5)
-    if NS1 < 8:
-        ts(T.CE[:, 768:1024], T.NC[:, 256:512], -1.0, None, A.mult, None, 256, ["NC"], ["CE2"], 0.5)
-    act(T.PN[:], T.IC[:].indirect(PUn), F.Copy, 512, ["IC", "PUn"], ["PN"], GA)
+        ts(blk("CE", 2 * h, 256), r("cqs", h, 512, 2), -2048.0, None, A.add)
+        cp(blk("CE", 2 * h + 1, 256), blk("CE", 2 * h, 256))
+        ts(blk("NX", h, 256), blk("CE", 2 * h, 256), -1.0, 2047.0, A.mult, A.add)
+        act(blk("ne", h, 256), blk("NX", h, 256), F.Sign)
+    act(r("PN"), ind(r("PERM"), PUn), F.Copy)
     for h in range(2):
-        act(T.PR0[:, 256 * h:256 * h + 256], T.PN[:, h::2], F.Copy, 256, ["PN"], ["PR0"])
+        act(blk("PR0", h, 256), r("PN", h, 512, 2), F.Copy)
 
     def lists(t):
-        PR = T["PR%d" % t]
         bk = 3 if t else 6
-        bn = "B%d" % bk
-        mm([(B[bk][:, 0:32], T.B0b[:, 15 - w:143 - w], PR[:, w::16], w == 0, w == 15, 32) for w in range(16)],
-           ["B0b", "PR%d" % t], [bn])
-        ts(T.PF[:, 32 * t:32 * t + 32], B[bk][:, 0:32], 256.0, None, A.add, None, 32, [bn], ["PF%d" % t])
-        ts(T.PU[:, 32 * t:32 * t + 32], B[bk][:, 0:32], 256.0, None, A.add, None, 32, [bn], ["PU%d" % t])
-
-    def columns(tt_):
-        par, m = tt_[0] & 1, 32 * len(tt_)
-        mm([(B[7][:, 32 * i + 8 * k:32 * i + 8 * k + 8], T["PR%d" % t][:, 128 * k:128 * k + 128], T.B0b[:, 15:143:16], True, True, 8)
-            for i, t in enumerate(tt_) for k in range(4)], ["B0b"] + ["PR%d" % t for t in tt_], ["B7"])
-        a = 32 * PWC[tt_[0]]
-        ts(T.ti[:, 0:m], B[7][:, 0:m], 512.0 if par else 256.0, None, A.add, None, m, ["B7"], ["ti0", "ti1"])
-        ts(T.ti[:, 64:64 + m], T.ti[:, 0:m], 128, None, A.bitwise_and, None, m, ["ti0", "ti1"], ["ti2"])
-        ts(T.ti[:, 0:m], T.ti[:, 0:m], 383, None, A.bitwise_and, None, m, ["ti0", "ti1"], ["ti0", "ti1"])
-        cp(T.PW[:, a:a + m], T.ti[:, 0:m], m, ["ti0", "ti1"], ["PWa%d" % t for t in tt_])
-        ts(T.PW[:, 128 + a:128 + a + m], T.ti[:, 64:64 + m], 1023.0 / 128, 1.0, A.mult, A.add, m, ["ti2"], ["PWb%d" % t for t in tt_])
+        mm([(B(bk, 0, 32), r("B0b", 15 - w, 143 - w), r("PR%d" % t, w, 512, 16), w == 0, w == 15) for w in range(16)])
+        act(blk("PF", t, 32), B(bk, 0, 32), F.Identity, bias=256.0)
+        cp(blk("PU", t, 32), blk("PF", t, 32))
 
     def compare(h):
-        c = slice(256 * h, 256 * h + 256)
         sb = 3 + 2 * h
         for n in range(8):
             bk, eb = (n % 2, n % 2) if h == 0 else (2 + 2 * (n % 2), 2 + n % 2)
-            its = []
-            sgn = h and (n * NS1) // 8 != ((n + 1) * NS1) // 8
-            for i in range(2):
-                o, j = B[bk][:, 256 * i:256 * i + 256], 2 * n + i
-                if sgn:
-                    its.append((o, T.Ih[:], T.NC[:, c], True, False, 256))
-                its.append((o, T.BT[:, 128 * j:128 * j + 128], T.QN[:, h::2], not sgn, True, 256))
-            mm(its, ["Ih", "NC", "QN", "BT%d" % (2 * n), "BT%d" % (2 * n + 1)], ["B%d" % bk])
-            e = T.E[:, 512 * eb:512 * eb + 512]
-            if sgn:
-                act(e, B[bk][:], F.Sign, 512, ["B%d" % bk], ["E%d" % eb])
-            else:
-                tt(e, B[bk][:], T.CE[:, 512 * h:512 * h + 512], A.is_equal, 512, ["B%d" % bk, "CE1", "CE%d" % (2 * h)], ["E%d" % eb])
-            mm([(B[sb][:, 0:256], T.Ib[:], T.E[:, 512 * eb + 256 * i:512 * eb + 256 * i + 256], n + i == 0, n + i == 8, 256)
-                for i in range(2)], ["Ib", "E%d" % eb], ["B%d" % sb])
-        if h and NS1:
-            cp(T.i5[:], B[sb][:, 0:256], 256, ["B5"], ["i5"])
-            ts(T.i5[:], T.i5[:], 1, None, A.bitwise_and, None, 256, ["i5"], ["i5"])
-            tt(T.t5[:, c], T.b5[:, c], T.i5[:], A.is_gt, 256, ["b5", "i5"], ["t51"], 2)
-        else:
-            tt(T.t5[:, c], B[sb][:, 0:256], T.b5[:, c], A.is_lt, 256, ["B%d" % sb, "b5"], ["t5%d" % h])
+            mm([(B(bk, 256 * i, 256 * i + 256), blk("BT", 2 * n + i), r("QN", h, 512, 2), True, True) for i in range(2)])
+            tt(blk("E", eb, 512), B(bk), blk("CE", h, 512), A.is_equal)
+            mm([(B(sb, 0, 256), DG(2 * n + i), blk("E", 2 * eb + i, 256), n + i == 0, n + i == 8) for i in range(2)])
+        tt(blk("t5", h, 256), B(sb, 0, 256), blk("ne", h, 256), A.is_lt)
+        tt(blk("WF", h, 256), B(sb, 0, 256), blk("ne", h, 256), A.mult)
 
     def tops(h):
-        c = slice(256 * h, 256 * h + 256)
-        tp = "t5%d" % h
-        mm([(B[6][:, 0:16], T.BM[:, 15 - w:143 - w], T.t5[:, 256 * h + w:256 * h + 256:16], w == 0, w == 15, 16) for w in range(16)],
-           ["BM", tp], ["B6"])
-        s = slice(16 * h, 16 * h + 16)
-        ts(T.HL[:, s], B[6][:, 0:16], 0.0, None, A.is_gt, None, 16, ["B6"], ["HL%d" % h])
-        ts(T.HX[:, s], T.IL[:, s], float(XO), None, A.add, None, 16, ["IL"], ["HX%d" % h])
-        tt(T.HX[:, s], T.HX[:, s], T.HL[:, s], A.mult, 16, ["HX%d" % h, "HL%d" % h], ["HX%d" % h])
-        mm([(B[7][:, 0:256], T.FST[:], T.t5[:, c], True, True, 256)], ["FST", tp], ["B7"])
-        act(B[7][:, 0:256], B[7][:, 0:256], F.Relu, 256, ["B7"], ["B7"], bias=-15.0, scale=-1.0)
-        tt(T.f5[:, c], B[7][:, 0:256], T.NX[:, c], A.mult, 256, ["B7", "N%d" % h], ["f5%d" % h])
-        mm([(B[7][:, 0:256], T.OBf[:], T.f5[:, c], True, True, 256, 4)], ["OBf", "f5%d" % h], ["B7"])
-        act(T.NX[:, XO + 256 * h:XO + 256 * h + 256], B[7][:, 0:256], F.Copy, 256, ["B7"], ["X%d" % h])
+        mm([(B(6, 0, 16), r("BM", 15 - w, 143 - w), r("t5", 256 * h + w, 256 * h + 256, 16), w == 0, w == 15) for w in range(16)])
+        act(blk("HL", h, 16), B(6, 0, 16), F.Sign)
+        act(blk("HL", 2 + h, 16), B(6, 0, 16), F.Sign, bias=-0.5)
+        act(blk("HX", h, 16), blk("IL", h, 16), F.Identity, bias=float(XO))
+        tt(blk("HX", h, 16), blk("HX", h, 16), blk("HL", h, 16), A.mult)
+        o = B(7, 0, 256)
+        mm([(o, r("FST"), blk("t5", h, 256), True, True)])
+        act(o, o, F.Relu, bias=-15.0, scale=-1.0)
+        tt(blk("f5", h, 256), o, blk("NX", h, 256), A.mult)
+        mm([(o, r("OBf"), blk("f5", h, 256), True, True)])
+        act(r("NX", XO + 256 * h, XO + 256 * h + 256), o, F.Copy)
 
     def chain(t):
         par = t & 1
-        s = slice(16 * par, 16 * par + 16)
-        PF, ab = T.PF[:, 32 * t + 16 * par:32 * t + 16 * par + 16], T.AB[:, 16 * t:16 * t + 16]
-        hl, il = T.HL[:, s], T.IL[:, s]
-        x0, x1 = T.tl[:, 32:48], T.tl[:, 48:64]
-        ly, lf, ln, lw = [T.tl[:, 64 + 16 * i:80 + 16 * i] for i in range(4)]
-        pf, lu, hn = "PF%d" % t, "LU%d" % t, "HL%d" % par
-        tt(ly, PF, T.HX[:, s], A.max, 16, [pf, "HX%d" % par], ["ly"])
-        cp(T.LU[:, 64 * t:64 * t + 16], ly, 16, ["ly"], [lu + "y"])
-        ts(x0, PF, 256.0, None, A.is_lt if par else A.is_ge, None, 16, [pf], ["x0"])
-        tt(ab, x0, hl, A.is_gt, 16, ["x0", hn], ["AB%d" % t])
-        tt(x1, PF, il, A.subtract, 16, [pf, "IL"], ["x1"])
-        tt(x1, x1, ab, A.mult, 16, ["x1", "AB%d" % t], ["x1"])
-        tt(ln, x1, il, A.add, 16, ["x1", "IL"], ["ln"])
-        cp(T.LU[:, 64 * t + 32:64 * t + 48], ln, 16, ["ln"], [lu + "N"])
-        act(x1, ab, F.Copy, 16, ["AB%d" % t], ["x1"], scale=512.0)
-        tt(lw, x1, ln, A.add, 16, ["x1", "ln"], ["lw"])
-        tt(x0, x0, hl, A.mult, 16, ["x0", hn], ["x0"])
-        act(x0, x0, F.Identity, 16, ["x0"], ["x0"], scale=-512.0, bias=512.0)
-        tt(lf, x0, PF, A.max, 16, ["x0", pf], ["lf"])
-        cp(T.LU[:, 64 * t + 16:64 * t + 32], lf, 16, ["lf"], [lu + "F"])
-        cp(T.LU[:, 64 * t + 48:64 * t + 64], lw, 16, ["lw"], [lu + "W"])
+        PF, il = blk("PF", 2 * t + par, 16), blk("IL", par, 16)
+        x0, x1, ly, ab = [blk("tl", i, 16) for i in range(4)]
+        cl = blk("CL", t, 16)
+        tt(ly, PF, blk("HX", par, 16), A.max)
+        cp(blk("LU", 2 * t, 16), ly)
+        ts(x0, PF, 256.0, None, A.is_lt if par else A.is_ge)
+        tt(cl, x0, blk("HL", 2 + par, 16), A.mult)
+        ts(ab, cl, 0.0, None, A.is_lt)
+        tt(x1, PF, il, A.subtract)
+        tt(x1, x1, ab, A.mult)
+        tt(x1, x1, il, A.add)
+        cp(blk("LU", 2 * t + 1, 16), x1)
         aw = "AW3" if t == 3 else "AW%d" % par
-        src = "NAT" if t == 3 else "IC"
-        h = slice(256 * par, 256 * par + 256)
-        act(T[aw][:, h], T[src][:].indirect(T.LU[:, 64 * t + 32:64 * t + 48]), F.Copy, 256, [src, lu + "N"], [aw], GA)
-        nx = "PN" if t == 3 else "PR%d" % (t + 1)
-        act(T[nx][:], T[aw][:].indirect(T.PU[:, 32 * t:32 * t + 32]), F.Copy, 512, [aw, aw + "s", "PU%d" % t], [nx], GA)
+        act(blk(aw, par, 256), ind(r("NAT" if t == 3 else "IC"), blk("LU", 2 * t + 1, 16)), F.Copy)
+        act(r("PN" if t == 3 else "PR%d" % (t + 1)), ind(r(aw), blk("PU", t, 32)), F.Copy)
+
+    def code(t, bk):
+        mm([(B(bk, w, 256, 16), blk("BT", w), blk("CL", t, 16), True, True) for w in range(16)])
+        act(blk("CD", t, 256), B(bk, 0, 256), F.Copy)
 
     def parents_out():
-        mm([(B[6][:, 0:32], T.B0b[:, 15 - w:143 - w], T.PN[:, 256 * (w & 1) + (w >> 1):256 * (w & 1) + 256:8],
-             w == 0, w == 15, 32) for w in range(16)], ["B0b", "PN"], ["B6"])
-        act(T.OP[:], B[6][:, 0:32], F.Identity, 32, ["B6"], ["OP"], bias=256.0)
+        mm([(B(7, 0, 32), r("B0b", 15 - w, 143 - w), r("PN", 256 * (w & 1) + (w >> 1), 256 * (w & 1) + 256, 8), w == 0, w == 15)
+            for w in range(16)])
+        act(r("OP"), B(7, 0, 32), F.Identity, bias=256.0)
+
+    def hop(t):
+        lo = 16 * t
+        a, b = r("PF", 32 * t + lo, 32 * t + 32), r("PF", 32 * t + 32 + lo, 32 * t + 64)
+        x, u = r("tl", 64 + lo, 96), r("LU", 128 + 32 * t, 160 + 16 * t)
+        tt(x, a, b, A.is_equal)
+        act(x, x, F.Copy, scale=512.0)
+        tt(x, x, a, A.max)
+        cp(u, x)
+        act(r("TH", 512 * t, 512 + 256 * t), ind(r("WF"), u), F.Copy)
+
+    def bit(o, src):
+        n = cols(o)
+        return acc(o, [(r("PK32"), r("ONE", 0, n)), (r("PK"), src), (Ib, r("RT", 0, n)), (In, r("RT", 0, n)), (r("PKn"), src)])
 
     def frames():
-        ts(T.QN[:], T.NX[:, 0:512].indirect(T.PU[:, 96:128]), -1.0, 2047.0, A.mult, A.add, 512, NW + ["PU3"], ["QN"], GA)
-        for n in range(16):
-            bk = 4 + n % 3
-            bn = "B%d" % bk
-            e = T.E[:, 512 * (n % 4):512 * (n % 4) + 512]
-            bt = T.BT[:, 128 * n:128 * n + 128]
-            if (n * NS2) // 16 != ((n + 1) * NS2) // 16:
-                mm([(B[bk][:], T.Ih[:], T.NC[:], True, False, 512), (B[bk][:], bt, T.QN[:], False, True, 512)],
-                   ["Ih", "NC", "QN", "BT%d" % n], [bn])
-                act(B[bk][:], B[bk][:], F.Abs, 512, [bn], [bn])
-                act(e, B[bk][:], F.Relu, 512, [bn], ["E%d" % (n % 4)], bias=float(n + 40), scale=-float(n + 40))
-                dg, dn = T.Ib[:], "Ib"
-            else:
-                mm([(B[bk][:], bt, T.QN[:], True, True, 512)], ["QN", "BT%d" % n], [bn])
-                tt(e, B[bk][:], T.CE[:, 256:768], A.is_equal, 512, [bn, "CE1"], ["E%d" % (n % 4)])
-                dg, dn = T.DG[:, 128 * n:128 * n + 128], "DG%d" % n
-                act(dg, T.Ib[:], F.Copy, 128, ["Ib"], [dn], scale=float(n + 40))
-            mm([(B[7][:], dg, e, n == 0, n == 15, 512)], [dn, "E%d" % (n % 4)], ["B7"])
-        act(T.WF[:, 0:512], B[7][:], F.Exp, 512, ["B7"], ["WA0", "WA1"], scale=LN2, bias=-40.0 * LN2)
-        act(T.LT[:, 0:512], B[7][:], F.Identity, 512, ["B7", "k40"], ["LT"], bias=k40)
-        tt(T.tl[:, 128:144], T.AB[:, 0:16], T.AB[:, 32:48], A.max, 16, ["AB0", "AB2"], ["x3"])
-        cp(T.tl[:, 144:160], T.AB[:, 16:32], 16, ["AB1"], ["x4"])
-        ts(T.tl[:, 0:32], T.IL[:], -512.0, None, A.add, None, 32, ["IL"], ["tl0"])
-        tt(T.tl[:, 0:32], T.tl[:, 0:32], T.tl[:, 128:160], A.mult, 32, ["tl0", "x3", "x4"], ["tl0"])
-        ts(T.LU[:, 256:288], T.tl[:, 0:32], 512.0, None, A.add, None, 32, ["tl0"], ["La"])
-        f5 = ["f50", "f51"]
-        act(T.f5[:], T.LT[:].indirect(T.LU[:, 256:288]), F.Identity, 512, ["LT", "LTz", "La", "pc"], f5, GA, bias=kcol)
-        act(T.WF[:, 512:1024], T.f5[:], F.Exp, 512, f5, ["FW"], scale=LN2)
-        act(T.f5[:], T.f5[:], F.Abs, 512, f5, f5)
-        act(T.FI[:, 0:512], T.f5[:], F.Exp, 512, f5, ["FI"], scale=-LN2)
+        for h in range(2):
+            o = B(4 + h, 0, 256)
+            mm(bit(o, blk("WF", h, 256)))
+            ts(o, o, 0.0, None, A.is_gt)
+            tt(blk("cw", h, 256), o, blk("TH", h, 256), A.mult)
+            its = []
+            for k in range(2):
+                c, rt = blk("cw", 2 * h + k), r("RT", 0, 128)
+                its += acc(B(4 + h, 256 + 128 * k, 384 + 128 * k), [(ONb, r("PK32")), (c, r("PK")), (Ib, rt), (In, rt), (c, r("PKn"))])
+            mm(its)
+            ts(blk("MT", h, 256), B(4 + h, 256, 512), 0.0, None, A.is_gt)
 
-    def onehot(t):
-        a, ns = 32 * PWC[t], NOH[t]
-        if ns:
-            act(T.oc[:, 0:32], T.PW[:, a:a + 32], F.Copy, 32, ["PWa%d" % t], ["oc0"], scale=-1.0)
-            act(T.oc[:, 32:64], T.PW[:, 128 + a:160 + a], F.Copy, 32, ["PWb%d" % t], ["oc1"], scale=-1.0)
+    def onehot():
+        mm([(B(7, 8 * k, 8 * k + 8), blk("PR1", k), r("B0b", 15, 143, 16), True, True) for k in range(4)])
+        a, b, c, d = [blk("ti", i, 32) for i in range(4)]
+        ts(a, B(7, 0, 32), 256.0, None, A.add)
+        ts(b, a, 128, None, A.bitwise_and)
+        ts(c, a, 1, 128, A.arith_shift_right, A.bitwise_and)
+        ts(d, a, 127, None, A.bitwise_and)
+        tt(blk("PW", 0, 32), c, d, A.add)
+        ts(blk("PW", 1, 32), b, 1023.0 / 128, 1.0, A.mult, A.add)
         for q in range(8):
             for k in range(4):
                 i = 8 * k + q
-                if 4 * q + k < ns:
-                    x = T.ox[:, 128 * (k & 1):128 * (k & 1) + 128]
-                    act(x, T.I128[:], F.Abs, 128, ["I128", "oc0"], ["ox%d" % (k & 1)], bias=T.oc[:, i:i + 1])
-                    act(T.OH[:, 128 * i:128 * i + 128], x, F.Relu, 128, ["ox%d" % (k & 1), "oc1", "PWb%d" % t], ["OH%d" % i],
-                        scale=T.oc[:, 32 + i:33 + i], bias=T.PW[:, 128 + a + i:129 + a + i])
-                    continue
-                ts(T.OH[:, 128 * i:128 * i + 128], T.I128[:], T.PW[:, 32 * PWC[t] + i:32 * PWC[t] + i + 1],
-                   T.PW[:, 128 + 32 * PWC[t] + i:129 + 32 * PWC[t] + i], A.is_equal, A.mult,
-                   128, ["I128", "PWa%d" % t, "PWb%d" % t], ["OH%d" % i], 0.5)
+                ts(blk("OH", i, 256), r("I256"), r("PW", i, i + 1), r("PW", 32 + i, 33 + i), A.is_equal, A.mult)
 
     def head(t):
-        XL = T["XL%d" % t]
-        lu, xs, pu = "LU%d" % t, "xxs%d" % t, "PU%d" % t
+        XL = "XL%d" % t
         p0 = 32 * t + 16 * (t & 1)
         for h in range(2):
-            ts(T.QU[:, 128 * h:128 * h + 128], T.NX[:, 0:512].indirect(T.PU[:, p0 + 8 * h:p0 + 8 * h + 8]), -1.0, 4095.0,
-               A.mult, A.add, 128, NW + [pu], ["QU%d" % h], GA)
-        ts(T.YH[:], T.NX[:].indirect(T.LU[:, 64 * t:64 * t + 16]), -1.0, 2047.0, A.mult, A.add, 256,
-           NW + ["X0", "X1", lu + "y"], ["YH"], GA)
-        mm([(B[6][:, 0:16], T.B0h[:, 15 - w:143 - w], T.YH[:, w::16], w == 0, w == 15, 16) for w in range(16)],
-           ["B0h", "YH"], ["B6"])
-        ts(T.YU[:], B[6][:, 0:16], 2048.0, None, A.add, None, 16, ["B6"], ["YU"])
-        ts(T.QH[:], T.QU[:], -2048.0, None, A.add, None, 256, ["QU0", "QU1"], ["QH"], 0.5)
-        mm([(B[5][:, 0:256], T.BT[:, 0:128], T.YH[:], True, True, 256),
-            (B[5][:, 256:512], T.L1[:], T.YH[:], True, False, 256),
-            (B[5][:, 256:512], T.L2[:], T.QH[:], False, True, 256)], ["BT0", "L1", "L2", "YH", "QH"], ["B5"])
-        tt(T.hm[:], B[5][:, 0:256], T.QH[:], A.mult, 256, ["B5", "QH"], ["hm"])
-        tt(T.hi[:], B[5][:, 256:512], T.hm[:], A.add, 256, ["B5", "hm"], ["hi"])
-        ts(T.hi[:], T.hi[:], 5, 4095, A.arith_shift_right, A.bitwise_and, 256, ["hi"], ["hi"])
-        cp(T.HU[:], T.hi[:], 256, ["hi"], ["HU"])
-        act(T.XY[:], XL[:, 0:4096].indirect(T.YU[:, 0:16]), F.Copy, 256, [xs, "YU"], ["XY"], GA)
-        mm([(B[6][:, 128 * h:128 * h + 128], T.XY[:, 128 * h:128 * h + 128], T.In[:], True, True, 128) for h in range(2)],
-           ["XY", "In"], ["B6"])
-        act(T.XT[:], B[6][:, 0:256], F.Copy, 256, ["B6"], ["XT"])
+            ts(blk("QU", h), ind(NW, r("PU", p0 + 8 * h, p0 + 8 * h + 8)), -1.0, 4095.0, A.mult, A.add)
+        ts(r("YH"), ind(r("NX"), blk("LU", 2 * t, 16)), -1.0, 2047.0, A.mult, A.add)
+        mm([(B(6, 0, 16), r("B0h", 15 - w, 143 - w), r("YH", w, 256, 16), w == 0, w == 15) for w in range(16)])
+        ts(r("YU"), B(6, 0, 16), 2048.0, None, A.add)
+        ts(r("QH"), r("QU"), -2048.0, None, A.add)
+        mm([(B(5, 0, 256), blk("BT", 0), r("YH"), True, True)] + acc(B(5, 256, 512), [(r("L1"), r("YH")), (r("L2"), r("QH"))]))
+        tt(r("hm"), B(5, 0, 256), r("QH"), A.mult)
+        tt(r("hi"), B(5, 256, 512), r("hm"), A.add)
+        ts(r("hi"), r("hi"), 5, 4095, A.arith_shift_right, A.bitwise_and)
+        cp(r("HU"), r("hi"))
+        act(r("XY"), ind(r(XL, 0, 4096), r("YU")), F.Copy)
+        mm([(B(6, 128 * h, 128 * h + 128), blk("XY", h), In, True, True) for h in range(2)])
+        act(r("XT"), B(6, 0, 256), F.Copy)
 
-    def scores(t):
-        XL = T["XL%d" % t]
-        xs, lm = "xxs%d" % t, "xlim%d" % t
-        for n in range(8):
-            c = slice(512 * n, 512 * n + 512)
-            act(T.XQ[:, c], XL[:, 0:4096].indirect(T.QU[:, 32 * n:32 * n + 32]), F.Copy, 512, [xs, "QU%d" % (n // 4)], ["XQ%d" % n], GA)
-            bk = n % 2 if len(CUTS) > 1 else n % 3
-            mm([(B[bk][:], T.Ib[:], T.XQ[:, c], True, False, 512),
-                (B[bk][:], T.XT[:, 128 * (n // 4):128 * (n // 4) + 128], T.EX[:, 512 * (n % 4):512 * (n % 4) + 512], False, True, 512)],
-               ["Ib", "XQ%d" % n, "XT", "EX%d" % (n % 4)], ["B%d" % bk])
-            ad = T.AD[:, 512 * (n % 4):512 * (n % 4) + 512]
-            act(ad, B[bk][:], F.Abs, 512, ["B%d" % bk], ["AD%d" % (n % 4)])
-            tt(T.CM[:, c], XL[:, 4096:8192].indirect(T.HU[:, 32 * n:32 * n + 32]), ad, A.is_ge, 512,
-               [lm, "HU", "AD%d" % (n % 4)], ["CM%d" % n], GA)
-
-    def bits(t, src, nm, bk, z, zn):
-        p = str(t & 1)
-        c = slice(256 * (t & 1), 256 * (t & 1) + 256)
-        o = B[bk][:, 0:256]
-        if nm == "cw":
-            its = [(o, T.OBb[:], cB, True, False, 256), (o, T.Ihalf[:], T.FWq[:, c], False, False, 256), (o, T.OBb[:], src, False, True, 256)]
-        else:
-            its = [(o, T.OBb[:], cE, True, False, 256), (o, T.OBm[:], cB, False, False, 256),
-                   (o, T.Ihalf[:], T.FWq[:, c], False, False, 256), (o, T.OBm[:], src, False, True, 256)]
-        mm(its, ["OBb", "OBm", "cB", "cE", "Ihalf", "FWq" + p, nm], ["B%d" % bk])
-        tt(z, o, T.FIq[:, c], A.mult, 256, ["B%d" % bk, "FIq" + p], [zn])
-        ts(z, z, 1, None, A.bitwise_and, None, 256, [zn], [zn])
+    def scores(t, lo, hi):
+        XL = "XL%d" % t
+        for n in range(lo, hi):
+            xq, bk, ad = blk("XQ", n, 512), B(n % 2), blk("AD", n % 4, 512)
+            if n in VQ[t]:
+                cp(xq, ind(r(XL, 0, 4096), blk("QU", n, 32)))
+            else:
+                act(xq, ind(r(XL, 0, 4096), blk("QU", n, 32)), F.Copy)
+            mm(acc(bk, [(Ib, xq), (blk("XT", n // 4), blk("EX", n % 4, 512))]))
+            act(ad, bk, F.Abs)
+            tt(blk("CM", n, 512), ind(r(XL, 4096, 8192), blk("HU", n, 32)), ad, A.is_ge)
 
     def early(t):
         par = t & 1
-        p = str(par)
-        c = slice(256 * par, 256 * par + 256)
-        XL = T["XL%d" % t]
-        Lf, Lw = T.LU[:, 64 * t + 16:64 * t + 32], T.LU[:, 64 * t + 48:64 * t + 64]
-        lu, pu, th = "LU%d" % t, "PU%d" % t, ("XLt0" if t == 0 else "xxs%d" % t)
-        p0 = 32 * t + 16 * par
-        ne = T.fl[:, 0:256]
-        act(ne, T.NX[:, c], F.Sign, 256, ["N" + p], ["ne"])
-        act(T.Ws[:, c], T.WF[:].indirect(Lw), F.Copy, 256, ["WA0", "WA1", "FW", lu + "W"], ["Ws" + p], GA)
-        act(T.FWq[:, c], T.WF[:, 512:1024].indirect(T.PU[:, p0:p0 + 16]), F.Copy, 256, ["FW", pu], ["FWq" + p], GA)
-        act(T.FIq[:, c], T.FI[:].indirect(Lf), F.Copy, 256, ["FI", "FIz", lu + "F"], ["FIq" + p], GA)
-        act(T.sc[:, 0:1], XL[:, 8193:8194], F.Identity, 1, [th], ["sc0"], scale=K, bias=-50.0 * K - BIG)
-        act(T.thr[:, c], T.STP[:].indirect(Lw), F.Identity, 256, ["STP", "STP1", lu + "W", "sc0"], ["thr" + p], GA,
-            bias=BIG, scale=T.sc[:, 0:1])
-
-    def early2(t):
-        par = t & 1
-        p = str(par)
-        c = slice(256 * par, 256 * par + 256)
-        ne = T.fl[:, 0:256]
-        b1, b2 = (3, 3) if t else (5, 4)
-        mm([(B[b2][:, 0:256], T.FST[:], ne, True, True, 256)], ["FST", "ne"], ["B%d" % b2])
-        act(T.fl[:, 768 + 256 * par:1024 + 256 * par], B[b2][:, 0:256], F.Relu, 256, ["B%d" % b2, "k1"], ["first" + p], bias=k1)
-        bits(t, T.Ws[:, c], "Ws" + p, b1, T.zi[:, c], "zi" + p)
+        ne, o = blk("ne", par, 256), B(7, 0, 256)
+        if t > 1:
+            act(ne, blk("NX", par, 256), F.Sign)
+        mm([(o, r("FST"), ne, True, True)])
+        act(blk("first", par, 256), o, F.Relu, bias=k1)
 
     def masks(t):
         par = t & 1
-        p = str(par)
-        XL = T["XL%d" % t]
-        Ly, Lf, Ln, Lw = [T.LU[:, 64 * t + 16 * i:64 * t + 16 * i + 16] for i in range(4)]
-        lu, pu, th = "LU%d" % t, "PU%d" % t, ("XLt0" if t == 0 else "xxs%d" % t)
-        p0 = 32 * t + 16 * par
-        PL = T.PU[:, p0:p0 + 16]
-        qne, first = T.fl[:, 256:512], T.fl[:, 768 + 256 * par:1024 + 256 * par]
-        cc = slice(256 * par, 256 * par + 256)
-        act(qne, T.NX[:, 0:512].indirect(PL), F.Sign, 256, NW + [pu], ["qne"], GA)
-        act(T.Ns[:], T.NX[:, 0:512].indirect(Ln), F.Copy, 256, NW + [lu + "N"], ["Ns"], GA)
-        for h in ((0, 1) if t == 0 else (1 - par,)):
-            its = []
-            bk = 6 if t == 0 and h else 7
-            bn = "B%d" % bk
-            for k in (2 * h, 2 * h + 1):
-                o = B[bk][:, 128 * (k & 1):128 * (k & 1) + 128]
-                its += [(o, T.WF[:, 128 * k:128 * k + 128], T.PK[:], True, False, 128), (o, T.ONb[:], T.PK32[:], False, True, 128)]
-            mm(its, ["WA%d" % h, "PK", "PK32", "ONb"], [bn])
-            c = slice(256 * h, 256 * h + 256)
-            cp(T.mi[:, c], B[bk][:, 0:256], 256, [bn], ["mi%d" % h])
-            tt(T.MT[:, c], T.mi[:, c], B[bk][:, 0:256], A.is_gt, 256, [bn, "mi%d" % h], ["MT%d" % h])
+        XL = "XL%d" % t
+        one, cd = r("ONE", 0, 256), blk("CD", t, 256)
+        W = blk("WF", par, 256)
+        ts(r("q"), r("QU"), 4095.0, None, A.is_lt)
+        act(r("Ns"), ind(NW, blk("LU", 2 * t + 1, 16)), F.Copy)
+        mm(acc(B(3, 256, 512), [(DG(13), one), (DG(13), cd)]))
+        tt(r("Nx"), B(3, 256, 512), blk("NX", par, 256), A.min)
+        mm([it for k in range(4) for it in acc(B(3, 128 * k, 128 * k + 128), [(r("Ihn"), blk("QH", k // 2)), (In, ONb)])])
         for q in range(8):
-            mm([(B[2][:, 16 * q:16 * q + 16], T.OH[:, 128 * (8 * k + q):128 * (8 * k + q) + 128],
-                 T.MT[:, 128 * k + 16 * q:128 * k + 16 * q + 16], k == 0, k == 3, 16) for k in range(4)],
-               ["MT0", "MT1"] + ["OH%d" % (8 * k + q) for k in range(4)], ["B2"])
-        act(T.ki[:], B[2][:, 0:128], F.Identity, 128, ["B2"], ["ki"], scale=1.0 / 1024, bias=RND)
-        act(T.ki[:], T.ki[:], F.Identity, 128, ["ki"], ["ki"], scale=1024.0, bias=-1024.0 * RND)
-        act(T.nh[:, 128:256], T.ki[:], F.Relu, 128, ["ki"], ["nh1"], scale=-1.0, bias=1.0)
-        tt(T.nh[:, 0:128], B[2][:, 0:128], T.ki[:], A.is_equal, 128, ["B2", "ki"], ["nh0"])
-        mm([(B[7][:, 128 * f:128 * f + 128], T.nh[:, 128 * f:128 * f + 128], T.Ib[:], True, True, 128) for f in range(2)],
-           ["nh0", "nh1", "Ib"], ["B7"])
-        tt(T.cw[:], B[7][:, 0:256], T.Ws[:, cc], A.mult, 256, ["B7", "Ws" + p], ["cw"])
-        bits(t, T.cw[:], "cw", 6, T.zi[:, 512:768], "zc")
-        o = B[5][:, 0:256]
-        mm([(o, T.OBb[:], cC, True, False, 256), (o, T.OBm[:], first, False, False, 256), (o, T.In[:], qne, False, True, 256)],
-           ["OBb", "OBm", "cC", "In", "qne", "first" + p], ["B5"])
-        tt(T.pj[:], o, T.zi[:, cc], A.is_lt, 256, ["B5", "zi" + p], ["pj"])
-        ts(T.sg[:], T.zi[:, 512:768], -2.0 / K, 1.0 / K, A.mult, A.add, 256, ["zc"], ["sg"])
-        tt(T.NJ[:], T.NX[:, 0:512].indirect(PL), T.pj[:], A.mult, 256, NW + ["pj", pu], ["NJ"], GA)
-        if t == 0:
-            act(T.sc[:, 1:2], XL[:, 8192:8193], F.Identity, 1, [th], ["sc1"], scale=-K, bias=50.0 * K)
-        else:
-            mm([(B[5][:, 0:1], T.ONf[:], T.sc[:, 4 + k:5 + k], k == 0, k == len(CUTS) - 1, 1, 4) for k in range(len(CUTS))],
-               ["ONf"] + ["cnt%d" % x for x in CUTS], ["B5"])
-            cp(T.si[:, 0:1], B[5][:, 0:1], 1, ["B5"], ["si"])
-            ts(T.si[:, 0:1], T.si[:, 0:1], 1, None, A.bitwise_and, None, 1, ["si"], ["si"])
-            tt(T.sc[:, 2:3], T.si[:, 0:1], XL[:, 8192:8193], A.add, 1, ["si", th], ["sc2"])
-            act(T.sc[:, 1:2], T.sc[:, 2:3], F.Identity, 1, ["sc2"], ["sc1"], scale=-K, bias=50.0 * K)
-        act(T.DJ[:], T.Ib[:], F.Copy, 128, ["Ib", "sc1"], ["DJ"], scale=T.sc[:, 1:2])
+            mm(acc(B(7, 16 * q, 16 * q + 16), [(r("OH", 256 * (8 * k + q) + 128 * par, 256 * (8 * k + q) + 128 * par + 128),
+                                               r("MT", 128 * k + 16 * q, 128 * k + 16 * q + 16)) for k in range(4)]))
+        ts(r("ki"), B(7, 0, 128), 1024.0 * RND, -1024.0 * RND, A.add, A.add)
+        tt(blk("nh", 0), B(7, 0, 128), r("ki"), A.is_equal)
+        act(blk("nh", 1), r("ki"), F.Relu, scale=-1.0, bias=1.0)
+        o = B(7, 256, 512)
+        its = []
+        for f in range(2):
+            its += acc(B(7, 256 + 128 * f, 384 + 128 * f), [(Ib, blk("ne", 2 * par + f)), (Ib, r("NEG", 0, 128)), (blk("nh", f), Ib)])
+        mm(its)
+        cw = r("cw", 0, 256)
+        tt(cw, o, W, A.mult)
+        for th in ([], [], [blk("TH", 0, 256)], [blk("TH", 1, 256), blk("TH", 2, 256)])[t]:
+            mm(bit(o, cw))
+            ts(o, o, 0.0, None, A.is_gt)
+            tt(cw, o, th, A.mult)
+        mm(bit(o, cw))
+        ts(r("cb"), o, 0.0, -1.0, A.is_gt, A.mult)
+        o = B(4, 0, 256)
+        if t == 3:
+            mm([(B(4, 128 * f, 128 * f + 128), blk("MT", 2 * par + f), Ib, True, True) for f in range(2)])
+            tt(r("cw", 256, 512), o, blk("TH", 2, 256), A.mult)
+            mm(bit(o, r("cw", 256, 512)))
+            ts(r("b3"), o, 0.0, None, A.is_gt)
+        its = []
+        for f in range(2):
+            held = (In, blk("b3", f)) if t == 3 else (blk("MT", 2 * par + f), In)
+            its += acc(B(4, 128 * f, 128 * f + 128),
+                       [held, (Ib, blk("q", f)), (OBb, blk("first", 2 * par + f)), (Ib, blk("CD", 2 * t + f))])
+        mm(its)
+        act(r("pj"), o, F.Relu, bias=-2.0)
+        o = B(4, 256, 512)
+        mm(acc(o, [(r("N256"), cd), (DG(8), r("q")), (DG(5), r("cb"))]))
+        act(r("sc", 0, 1), r(XL, 8193, 8194), F.Identity, bias=-512.0)
+        act(r("thr"), o, F.Identity, bias=r("sc", 0, 1))
+        act(r("sc", 1, 2), r(XL, 8192, 8193), F.Identity, scale=-KL, bias=-32.0 * KL - 48 * LN2)
+        if t:
+            act(r("cn", 0, 2), B(2, 384, 386), F.Copy)
+            mm(acc(B(2, 386, 387), [(ONb, r("cn", f, f + 1)) for f in range(2)]))
+            cp(r("si", 0, 1), B(2, 386, 387))
+            ts(r("si", 0, 1), r("si", 0, 1), 1, None, A.bitwise_and)
+            ts(r("sc", 2, 3), r("si", 0, 1), -KL, r("sc", 1, 2), A.mult, A.add)
 
-    def back(t):
+    def piece(t, f):
         par = t & 1
-        lo = 0
-        for hi in CUTS:
-            piece(t, lo, hi)
-            if lo == 0 and t < 3:
-                early2(t + 1)
-            lo = hi
-        c = slice(256 * par, 256 * par + 256)
-        if t == 2:
-            act(T.OC[:, 0::2], T.NX[:, c], F.Identity, 256, ["N0"], ["OC0"], bias=4095.0, scale=-1.0)
-
-    def piece(t, lo, hi):
-        par = t & 1
-        p, s, n = str(par), str(hi), hi - lo
-        c = slice(lo, hi)
-        d = slice(256 * par + lo, 256 * par + hi)
-        first = T.fl[:, 768 + 256 * par + lo:768 + 256 * par + hi]
-        sb = 3 if lo == 0 else 2
-        sn = "B%d" % sb
-        for q in range(lo // 64, hi // 64):
-            e = slice(64 * q, 64 * q + 64)
-            o = B[sb][:, e]
-            its = [(o, T.OBb[:], T.CST[:, e], True, False, 64), (o, T.D3[:], T.fl[:, 256 + 64 * q:320 + 64 * q], False, False, 64),
-                   (o, T.DJ[:], T.pj[:, e], False, False, 64), (o, T.D1[:], T.sg[:, e], False, False, 64)]
-            its += [(o, T.BM[:, 15 - j:143 - j], T.CM[:, 1024 * q + j:1024 * q + 1024:16], False, j == 15, 64) for j in range(16)]
-            mm(its, ["OBb", "cA", "D3", "qne", "DJ", "pj", "D1", "sg", "BM", "CM%d" % (2 * q), "CM%d" % (2 * q + 1)], [sn])
-        Sp, H0, H1 = B[sb][:, c], B[4][:, c], B[4][:, 256 + lo:256 + hi]
-        h0, h1 = "H0" + s, "H1" + s
-        tt(T.u[:, c], Sp, T.sg[:, c], A.mult, n, [sn, "sg"], ["u" + s])
-        tt(T.u[:, c], Sp, T.u[:, c], A.min, n, [sn, "u" + s], ["u" + s])
-        act(T.w[:, c], T.u[:, c], F.Exp, n, ["u" + s], ["w" + s], scale=6 * LN2)
-        tt(H0, Sp, T.thr[:, d], A.is_le, n, [sn, "thr" + p, "B4"], [h0])
-        tt(T.Wp[:, c], H0, T.Ws[:, d], A.mult, n, [h0, "Ws" + p], ["Wp" + s])
-        mm([(B[5][:, c], T.TRI[:], T.w[:, c], True, True, n)], ["TRI", "w" + s], ["B5"])
-        ts(H1, B[5][:, c], 0.0, None, A.is_lt, None, n, ["B5"], [h1])
-        tt(T.b[:, c], H1, T.FWq[:, d], A.mult, n, [h1, "FWq" + p], ["b" + s])
-        tt(T.a[:, c], H1, T.NJ[:, c], A.mult, n, [h1, "NJ"], ["a" + s])
-        bw, bn = (7, 6) if lo == 0 else (0, 1)
-        wn, nn = "B%d" % bw, "B%d" % bn
-        mm([(B[bw][:, c], T.OBb[:], T.b[:, c], True, True, n)], ["OBb", "b" + s], [wn])
-        mm([(B[bn][:, c], T.OBf[:], T.a[:, c], True, True, n, 4)], ["OBf", "a" + s], [nn])
-        tt(H0, B[bw][:, c], T.Wp[:, c], A.not_equal, n, [wn, "Wp" + s], [h0])
-        tt(H1, H0, T.Ns[:, c], A.mult, n, [h0, "Ns"], [h1])
-        tt(T.t[:, c], B[bn][:, c], first, A.mult, n, [nn, "first" + p], ["t" + s])
+        X, Z1, Z2 = ((2, 4, 5), (6, 0, 1))[f]
+        d = 2 * par + f
+        v, ta, tb = B(X, 0, 128), B(X, 128, 256), B(X, 256, 384)
+        wA, wB, KP, cb = [blk(n, f) for n in ("wA", "wB", "KP", "cb")]
+        HA, HB, pA, pB = blk("H", 2 * f), blk("H", 2 * f + 1), blk("p", 2 * f), blk("p", 2 * f + 1)
+        cd, first, neg = blk("CD", 2 * t + f), blk("first", d), r("NEG", 0, 128)
+        for k in range(2):
+            o, e = B(X, 64 * k, 64 * k + 64), 1024 * (2 * f + k)
+            mm(acc(o, [(DG(5), blk("pj", 2 * f + k, 64)), (DG(5), blk("cb", 2 * f + k, 64))]
+                   + [(r("BM", 15 - j, 143 - j), r("CM", e + j, e + 1024, 16)) for j in range(16)]))
+        act(wA, v, F.Exp, scale=KL, bias=r("sc", 2, 3) if t else r("sc", 1, 2))
+        act(wB, v, F.Exp, scale=-KL, bias=48 * LN2 - 32 * KL)
+        mm([(ta, r("TRI"), wA, True, True)] + acc(tb, [(r("N60"), neg), (r("N60"), cd), (r("TRI"), wB)]))
+        ts(blk("H", f, 256), B(X, 128, 384), -2.0 ** -50, None, A.is_lt)
+        tt(blk("p", f, 256), B(3, 256 * f, 256 * f + 256), blk("H", f, 256), A.mult)
+        tt(KP, v, blk("thr", f), A.is_le)
+        z, y = B(Z1, 0, 128), B(Z2, 0, 128)
+        mm(acc(z, [(r("Ifn"), blk("Nx", f))], stop=False))
+        mm(acc(y, [(DG(12), first), (DG(13), neg)], stop=False))
+        mm(acc(z, [(r("O8k"), HA), (r("O2k"), HB)], start=False, stop=False) + acc(y, [(r("O6k"), HA)], start=False, stop=False))
+        mm(acc(y, [(r("OBh"), pA)], start=False) + acc(z, [(r("OBh"), pB), (In, KP)], start=False))
+        act(blk("AB", f), z, F.Abs, scale=4096.0)
+        tt(y, y, blk("Ns", f), A.max)
         if t < 3:
-            tt(T.NX[:, d], H1, T.t[:, c], A.add, n, [h1, "t" + s], ["N" + p])
-            k = 4 + CUTS.index(hi)
-            act(T.w[:, c], T.t[:, c], F.Sign, n, ["t" + s], ["w" + s, "cnt" + s], acc=T.sc[:, k:k + 1])
-            tt(T.tw[:, c], B[bw][:, c], T.w[:, c], A.mult, n, [wn, "w" + s], ["tw" + s])
-            tt(H0, H0, T.Wp[:, c], A.mult, n, [h0, "Wp" + s], [h0])
-            tt(T.WF[:, d], H0, T.tw[:, c], A.max, n, [h0, "tw" + s], ["WA" + p])
+            tt(blk("NX", d), y, blk("AB", f), A.min)
+            o = B(7, 128 * f, 128 * f + 128)
+            mm(acc(o, [(DG(6), blk("MT", d)), (cb, DG(4)), (cd, DG(4))] + ([(blk("CD", f), r("D10"))] if t == 2 else [])
+                   + [(KP, DG(7)), (HA, r("MJ")), (HB, r("N35"))]))
+            ts(blk("MT", d), o, 40.0, None, A.is_gt)
+            mm([(B(2, 384 + f, 385 + f), HA, r("ONE", 0, 1), True, True)])
         else:
-            tt(H1, H1, T.t[:, c], A.add, n, [h1, "t" + s], [h1])
-            ts(T.OC[:, 2 * lo + 1:2 * hi:2], H1, -1.0, 4095.0, A.mult, A.add, n, [h1], ["OC" + s])
-
+            tt(y, y, blk("AB", f), A.min)
+            ts(r("OC", 256 * f + 1, 256 * f + 256, 2), y, -1.0, 4095.0, A.mult, A.add)
+        if t < 2:
+            o = B(Z2, 128, 256)
+            mm(acc(o, [(DG(16), first), (DG(16), neg), (r("PW2"), HA)]))
+            tt(blk("WF", d), o, blk("WF", d), A.max)
 
     lists(0)
-    columns((0,))
     compare(0)
-    compare(1)
     tops(0)
-    tops(1)
     chain(0)
+    compare(1)
     head(0)
-    scores(0)
     lists(1)
+    onehot()
+    tops(1)
+    hop(0)
+    frames()
+    code(0, 7)
+    early(0)
     chain(1)
     lists(2)
+    hop(1)
     chain(2)
     lists(3)
-    frames()
-    onehot(0)
-    early(0)
-    early2(0)
-    masks(0)
-    columns((1, 3))
-    columns((2,))
     chain(3)
     parents_out()
     for t in range(4):
         if t > 0:
             head(t)
-            scores(t)
-            masks(t)
+        masks(t)
+        scores(t, 0, 8)
         if t < 3:
-            onehot(t + 1)
+            code(t + 1, 7)
             early(t + 1)
-        back(t)
+        piece(t, 0)
+        piece(t, 1)
+        if t == 2:
+            act(r("OC", 0, 512, 2), blk("NX", 0, 256), F.Identity, bias=4095.0, scale=-1.0)
     return ops
 
 
-EXT = {"xcq": ("dcq", 2600), "xpt": ("dpt", 2300), "xth": ("dth", 2400), "xxs0": ("dxs", 7000), "xlim0": ("dlim", 11000),
-       "xxs1": ("arr1", 22000), "xlim1": ("arr1", 22000), "xxs2": ("arr2", 34000), "xlim2": ("arr2", 34000),
-       "xxs3": ("arr3", 46000), "xlim3": ("arr3", 46000)}
+EXT = {"dcq": 2600, "dpt": 2300, "dth": 2400, "dxs": 7000, "dlim": 11000}
+SEND = 14000.0
+
+
+def outside(x):
+    n = x[0]
+    if n in ("cqs", "pts", "ths"):
+        return {"cqs": "dcq", "pts": "dpt", "ths": "dth"}[n]
+    if n == "XL0":
+        return "dxs" if x[1] < 4096 else ("dlim" if x[1] < 8192 else None)
+    return "arr" + n[2] if n[:2] == "XL" else None
+
+
+def meet(a, b):
+    if a[2] <= b[1] or b[2] <= a[1]:
+        return False
+    return not (a[3] == b[3] > 1 and (a[1] - b[1]) % a[3])
 
 
 def schedule(ops):
     n = len(ops)
-    lastw, readers = {}, {}
-    deps = [set() for _ in range(n)]
+    seen = {}
+    deps, below = [], []
     for i, o in enumerate(ops):
-        rd, wr = list(o["r"]), list(o["w"])
-        for r in rd:
-            if r in lastw:
-                deps[i].add(lastw[r])
-            if r[0] == "B" and r[1:].isdigit():
-                deps[i].update(x for x in readers.get(r, []) if ops[x]["e"] != o["e"])
-        for r in wr:
-            if r in lastw:
-                deps[i].add(lastw[r])
-            deps[i].update(readers.get(r, []))
-        for r in rd:
-            readers.setdefault(r, []).append(i)
-        for r in wr:
-            lastw[r] = i
-            readers[r] = []
-        deps[i].discard(i)
+        d = set()
+        use = [(x, False) for x in o["r"]] + [(x, True) for x in o["w"]]
+        for x, w in use:
+            for j, y, v in seen.get(x[0], []):
+                if psum(x) and (ops[j]["e"] != o["e"] or o["e"] == "P") or (w or v) and meet(x, y):
+                    d.add(j)
+        for x, w in use:
+            if w or o["e"] != "D":
+                seen.setdefault(x[0], []).append((i, x, w))
+        d.discard(i)
+        keep, cover = [], 0
+        for j in sorted(d, reverse=True):
+            if not cover >> j & 1:
+                keep.append(j)
+                cover |= below[j] if ops[j]["e"] != "D" else 0
+        deps.append(keep)
+        below.append(cover | 1 << i)
     succ = [[] for _ in range(n)]
     for i in range(n):
         for d in deps[i]:
             succ[d].append(i)
-    if "start" not in CACHE:
-        CACHE["start"] = arrange(ops, deps, succ)
-    start = CACHE["start"]
-    for i in range(n):
-        ops[i]["t"] = start[i]
-    return sorted(range(n), key=lambda i: (start[i], i)), deps, succ, max(start[i] + ops[i]["c"] for i in range(n))
+    start = arrange(ops, deps, succ)
+    return sorted(range(n), key=lambda i: (start[i], i)), deps, start
 
 
 CACHE = {}
-LAT = 220.0
-ROUNDS = 4500
+LAT = 200.0
+ROUNDS = 4000
 
 
 def place(seq, pre, eng, cost, rel):
-    line = {"V": [], "S": [], "P": [], "G": []}
+    line = {"V": [], "S": [], "P": [], "G": [], "D": []}
     st = [0.0] * len(seq)
     for i in seq:
         e, c, t = eng[i], cost[i], rel[i]
@@ -661,7 +591,7 @@ def place(seq, pre, eng, cost, rel):
 def arrange(ops, deps, succ):
     n = len(ops)
     eng, cost = [o["e"] for o in ops], [o["c"] for o in ops]
-    rel = [max([EXT[r][1] for r in o["r"] if r in EXT] + [0.0]) for o in ops]
+    rel = [max([EXT.get(outside(x), 0.0) for x in o["r"]] + [0.0]) for o in ops]
     way = [0.0] * n
     for i in range(n - 1, -1, -1):
         way[i] = cost[i] + max([way[s] + LAT for s in succ[i]] + [0.0])
@@ -674,7 +604,7 @@ def arrange(ops, deps, succ):
             rnd = (rnd * 1103515245 + 12345) % 2147483648
             t0, amp = rnd / 2147483648.0 * span, (500.0, 1500.0, 4000.0)[k % 3]
             for i in range(n):
-                if abs(best[i] - t0) < 9000:
+                if abs(best[i] - t0) < 7000:
                     rnd = (rnd * 1103515245 + 12345) % 2147483648
                     key[i] += rnd / 2147483648.0 * amp
                 for d in deps[i]:
@@ -703,7 +633,9 @@ def rank_program(g, core, T, topo):
     g.sync.dma_start(T.XL0[:, 4096:8192], T.lim[:]).then_inc(sem.dlim, 16)
 
     ops = build(g, T)
-    order, deps, succ, _ = schedule(ops)
+    if "plan" not in CACHE:
+        CACHE["plan"] = schedule(ops)
+    order, deps, start = CACHE["plan"]
     Q = {"V": g.vector, "S": g.scalar, "P": g.tensor, "G": g}
     SM = {"V": sem.sV, "S": sem.sS, "P": sem.sP, "G": sem.sG}
     arrive = {}
@@ -711,8 +643,7 @@ def rank_program(g, core, T, topo):
         arrive["arr%d" % t] = len(topo.engines(T.cores[(rank + t) % n], core))
     count = {"V": 0, "S": 0, "P": 0, "G": 0}
     mark = {}
-    outs = ["OP", "OC0", "XLt0"] + ["OC%d" % x for x in CUTS]
-    last = {}
+    wrote = []
 
     known = {e: {} for e in Q}
     after = {}
@@ -724,34 +655,27 @@ def rank_program(g, core, T, topo):
             for k, x in after.get((name, v), {}).items():
                 known[e][k] = max(known[e].get(k, 0), x)
 
-    sent = [0, 0]
-
-    def send():
-        t = sent[0] + 1
-        if t == 1:
-            wait("G", "dxs", sem.dxs, 16)
-            wait("G", "dlim", sem.dlim, 16)
-            wait("G", last["XLt0"][0], SM[last["XLt0"][0]], last["XLt0"][1])
-        else:
-            g.wait_ge(sem.sent, sent[1])
-        dst = T.cores[(rank - t) % n]
-        rid, pid, _ = topo.addr(dst)
-        g.remote_dma(T["XL%d" % t][:], T.XL0[:], sem["arr%d" % t], sem.sent, pid, rid, topo.mask(core, dst))
-        sent[0] = t
-        sent[1] += len(topo.engines(core, dst))
+    def ready(q, x):
+        need = {}
+        for y, e, c in wrote:
+            if y[0] == x[0] and meet(x, y):
+                need[e] = max(need.get(e, 0), c)
+        for e in need:
+            q.wait_ge(SM[e], need[e])
 
     for i in order:
         o = ops[i]
         e = o["e"]
-        if e == "G" and sent[0] == 0 and o["t"] >= EXT["xlim0"][1] and last.get("XLt0", "G")[0] == "V":
-            send()
-        for r in o["r"]:
-            if r in EXT:
-                wait(e, EXT[r][0], sem[EXT[r][0]], arrive.get(EXT[r][0], 16))
+        if e == "D":
+            continue
+        for x in o["r"]:
+            s = outside(x)
+            if s:
+                wait(e, s, sem[s], arrive.get(s, 16))
         need = {}
         for d in deps[i]:
             de = ops[d]["e"]
-            if de == "P" and e == "P":
+            if de == "D" or de == "P" and e == "P":
                 continue
             need[de] = max(need.get(de, 0), mark[d])
         for de in sorted(need, key=lambda x: x == e):
@@ -761,22 +685,26 @@ def rank_program(g, core, T, topo):
         ins.then_inc(SM[e], 1)
         mark[i] = count[e]
         after[(e, count[e])] = dict(known[e])
-        for r in o["w"]:
-            if r in outs:
-                last[r] = (e, count[e])
-    while sent[0] < n - 1:
-        send()
-    g.wait_ge(sem.sent, sent[1])
+        for x in o["w"]:
+            if x[0] in ("OP", "OC", "XL0"):
+                wrote.append((x, e, count[e]))
 
-    g.sync.wait_ge(SM[last["OP"][0]], last["OP"][1])
+    g.wait_ge(sem.dxs, 16)
+    g.wait_ge(sem.dlim, 16)
+    ready(g, r("XL0", 8192, XW))
+    left = 0
+    for t in range(1, n):
+        dst = T.cores[(rank - t) % n]
+        rid, pid, _ = topo.addr(dst)
+        g.remote_dma(T["XL%d" % t][:], T.XL0[:], sem["arr%d" % t], sem.sent, pid, rid, topo.mask(core, dst))
+        left += len(topo.engines(core, dst))
+        g.wait_ge(sem.sent, left)
+
+    ready(g.sync, r("OP"))
     g.sync.dma_start(T.yp[:], T.OP[:]).then_inc(sem.dout, 16)
-    g.sync.wait_ge(SM[last["OC0"][0]], last["OC0"][1])
-    lo = 0
-    for hi in CUTS:
-        r = last["OC%d" % hi]
-        g.sync.wait_ge(SM[r[0]], r[1])
-        g.sync.dma_start(T.yc[:, 2 * lo:2 * hi], T.OC[:, 2 * lo:2 * hi]).then_inc(sem.dout, 16)
-        lo = hi
-    g.sync.wait_ge(sem.dout, 16 + 16 * len(CUTS))
+    for f in range(2):
+        ready(g.sync, r("OC", 256 * f, 256 * f + 256))
+        g.sync.dma_start(T.yc[:, 256 * f:256 * f + 256], T.OC[:, 256 * f:256 * f + 256]).then_inc(sem.dout, 16)
+    g.sync.wait_ge(sem.dout, 48)
     for e in count:
         g.sync.wait_ge(SM[e], count[e])

@@ -31,11 +31,11 @@ for _n, _c, _d in [
     ("I144", 144, "float32"), ("IL", 32, "float32"), ("I256", 256, "bfloat16"),
     ("EQ", 16, "bfloat16"), ("B0b", 144, "bfloat16"), ("CE", 1024, "float16"), ("HX", 32, "float32"),
     ("OBf", 128, "float32"), ("OBb", 128, "bfloat16"), ("OBh", 128, "float16"), ("Ifn", 128, "float32"),
-    ("ONE", 512, "bfloat16"), ("NEG", 256, "bfloat16"), ("RT", 256, "bfloat16"),
+    ("ONE", 512, "bfloat16"), ("NEG", 128, "bfloat16"), ("RT", 256, "bfloat16"),
     ("Ihn", 128, "float16"), ("In", 128, "bfloat16"), ("DG", 17 * 128, "bfloat16"),
-    ("N35", 128, "bfloat16"), ("D10", 128, "bfloat16"), ("N256", 128, "bfloat16"), ("N60", 128, "bfloat16"),
-    ("MJ", 128, "bfloat16"), ("O2k", 128, "bfloat16"), ("O6k", 128, "bfloat16"), ("O8k", 128, "bfloat16"),
-    ("PW2", 128, "bfloat16"),
+    ("N35", 128, "float16"), ("N10", 128, "bfloat16"), ("N16", 128, "bfloat16"), ("D60", 128, "bfloat16"),
+    ("N8k", 128, "bfloat16"), ("MJ", 128, "float16"), ("O2k", 128, "float16"), ("OBm", 128, "bfloat16"),
+    ("O8k", 128, "float16"), ("PW2", 128, "float16"), ("o16", 8, "float16"), ("C3", 16, "bfloat16"), ("CU", 64, "uint16"),
     ("L1", 128, "float16"), ("L2", 128, "float16"), ("BT", 2048, "float16"), ("BM", 144, "bfloat16"),
     ("B0h", 144, "float16"), ("EX", 2048, "bfloat16"), ("FST", 128, "bfloat16"), ("TRI", 128, "bfloat16"),
     ("PK", 128, "bfloat16"), ("PKn", 128, "bfloat16"), ("PK32", 128, "bfloat16"), ("c1", 128, "bfloat16"),
@@ -49,18 +49,19 @@ for _n, _c, _d in [
     ("Ns", 256, "float32"), ("Nx", 256, "float32"), ("thr", 256, "float32"), ("MT", 512, "bfloat16"),
     ("OH", 8192, "bfloat16"), ("ki", 128, "float32"), ("nh", 256, "bfloat16"), ("cw", 512, "bfloat16"),
     ("cb", 256, "bfloat16"), ("b3", 256, "bfloat16"), ("q", 256, "bfloat16"), ("pj", 256, "bfloat16"),
-    ("wA", 256, "bfloat16"), ("wB", 256, "bfloat16"), ("H", 512, "bfloat16"),
+    ("wA", 256, "bfloat16"), ("wB", 256, "bfloat16"), ("H", 512, "float16"),
     ("KP", 256, "bfloat16"), ("p", 512, "float16"), ("AB", 256, "float32"),
     ("sc", 16, "float32"), ("si", 8, "int32"), ("cn", 8, "bfloat16"), ("OC", 512, "float32"), ("OP", 32, "float32"),
 ]:
     _sb(_n, _c, _d)
 
-SEMAPHORES = ["sV", "sS", "sP", "sG", "dcq", "dpt", "dth", "dxs", "dlim", "dout", "sent", "arr1", "arr2", "arr3"]
+SEMAPHORES = ["sV", "sS", "sP", "sG", "dcq", "dpt", "dth", "dxs", "dlim", "dout", "sent",
+              "arr1a", "arr1b", "arr2a", "arr2b", "arr3a", "arr3b"]
 
 CY = 0.83
 PCY = 0.42
 GA = 1.56
-VQ = ((), (1, 3), (1, 3), (1, 3))
+VQ = ((), (1,), (1,), (1, 3))
 
 
 def r(name, lo=0, hi=None, st=1, p=None):
@@ -83,7 +84,7 @@ def narrow(x):
     return SCRATCH[x[0]][2] in ("bfloat16", "float16", "uint16")
 
 
-def build(g, T):
+def build(g, T, send):
     ops = []
     V, S, P = g.vector, g.scalar, g.tensor
 
@@ -160,7 +161,7 @@ def build(g, T):
     def DG(j):
         return blk("DG", j)
 
-    pcol, gcol, kcol, g16, k1, k0, kln = [r("pcf", i, i + 1) for i in range(7)]
+    pcol, gcol, kcol, g16, k1, k0, kln, kn = [r("pcf", i, i + 1) for i in range(8)]
     Ib, In, OBb, ONb = DG(0), r("In"), r("OBb"), r("ONE", 0, 128)
 
     io(r("pci", 0, 1), [[0, 1]], 0, 1, False)
@@ -181,6 +182,7 @@ def build(g, T):
     ms(r("ONE"), 1.0)
     ms(r("NEG"), -1.0)
     ms(r("RT"), RND)
+    ms(r("cn", 2, 3), 0.5)
     for q in range(4):
         sel(blk("EX", q, 512), r("ONE"), [[-1, 32], [0, 16]], A.is_equal, 0.0, -32 * q, 1)
     ts(r("pci", 1, 2), r("pci", 0, 1), 4, None, A.arith_shift_right)
@@ -189,6 +191,7 @@ def build(g, T):
     act(g16, gcol, F.Copy, scale=16.0)
     act(k1, kcol, F.Identity, scale=-1.0, bias=1.0)
     act(k0, k1, F.Relu)
+    act(kn, kcol, F.Copy, scale=-1.0)
     act(kln, kcol, F.Copy, scale=LN2)
     I128f = r("I144", 15, 143)
     ts(OBb, r("IG"), gcol, None, A.is_equal)
@@ -198,11 +201,16 @@ def build(g, T):
         ts(blk("BT", j), OBb, r("EQ", j, j + 1), None, A.mult)
     for j in range(1, 17):
         act(DG(j), Ib, F.Copy, scale=2.0 ** j)
-    for nm, v in (("In", -1.0), ("N35", -35.0), ("D10", 10.0), ("N256", -256.0), ("N60", -2.0 ** 60), ("Ifn", -1.0)):
+    for nm, v in (("In", -1.0), ("N10", -10.0), ("N16", -16.0), ("D60", 2.0 ** 60), ("N8k", -8192.0), ("Ifn", -1.0)):
         act(r(nm), Ib, F.Copy, scale=v)
-    for nm, v in (("OBf", 1.0), ("O2k", 2048.0), ("O6k", 6144.0), ("O8k", 8192.0), ("MJ", 12.0)):
+    for nm, v in (("OBf", 1.0), ("OBm", -1.0), ("c1", 12.0)):
         act(r(nm), OBb, F.Copy, scale=v)
-    sel(r("MJ"), r("MJ"), [[1, 128]], A.not_equal, 76.0, 0, -1)
+    sel(r("c1"), r("c1"), [[1, 128]], A.not_equal, 76.0, 0, -1)
+    cp(r("MJ"), r("c1"))
+    for nm, src, v in (("N35", Ib, -35.0), ("O2k", OBb, 2047.0), ("O8k", OBb, 8192.0)):
+        ts(r(nm), src, v, None, A.mult)
+    cp(r("o16"), r("ONE", 0, 8))
+    io(r("C3"), [[1, 16]], 0, 0)
     cp(r("OBh"), OBb)
     ts(r("Ihn"), Ib, -1.0, None, A.mult)
     ts(r("L1"), blk("BT", 0), 2080.0, None, A.mult)
@@ -229,9 +237,11 @@ def build(g, T):
     mm([(B(7, 0, 2), r("S8", p=(0, 8)), r("thb", 0, 2, p=(0, 8)), True, True)])
     act(r("XL0", 8192, 8194), B(7, 0, 2), F.Copy)
 
-    made = [x for o in ops if o["e"] == "G" for x in o["w"]]
-    for t in range(1, 4):
-        op("D", SEND, made + [r("XL%d" % (t - 1), 4096, XW)], [r("XL%d" % t)], None)
+    for k, (t, lo, hi) in enumerate(SENDS):
+        op("G", 300, [r("XL0", lo, min(hi, 4096)), r("XL0", max(lo, 4096), min(hi, 8192)), r("XL0", min(hi, 8192), hi)],
+           [r("XL%d" % t, lo, hi), r("ths", 4, 5)], lambda k=k: send(k))
+        ops[-1]["r"] = [x for x in ops[-1]["r"] if x[2] > x[1]]
+        ops[-1]["late"] = SEND * (hi - lo) / XW
 
     NW = r("NX", 0, 512)
     PUn = r("PU", 128, 160)
@@ -247,7 +257,7 @@ def build(g, T):
         act(blk("PR0", h, 256), r("PN", h, 512, 2), F.Copy)
 
     def lists(t):
-        bk = 3 if t else 6
+        bk = (6, 3, 7, 7)[t]
         mm([(B(bk, 0, 32), r("B0b", 15 - w, 143 - w), r("PR%d" % t, w, 512, 16), w == 0, w == 15) for w in range(16)])
         act(blk("PF", t, 32), B(bk, 0, 32), F.Identity, bias=256.0)
         cp(blk("PU", t, 32), blk("PF", t, 32))
@@ -293,9 +303,9 @@ def build(g, T):
         act(blk(aw, par, 256), ind(r("NAT" if t == 3 else "IC"), blk("LU", 2 * t + 1, 16)), F.Copy)
         act(r("PN" if t == 3 else "PR%d" % (t + 1)), ind(r(aw), blk("PU", t, 32)), F.Copy)
 
-    def code(t, bk):
-        mm([(B(bk, w, 256, 16), blk("BT", w), blk("CL", t, 16), True, True) for w in range(16)])
-        act(blk("CD", t, 256), B(bk, 0, 256), F.Copy)
+    def code(t):
+        ts(blk("CU", t, 16), blk("CL", t, 16), -1.0, 1.0, A.mult, A.add)
+        act(blk("CD", t, 256), ind(r("C3"), blk("CU", t, 16)), F.Copy)
 
     def parents_out():
         mm([(B(7, 0, 32), r("B0b", 15 - w, 143 - w), r("PN", 256 * (w & 1) + (w >> 1), 256 * (w & 1) + 256, 8), w == 0, w == 15)
@@ -338,10 +348,12 @@ def build(g, T):
         ts(d, a, 127, None, A.bitwise_and)
         tt(blk("PW", 0, 32), c, d, A.add)
         ts(blk("PW", 1, 32), b, 1023.0 / 128, 1.0, A.mult, A.add)
+
+    def hot(par):
         for q in range(8):
             for k in range(4):
                 i = 8 * k + q
-                ts(blk("OH", i, 256), r("I256"), r("PW", i, i + 1), r("PW", 32 + i, 33 + i), A.is_equal, A.mult)
+                ts(blk("OH", 2 * i + par), blk("I256", par), r("PW", i, i + 1), r("PW", 32 + i, 33 + i), A.is_equal, A.mult)
 
     def head(t):
         XL = "XL%d" % t
@@ -379,7 +391,7 @@ def build(g, T):
         if t > 1:
             act(ne, blk("NX", par, 256), F.Sign)
         mm([(o, r("FST"), ne, True, True)])
-        act(blk("first", par, 256), o, F.Relu, bias=k1)
+        act(blk("first", par, 256), o, F.Identity, bias=kn)
 
     def masks(t):
         par = t & 1
@@ -388,19 +400,19 @@ def build(g, T):
         W = blk("WF", par, 256)
         ts(r("q"), r("QU"), 4095.0, None, A.is_lt)
         act(r("Ns"), ind(NW, blk("LU", 2 * t + 1, 16)), F.Copy)
-        mm(acc(B(3, 256, 512), [(DG(13), one), (DG(13), cd)]))
+        mm(acc(B(3, 256, 512), [(DG(14), one), (r("N8k"), cd)]))
         tt(r("Nx"), B(3, 256, 512), blk("NX", par, 256), A.min)
-        mm([it for k in range(4) for it in acc(B(3, 128 * k, 128 * k + 128), [(r("Ihn"), blk("QH", k // 2)), (In, ONb)])])
+        mm([(B(3, 0, 256), r("Ihn"), r("QH"), True, True)])
         for q in range(8):
             mm(acc(B(7, 16 * q, 16 * q + 16), [(r("OH", 256 * (8 * k + q) + 128 * par, 256 * (8 * k + q) + 128 * par + 128),
                                                r("MT", 128 * k + 16 * q, 128 * k + 16 * q + 16)) for k in range(4)]))
         ts(r("ki"), B(7, 0, 128), 1024.0 * RND, -1024.0 * RND, A.add, A.add)
-        tt(blk("nh", 0), B(7, 0, 128), r("ki"), A.is_equal)
-        act(blk("nh", 1), r("ki"), F.Relu, scale=-1.0, bias=1.0)
+        tt(blk("nh", 0), B(7, 0, 128), r("ki"), A.not_equal)
+        act(blk("nh", 1), r("ki"), F.Sign)
         o = B(7, 256, 512)
         its = []
         for f in range(2):
-            its += acc(B(7, 256 + 128 * f, 384 + 128 * f), [(Ib, blk("ne", 2 * par + f)), (Ib, r("NEG", 0, 128)), (blk("nh", f), Ib)])
+            its += acc(B(7, 256 + 128 * f, 384 + 128 * f), [(Ib, blk("ne", 2 * par + f)), (blk("nh", f), In)])
         mm(its)
         cw = r("cw", 0, 256)
         tt(cw, o, W, A.mult)
@@ -418,22 +430,22 @@ def build(g, T):
             ts(r("b3"), o, 0.0, None, A.is_gt)
         its = []
         for f in range(2):
-            held = (In, blk("b3", f)) if t == 3 else (blk("MT", 2 * par + f), In)
+            held = (r("N16"), blk("b3", f)) if t == 3 else (blk("MT", 2 * par + f), r("N16"))
             its += acc(B(4, 128 * f, 128 * f + 128),
-                       [held, (Ib, blk("q", f)), (OBb, blk("first", 2 * par + f)), (Ib, blk("CD", 2 * t + f))])
+                       [held, (DG(4), blk("q", f)), (r("OBm"), blk("ne", 2 * par + f)), (r("N16"), blk("CD", 2 * t + f))])
         mm(its)
-        act(r("pj"), o, F.Relu, bias=-2.0)
+        act(r("pj"), o, F.Sign, bias=-0.5)
         o = B(4, 256, 512)
-        mm(acc(o, [(r("N256"), cd), (DG(8), r("q")), (DG(5), r("cb"))]))
-        act(r("sc", 0, 1), r(XL, 8193, 8194), F.Identity, bias=-512.0)
+        mm(acc(o, [(DG(8), cd), (DG(8), r("q")), (DG(5), r("cb"))]))
+        act(r("sc", 0, 1), r(XL, 8193, 8194), F.Identity, bias=-768.0 - 16.0)
         act(r("thr"), o, F.Identity, bias=r("sc", 0, 1))
-        act(r("sc", 1, 2), r(XL, 8192, 8193), F.Identity, scale=-KL, bias=-32.0 * KL - 48 * LN2)
+        act(r("sc", 1, 2), r(XL, 8192, 8193), F.Identity, scale=-KL, bias=-16.0 * KL - 48 * LN2)
         if t:
             act(r("cn", 0, 2), B(2, 384, 386), F.Copy)
-            mm(acc(B(2, 386, 387), [(ONb, r("cn", f, f + 1)) for f in range(2)]))
-            cp(r("si", 0, 1), B(2, 386, 387))
-            ts(r("si", 0, 1), r("si", 0, 1), 1, None, A.bitwise_and)
-            ts(r("sc", 2, 3), r("si", 0, 1), -KL, r("sc", 1, 2), A.mult, A.add)
+            cn, rt = [r("cn", f, f + 1) for f in range(2)], r("RT", 0, 1)
+            mm(acc(B(2, 386, 387), [(Ib, r("cn", 2, 3))] + [(r("NEG", 0, 128), x) for x in cn]
+                   + [(DG(1), rt), (In, rt), (In, rt)] + [(ONb, x) for x in cn]))
+            act(r("sc", 2, 3), B(2, 386, 387), F.Identity, scale=-KL, bias=r("sc", 1, 2))
 
     def piece(t, f):
         par = t & 1
@@ -442,37 +454,38 @@ def build(g, T):
         v, ta, tb = B(X, 0, 128), B(X, 128, 256), B(X, 256, 384)
         wA, wB, KP, cb = [blk(n, f) for n in ("wA", "wB", "KP", "cb")]
         HA, HB, pA, pB = blk("H", 2 * f), blk("H", 2 * f + 1), blk("p", 2 * f), blk("p", 2 * f + 1)
-        cd, first, neg = blk("CD", 2 * t + f), blk("first", d), r("NEG", 0, 128)
+        cd, first = blk("CD", 2 * t + f), blk("first", d)
         for k in range(2):
             o, e = B(X, 64 * k, 64 * k + 64), 1024 * (2 * f + k)
-            mm(acc(o, [(DG(5), blk("pj", 2 * f + k, 64)), (DG(5), blk("cb", 2 * f + k, 64))]
+            mm(acc(o, [(DG(4), blk("pj", 2 * f + k, 64)), (DG(5), blk("cb", 2 * f + k, 64))]
                    + [(r("BM", 15 - j, 143 - j), r("CM", e + j, e + 1024, 16)) for j in range(16)]))
         act(wA, v, F.Exp, scale=KL, bias=r("sc", 2, 3) if t else r("sc", 1, 2))
-        act(wB, v, F.Exp, scale=-KL, bias=48 * LN2 - 32 * KL)
-        mm([(ta, r("TRI"), wA, True, True)] + acc(tb, [(r("N60"), neg), (r("N60"), cd), (r("TRI"), wB)]))
+        act(wB, v, F.Exp, scale=-KL, bias=48 * LN2 - 48 * KL)
+        mm([(ta, r("TRI"), wA, True, True)] + acc(tb, [(r("D60"), cd), (r("TRI"), wB)]))
         ts(blk("H", f, 256), B(X, 128, 384), -2.0 ** -50, None, A.is_lt)
-        tt(blk("p", f, 256), B(3, 256 * f, 256 * f + 256), blk("H", f, 256), A.mult)
+        tt(pA, B(3, 128 * f, 128 * f + 128), HA, A.mult)
+        tt(pB, B(3, 128 * f, 128 * f + 128), HB, A.mult)
         tt(KP, v, blk("thr", f), A.is_le)
         z, y = B(Z1, 0, 128), B(Z2, 0, 128)
         mm(acc(z, [(r("Ifn"), blk("Nx", f))], stop=False))
-        mm(acc(y, [(DG(12), first), (DG(13), neg)], stop=False))
-        mm(acc(z, [(r("O8k"), HA), (r("O2k"), HB)], start=False, stop=False) + acc(y, [(r("O6k"), HA)], start=False, stop=False))
+        mm(acc(y, [(DG(12), first)], stop=False))
+        mm(acc(z, [(r("O8k"), HA), (r("O2k"), HB)], start=False, stop=False) + acc(y, [(r("O2k"), HA)], start=False, stop=False))
         mm(acc(y, [(r("OBh"), pA)], start=False) + acc(z, [(r("OBh"), pB), (In, KP)], start=False))
         act(blk("AB", f), z, F.Abs, scale=4096.0)
         tt(y, y, blk("Ns", f), A.max)
         if t < 3:
             tt(blk("NX", d), y, blk("AB", f), A.min)
             o = B(7, 128 * f, 128 * f + 128)
-            mm(acc(o, [(DG(6), blk("MT", d)), (cb, DG(4)), (cd, DG(4))] + ([(blk("CD", f), r("D10"))] if t == 2 else [])
+            mm(acc(o, [(DG(6), blk("MT", d)), (cb, DG(4)), (cd, r("N16"))] + ([(blk("CD", f), r("N10"))] if t == 2 else [])
                    + [(KP, DG(7)), (HA, r("MJ")), (HB, r("N35"))]))
-            ts(blk("MT", d), o, 40.0, None, A.is_gt)
-            mm([(B(2, 384 + f, 385 + f), HA, r("ONE", 0, 1), True, True)])
+            ts(blk("MT", d), o, 14.0 if t == 2 else 24.0, None, A.is_gt)
+            mm([(B(2, 384 + f, 385 + f), HA, r("o16", 0, 1), True, True)])
         else:
             tt(y, y, blk("AB", f), A.min)
             ts(r("OC", 256 * f + 1, 256 * f + 256, 2), y, -1.0, 4095.0, A.mult, A.add)
         if t < 2:
             o = B(Z2, 128, 256)
-            mm(acc(o, [(DG(16), first), (DG(16), neg), (r("PW2"), HA)]))
+            mm(acc(o, [(DG(16), first), (r("PW2"), HA)]))
             tt(blk("WF", d), o, blk("WF", d), A.max)
 
     lists(0)
@@ -483,25 +496,28 @@ def build(g, T):
     head(0)
     lists(1)
     onehot()
+    hot(0)
     tops(1)
     hop(0)
     frames()
-    code(0, 7)
+    code(0)
     early(0)
-    chain(1)
-    lists(2)
-    hop(1)
-    chain(2)
-    lists(3)
-    chain(3)
-    parents_out()
     for t in range(4):
         if t > 0:
             head(t)
         masks(t)
         scores(t, 0, 8)
+        if t == 0:
+            hot(1)
+        if t == 2:
+            hop(1)
+        if t == 3:
+            parents_out()
         if t < 3:
-            code(t + 1, 7)
+            if t:
+                lists(t + 1)
+            chain(t + 1)
+            code(t + 1)
             early(t + 1)
         piece(t, 0)
         piece(t, 1)
@@ -511,7 +527,8 @@ def build(g, T):
 
 
 EXT = {"dcq": 2600, "dpt": 2300, "dth": 2400, "dxs": 7000, "dlim": 11000}
-SEND = 14000.0
+SEND = 16000.0
+SENDS = ((1, 0, 4096), (1, 4096, XW), (2, 0, 4096), (2, 4096, XW), (3, 0, 4096), (3, 4096, XW))
 
 
 def outside(x):
@@ -520,7 +537,7 @@ def outside(x):
         return {"cqs": "dcq", "pts": "dpt", "ths": "dth"}[n]
     if n == "XL0":
         return "dxs" if x[1] < 4096 else ("dlim" if x[1] < 8192 else None)
-    return "arr" + n[2] if n[:2] == "XL" else None
+    return "arr" + n[2] + "ab"[x[1] >= 4096] if n[:2] == "XL" else None
 
 
 def meet(a, b):
@@ -541,14 +558,15 @@ def schedule(ops):
                 if psum(x) and (ops[j]["e"] != o["e"] or o["e"] == "P") or (w or v) and meet(x, y):
                     d.add(j)
         for x, w in use:
-            if w or o["e"] != "D":
-                seen.setdefault(x[0], []).append((i, x, w))
+            seen.setdefault(x[0], []).append((i, x, w))
+        if "late" in o and d:
+            d.update(j for j in range(i) if ops[j]["e"] == "G")
         d.discard(i)
         keep, cover = [], 0
         for j in sorted(d, reverse=True):
             if not cover >> j & 1:
                 keep.append(j)
-                cover |= below[j] if ops[j]["e"] != "D" else 0
+                cover |= below[j] if "late" not in ops[j] else 0
         deps.append(keep)
         below.append(cover | 1 << i)
     succ = [[] for _ in range(n)]
@@ -561,17 +579,17 @@ def schedule(ops):
 
 CACHE = {}
 LAT = 200.0
-ROUNDS = 4000
+ROUNDS = 6000
 
 
 def place(seq, pre, eng, cost, rel):
-    line = {"V": [], "S": [], "P": [], "G": [], "D": []}
+    line = {"V": [], "S": [], "P": [], "G": []}
     st = [0.0] * len(seq)
     for i in seq:
         e, c, t = eng[i], cost[i], rel[i]
-        for d in pre[i]:
-            w = 0.0 if e == "P" and eng[d] == "P" else (0.5 * LAT if eng[d] == e else LAT)
-            t = max(t, st[d] + cost[d] + w)
+        for d, w in pre[i]:
+            if st[d] + w > t:
+                t = st[d] + w
         ln = line[e]
         lo, hi = 0, len(ln)
         while lo < hi:
@@ -592,9 +610,14 @@ def arrange(ops, deps, succ):
     n = len(ops)
     eng, cost = [o["e"] for o in ops], [o["c"] for o in ops]
     rel = [max([EXT.get(outside(x), 0.0) for x in o["r"]] + [0.0]) for o in ops]
+
+    def gap(a, b):
+        return ops[a].get("late", 0.0) + (0.0 if eng[a] == eng[b] == "P" else (0.5 * LAT if eng[a] == eng[b] else LAT))
+    fore = [[(d, cost[d] + gap(d, i)) for d in deps[i]] for i in range(n)]
+    aft = [[(s, cost[s] + gap(i, s)) for s in succ[i]] for i in range(n)]
     way = [0.0] * n
     for i in range(n - 1, -1, -1):
-        way[i] = cost[i] + max([way[s] + LAT for s in succ[i]] + [0.0])
+        way[i] = cost[i] + max([way[s] + gap(i, s) for s in succ[i]] + [0.0])
     best, span, rnd = None, 1e18, 12345
     for k in range(ROUNDS):
         if best is None:
@@ -610,10 +633,10 @@ def arrange(ops, deps, succ):
                 for d in deps[i]:
                     key[i] = max(key[i], key[d] + 1e-3)
             seq = sorted(range(n), key=lambda i: (key[i], i))
-        st = place(seq, deps, eng, cost, rel)
+        st = place(seq, fore, eng, cost, rel)
         for _r in range(6 if best is None else 1):
-            back = place(sorted(range(n), key=lambda i: (-st[i] - cost[i], -i)), succ, eng, cost, [0.0] * n)
-            st = place(sorted(range(n), key=lambda i: (-back[i] - cost[i], i)), deps, eng, cost, rel)
+            back = place(sorted(range(n), key=lambda i: (-st[i] - cost[i], -i)), aft, eng, cost, [0.0] * n)
+            st = place(sorted(range(n), key=lambda i: (-back[i] - cost[i], i)), fore, eng, cost, rel)
             sp = max(st[i] + cost[i] for i in range(n))
             if sp <= span:
                 best, span = st, sp
@@ -632,7 +655,19 @@ def rank_program(g, core, T, topo):
     g.sync.dma_start(T.XL0[:, 0:4096], T.xs[:]).then_inc(sem.dxs, 16)
     g.sync.dma_start(T.XL0[:, 4096:8192], T.lim[:]).then_inc(sem.dlim, 16)
 
-    ops = build(g, T)
+    left = [0]
+
+    def send(k):
+        t, lo, hi = SENDS[k]
+        if k:
+            g.wait_ge(sem.sent, left[0])
+        dst = T.cores[(rank - t) % n]
+        rid, pid, _ = topo.addr(dst)
+        x = r("XL%d" % t, lo, hi)
+        g.remote_dma(T[x[0]][:, lo:hi], T.XL0[:, lo:hi], sem[outside(x)], sem.sent, pid, rid, topo.mask(core, dst))
+        left[0] += len(topo.engines(core, dst))
+
+    ops = build(g, T, send)
     if "plan" not in CACHE:
         CACHE["plan"] = schedule(ops)
     order, deps, start = CACHE["plan"]
@@ -640,7 +675,7 @@ def rank_program(g, core, T, topo):
     SM = {"V": sem.sV, "S": sem.sS, "P": sem.sP, "G": sem.sG}
     arrive = {}
     for t in range(1, n):
-        arrive["arr%d" % t] = len(topo.engines(T.cores[(rank + t) % n], core))
+        arrive["arr%da" % t] = arrive["arr%db" % t] = len(topo.engines(T.cores[(rank + t) % n], core))
     count = {"V": 0, "S": 0, "P": 0, "G": 0}
     mark = {}
     wrote = []
@@ -666,8 +701,6 @@ def rank_program(g, core, T, topo):
     for i in order:
         o = ops[i]
         e = o["e"]
-        if e == "D":
-            continue
         for x in o["r"]:
             s = outside(x)
             if s:
@@ -675,12 +708,14 @@ def rank_program(g, core, T, topo):
         need = {}
         for d in deps[i]:
             de = ops[d]["e"]
-            if de == "D" or de == "P" and e == "P":
+            if "late" in ops[d] or de == "P" and e == "P":
                 continue
             need[de] = max(need.get(de, 0), mark[d])
         for de in sorted(need, key=lambda x: x == e):
             wait(e, de, SM[de], need[de])
         ins = o["f"]()
+        if "late" in o:
+            continue
         count[e] += 1
         ins.then_inc(SM[e], 1)
         mark[i] = count[e]
@@ -689,17 +724,7 @@ def rank_program(g, core, T, topo):
             if x[0] in ("OP", "OC", "XL0"):
                 wrote.append((x, e, count[e]))
 
-    g.wait_ge(sem.dxs, 16)
-    g.wait_ge(sem.dlim, 16)
-    ready(g, r("XL0", 8192, XW))
-    left = 0
-    for t in range(1, n):
-        dst = T.cores[(rank - t) % n]
-        rid, pid, _ = topo.addr(dst)
-        g.remote_dma(T["XL%d" % t][:], T.XL0[:], sem["arr%d" % t], sem.sent, pid, rid, topo.mask(core, dst))
-        left += len(topo.engines(core, dst))
-        g.wait_ge(sem.sent, left)
-
+    g.wait_ge(sem.sent, left[0])
     ready(g.sync, r("OP"))
     g.sync.dma_start(T.yp[:], T.OP[:]).then_inc(sem.dout, 16)
     for f in range(2):

@@ -5,7 +5,7 @@ A = AluOpType
 F = ActivationFunctionType
 LN2 = math.log(2.0)
 XW = 8208
-XO = 520
+XO = 512
 KL = 6 * LN2
 RND = 1.5 * 2.0 ** 23
 
@@ -24,34 +24,35 @@ for _i in range(8):
 for _n, _c, _d in [
     ("cqs", 512, "int32"), ("pts", 32, "int32"), ("ths", 8, "int32"), ("thb", 8, "bfloat16"),
     ("LU", 192, "uint16"), ("PU", 160, "uint16"), ("PF", 128, "float32"), ("PW", 64, "bfloat16"),
-    ("NX", 1040, "float32"), ("WF", 528, "bfloat16"), ("TH", 768, "bfloat16"),
+    ("NX", 1024, "float32"), ("WF", 528, "bfloat16"), ("TH", 768, "bfloat16"), ("TT", 512, "bfloat16"),
     ("IC", 512, "bfloat16"), ("NAT", 512, "bfloat16"), ("PERM", 512, "bfloat16"),
     ("AW0", 512, "bfloat16"), ("AW1", 512, "bfloat16"), ("AW3", 512, "bfloat16"),
     ("pci", 8, "int32"), ("pcf", 16, "float32"), ("IG", 128, "float32"), ("IJ", 128, "float32"),
-    ("I144", 144, "float32"), ("IL", 32, "float32"), ("I256", 256, "bfloat16"),
-    ("EQ", 16, "bfloat16"), ("B0b", 144, "bfloat16"), ("CE", 1024, "float16"), ("HX", 32, "float32"),
-    ("OBf", 128, "float32"), ("OBb", 128, "bfloat16"), ("OBh", 128, "float16"), ("Ifn", 128, "float32"),
-    ("ONE", 512, "bfloat16"), ("NEG", 128, "bfloat16"), ("RT", 256, "bfloat16"),
-    ("Ihn", 128, "float16"), ("In", 128, "bfloat16"), ("DG", 17 * 128, "bfloat16"),
-    ("N35", 128, "float16"), ("N10", 128, "bfloat16"), ("N16", 128, "bfloat16"), ("D60", 128, "bfloat16"),
-    ("N8k", 128, "bfloat16"), ("MJ", 128, "float16"), ("O2k", 128, "float16"), ("OBm", 128, "bfloat16"),
-    ("O8k", 128, "float16"), ("PW2", 128, "float16"), ("o16", 8, "float16"), ("C3", 16, "bfloat16"), ("CU", 64, "uint16"),
-    ("L1", 128, "float16"), ("L2", 128, "float16"), ("BT", 2048, "float16"), ("BM", 144, "bfloat16"),
-    ("B0h", 144, "float16"), ("EX", 2048, "bfloat16"), ("FST", 128, "bfloat16"), ("TRI", 128, "bfloat16"),
+    ("I144", 144, "float32"), ("IL", 32, "float32"),
+    ("B0b", 144, "bfloat16"), ("CE", 1024, "float16"), ("HX", 32, "float32"),
+    ("OBb", 128, "bfloat16"),
+    ("ONE", 512, "bfloat16"), ("NEG", 128, "bfloat16"), ("RT", 256, "bfloat16"), ("ZR", 128, "bfloat16"),
+    ("In", 128, "bfloat16"), ("DG", 17 * 128, "bfloat16"),
+    ("N35", 128, "bfloat16"), ("N10", 128, "bfloat16"), ("N16", 128, "bfloat16"), ("D60", 128, "bfloat16"),
+    ("N8k", 128, "bfloat16"), ("MJ", 128, "bfloat16"), ("O2k", 128, "float16"), ("OBm", 128, "bfloat16"),
+    ("O8k", 128, "bfloat16"), ("PW2", 128, "bfloat16"), ("D32", 128, "bfloat16"), ("CU", 64, "uint16"),
+    ("L1", 128, "float16"), ("L2", 128, "float16"), ("BT", 2048, "bfloat16"), ("BM", 144, "bfloat16"),
+    ("EX", 512, "bfloat16"), ("FST", 128, "bfloat16"), ("TRI", 128, "bfloat16"),
     ("PK", 128, "bfloat16"), ("PKn", 128, "bfloat16"), ("PK32", 128, "bfloat16"), ("c1", 128, "bfloat16"),
-    ("S8", 128, "bfloat16"), ("QN", 512, "float16"), ("E", 2048, "bfloat16"),
-    ("ne", 512, "bfloat16"), ("t5", 512, "bfloat16"), ("f5", 512, "float32"),
+    ("S8", 128, "bfloat16"), ("QN", 512, "float16"), ("E", 4096, "bfloat16"),
+    ("ne", 512, "bfloat16"), ("t5", 512, "bfloat16"), ("f5", 512, "float16"),
     ("HL", 64, "float32"), ("tl", 192, "float32"), ("ti", 128, "int32"), ("PN", 512, "bfloat16"),
-    ("CL", 64, "float16"), ("CD", 1024, "bfloat16"), ("first", 512, "bfloat16"),
+    ("CL", 64, "float16"), ("CD", 1024, "bfloat16"), ("F16", 128, "bfloat16"), ("K16", 128, "bfloat16"),
     ("QU", 256, "uint16"), ("QH", 256, "float16"), ("YH", 256, "float16"), ("YU", 16, "uint16"),
     ("XY", 256, "bfloat16"), ("XT", 256, "bfloat16"), ("hm", 256, "float32"), ("hi", 256, "int32"),
-    ("HU", 256, "uint16"), ("XQ", 4096, "bfloat16"), ("AD", 2048, "float32"), ("CM", 4096, "bfloat16"),
-    ("Ns", 256, "float32"), ("Nx", 256, "float32"), ("thr", 256, "float32"), ("MT", 512, "bfloat16"),
-    ("OH", 8192, "bfloat16"), ("ki", 128, "float32"), ("nh", 256, "bfloat16"), ("cw", 512, "bfloat16"),
+    ("HU", 256, "uint16"), ("XQ", 4096, "bfloat16"), ("AD", 4096, "float32"), ("CM", 4096, "bfloat16"),
+    ("Ns", 256, "float32"), ("Nx", 512, "float32"), ("thr", 256, "float32"),
+    ("MT", 1024, "bfloat16"), ("TG", 1024, "bfloat16"),
+    ("OH", 4096, "bfloat16"), ("ki", 128, "float32"), ("nh", 256, "bfloat16"), ("cw", 512, "bfloat16"),
     ("cb", 256, "bfloat16"), ("b3", 256, "bfloat16"), ("q", 256, "bfloat16"), ("pj", 256, "bfloat16"),
-    ("wA", 256, "bfloat16"), ("wB", 256, "bfloat16"), ("H", 512, "float16"),
-    ("KP", 256, "bfloat16"), ("p", 512, "float16"), ("AB", 256, "float32"),
-    ("sc", 16, "float32"), ("si", 8, "int32"), ("cn", 8, "bfloat16"), ("OC", 512, "float32"), ("OP", 32, "float32"),
+    ("wA", 256, "bfloat16"), ("wB", 256, "bfloat16"), ("HA", 256, "float16"), ("HB", 256, "float16"),
+    ("KP", 256, "bfloat16"), ("pA", 256, "float16"), ("pB", 256, "float16"), ("AB", 256, "float32"),
+    ("sc", 16, "float32"), ("cn", 8, "bfloat16"), ("OC", 512, "float32"), ("OP", 32, "float32"),
 ]:
     _sb(_n, _c, _d)
 
@@ -61,7 +62,10 @@ SEMAPHORES = ["sV", "sS", "sP", "sG", "dcq", "dpt", "dth", "dxs", "dlim", "dout"
 CY = 0.83
 PCY = 0.42
 GA = 1.56
-VQ = ((), (1,), (1,), (1, 3))
+ES = ((), ())
+CUT = 192
+VQ = ((), (1, 3), (1, 3), (1, 3))
+XM = (6,)
 
 
 def r(name, lo=0, hi=None, st=1, p=None):
@@ -97,7 +101,8 @@ def build(g, T, send):
 
     def op(eng, ns, rd, wr, fn):
         rd = [x for x in rd if isinstance(x, tuple)]
-        ops.append({"e": eng, "c": ns, "r": rd + [x[5] for x in rd if x[5]], "w": wr, "f": fn})
+        ops.append({"e": eng, "c": ns, "r": rd + [x[5] for x in rd if x[5]], "w": wr, "f": fn,
+                    "g": sum(cols(x) * CY for x in rd if x[5])})
 
     def vc(out, in0, f):
         if in0[5]:
@@ -172,76 +177,72 @@ def build(g, T, send):
     io(r("IC"), [[1, 512]], -256, 0)
     io(r("IL"), [[16, 32]], 0, 0)
     io(r("NAT"), [[1, 2], [2, 256]], -256, 0)
-    io(r("NX", 512, 520), [[0, 8]], 0, 0)
-    io(r("NX", XO + 256, 1040), [[0, 264]], 0, 0)
-    io(r("XL0", 8192, XW), [[0, 16]], 0, 0)
-    io(r("I256"), [[1, 256]], 0, 0)
-    io(r("AW0", 256, 512), [[1, 256]], 0, 0)
-    io(r("AW1", 0, 256), [[1, 256]], -256, 0)
-    io(r("AW3", 0, 256), [[2, 256]], -256, 0)
+    io(blk("AW0", 1, 256), [[1, 256]], 0, 0)
+    io(blk("AW1", 0, 256), [[1, 256]], -256, 0)
+    io(blk("AW3", 0, 256), [[2, 256]], -256, 0)
+    io(blk("NX", 3, 256), [[0, 256]], 0, 0)
+    ms(r("XL0", 8192, XW), 0.0)
     ms(r("ONE"), 1.0)
     ms(r("NEG"), -1.0)
     ms(r("RT"), RND)
+    act(r("ZR"), r("RT", 0, 128), F.Copy, scale=0.0)
     ms(r("cn", 2, 3), 0.5)
-    for q in range(4):
-        sel(blk("EX", q, 512), r("ONE"), [[-1, 32], [0, 16]], A.is_equal, 0.0, -32 * q, 1)
+    io(r("EX"), [[1, 32], [0, 16]], 0, 0)
     ts(r("pci", 1, 2), r("pci", 0, 1), 4, None, A.arith_shift_right)
     ts(r("pci", 2, 3), r("pci", 0, 1), 15, None, A.bitwise_and)
     cp(r("pcf", 0, 3), r("pci", 0, 3))
+    ts(r("pci", 3, 4), r("pci", 0, 1), 31, None, A.bitwise_and)
+    cp(r("pcf", 8, 9), r("pci", 3, 4))
+    ts(r("EX"), r("EX"), r("pcf", 8, 9), None, A.is_equal)
     act(g16, gcol, F.Copy, scale=16.0)
     act(k1, kcol, F.Identity, scale=-1.0, bias=1.0)
     act(k0, k1, F.Relu)
-    act(kn, kcol, F.Copy, scale=-1.0)
+    act(kn, kcol, F.Copy, scale=-65536.0)
     act(kln, kcol, F.Copy, scale=LN2)
     I128f = r("I144", 15, 143)
     ts(OBb, r("IG"), gcol, None, A.is_equal)
-    ts(r("EQ"), r("IJ", 0, 16), kcol, None, A.is_equal)
     ts(Ib, I128f, pcol, None, A.is_equal)
-    for j in range(16):
-        ts(blk("BT", j), OBb, r("EQ", j, j + 1), None, A.mult)
-    for j in range(1, 17):
+    for q in range(4):
+        sel(blk("BT", q, 512), r("ONE"), [[-1, 4], [-16, 8], [0, 16]], A.is_equal, 0.0, -4 * q, 1)
+    for j in range(1, 16):
         act(DG(j), Ib, F.Copy, scale=2.0 ** j)
-    for nm, v in (("In", -1.0), ("N10", -10.0), ("N16", -16.0), ("D60", 2.0 ** 60), ("N8k", -8192.0), ("Ifn", -1.0)):
+    for nm, v in (("In", -1.0), ("N10", -10.0), ("N16", -16.0), ("N35", -35.0), ("D60", 2.0 ** 60), ("N8k", -8192.0),
+                  ("D32", 1.0 / 32)):
         act(r(nm), Ib, F.Copy, scale=v)
-    for nm, v in (("OBf", 1.0), ("OBm", -1.0), ("c1", 12.0)):
+    for nm, v in (("OBm", -1.0), ("PKn", 12.0), ("O8k", 8192.0)):
         act(r(nm), OBb, F.Copy, scale=v)
-    sel(r("c1"), r("c1"), [[1, 128]], A.not_equal, 76.0, 0, -1)
-    cp(r("MJ"), r("c1"))
-    for nm, src, v in (("N35", Ib, -35.0), ("O2k", OBb, 2047.0), ("O8k", OBb, 8192.0)):
-        ts(r(nm), src, v, None, A.mult)
-    cp(r("o16"), r("ONE", 0, 8))
-    io(r("C3"), [[1, 16]], 0, 0)
-    cp(r("OBh"), OBb)
-    ts(r("Ihn"), Ib, -1.0, None, A.mult)
+    mm(acc(B(6, 0, 128), [(Ib, r("PKn")), (Ib, DG(6))]))
+    act(r("MJ"), B(6, 0, 128), F.Copy)
+    ts(r("O2k"), OBb, 2047.0, None, A.mult)
     ts(r("L1"), blk("BT", 0), 2080.0, None, A.mult)
     ts(r("L2"), Ib, 3232.0, None, A.mult)
     ts(r("BM"), r("I144"), g16, None, A.is_equal)
     ts(r("B0b"), r("I144"), pcol, k0, A.is_equal, A.mult)
-    cp(r("B0h"), r("B0b"))
     sel(r("c1"), OBb, [[1, 128]], A.is_gt, 0.0, 0, -1)
     sel(r("FST"), r("c1"), [[1, 128]], A.not_equal, -16.0, 0, -1)
-    act(r("c1"), r("c1"), F.Identity, bias=1.0 / 32, scale=47.0 / 32)
-    sel(r("c1"), r("c1"), [[1, 128]], A.not_equal, -1.0, 0, -1)
+    act(r("F16"), r("FST"), F.Copy, scale=65536.0)
+    act(r("K16"), Ib, F.Copy, scale=kn)
+    mm(acc(B(6, 128, 256), [(DG(1), r("c1")), (r("c1"), r("D32")), (Ib, In)]))
+    act(r("TRI"), B(6, 128, 256), F.Copy)
     act(r("PK"), r("IJ"), F.Exp, scale=-LN2, bias=-LN2)
     ops[-1]["c"] += 1300
     act(r("WF", 512, 528), r("IJ", 0, 16), F.Exp, scale=0.0, bias=kln)
-    for nm, src in (("TRI", "c1"), ("PK", "PK")):
-        sel(r(nm), r(src), [[-16, 8], [0, 16]], A.is_ge, 0.0, 0, 1)
-        sel(r(nm), r(nm), [[16, 8], [0, 16]], A.is_ge, 0.0, 15, -1)
+    tt(r("PK"), r("PK"), OBb, A.mult)
     act(r("PK32"), r("PK"), F.Copy, scale=1.0 / 32)
     act(r("PKn"), r("PK"), F.Copy, scale=-1.0)
+    act(blk("TT", 1, 256), r("RT"), F.Exp, scale=0.0, bias=kln)
     ts(r("PW2"), OBb, r("WF", 512, 513), None, A.mult)
     act(r("IL"), r("IL"), F.Identity, bias=kcol)
     ts(r("S8", p=(0, 8)), r("IG", p=(0, 8)), r("pcf", 0, 1, p=(0, 8)), None, A.is_equal)
     cp(r("thb", 0, 2, p=(0, 8)), r("ths", 0, 2, p=(0, 8)))
     mm([(B(7, 0, 2), r("S8", p=(0, 8)), r("thb", 0, 2, p=(0, 8)), True, True)])
-    act(r("XL0", 8192, 8194), B(7, 0, 2), F.Copy)
+    act(r("XL0", 8192, 8193), B(7, 0, 1), F.Copy)
+    act(r("XL0", 8193, 8194), B(7, 1, 2), F.Identity, bias=-208.0)
 
     for k, (t, lo, hi) in enumerate(SENDS):
-        op("G", 300, [r("XL0", lo, min(hi, 4096)), r("XL0", max(lo, 4096), min(hi, 8192)), r("XL0", min(hi, 8192), hi)],
+        op("G", 300, [r("XL0", 0, 4096), r("XL0", 4096, 8192), r("XL0", 8192, XW)],
            [r("XL%d" % t, lo, hi), r("ths", 4, 5)], lambda k=k: send(k))
-        ops[-1]["r"] = [x for x in ops[-1]["r"] if x[2] > x[1]]
-        ops[-1]["late"] = SEND * (hi - lo) / XW
+        ops[-1]["late"] = SEND * (hi - lo) / XW * (1 if k else 2)
 
     NW = r("NX", 0, 512)
     PUn = r("PU", 128, 160)
@@ -259,15 +260,21 @@ def build(g, T, send):
     def lists(t):
         bk = (6, 3, 7, 7)[t]
         mm([(B(bk, 0, 32), r("B0b", 15 - w, 143 - w), r("PR%d" % t, w, 512, 16), w == 0, w == 15) for w in range(16)])
+        ts(blk("PU", t, 32), B(bk, 0, 32), 256.0, None, A.add)
         act(blk("PF", t, 32), B(bk, 0, 32), F.Identity, bias=256.0)
-        cp(blk("PU", t, 32), blk("PF", t, 32))
 
     def compare(h):
         sb = 3 + 2 * h
         for n in range(8):
-            bk, eb = (n % 2, n % 2) if h == 0 else (2 + 2 * (n % 2), 2 + n % 2)
-            mm([(B(bk, 256 * i, 256 * i + 256), blk("BT", 2 * n + i), r("QN", h, 512, 2), True, True) for i in range(2)])
-            tt(blk("E", eb, 512), B(bk), blk("CE", h, 512), A.is_equal)
+            bk, eb = (0, 1, 2, 4)[n % 4], 4 * h + n % 4
+            if n in ES[h]:
+                mm([it for i in range(2) for it in acc(B(bk, 256 * i, 256 * i + 256),
+                                                       [(In, blk("CE", 2 * h, 256)), (blk("BT", 2 * n + i), r("QN", h, 512, 2))])])
+                act(B(bk), B(bk), F.Abs)
+                act(blk("E", eb, 512), B(bk), F.Relu, scale=-1.0, bias=1.0)
+            else:
+                mm([(B(bk, 256 * i, 256 * i + 256), blk("BT", 2 * n + i), r("QN", h, 512, 2), True, True) for i in range(2)])
+                tt(blk("E", eb, 512), B(bk), blk("CE", h, 512), A.is_equal)
             mm([(B(sb, 0, 256), DG(2 * n + i), blk("E", 2 * eb + i, 256), n + i == 0, n + i == 8) for i in range(2)])
         tt(blk("t5", h, 256), B(sb, 0, 256), blk("ne", h, 256), A.is_lt)
         tt(blk("WF", h, 256), B(sb, 0, 256), blk("ne", h, 256), A.mult)
@@ -281,31 +288,32 @@ def build(g, T, send):
         o = B(7, 0, 256)
         mm([(o, r("FST"), blk("t5", h, 256), True, True)])
         act(o, o, F.Relu, bias=-15.0, scale=-1.0)
-        tt(blk("f5", h, 256), o, blk("NX", h, 256), A.mult)
-        mm([(o, r("OBf"), blk("f5", h, 256), True, True)])
-        act(r("NX", XO + 256 * h, XO + 256 * h + 256), o, F.Copy)
+        tt(blk("f5", h, 256), o, blk("CE", 2 * h, 256), A.mult)
+        mm([(o, OBb, blk("f5", h, 256), True, True)])
+        act(r("NX", XO + 256 * h, XO + 256 * h + 256), o, F.Identity, scale=-1.0, bias=2047.0)
 
     def chain(t):
         par = t & 1
         PF, il = blk("PF", 2 * t + par, 16), blk("IL", par, 16)
-        x0, x1, ly, ab = [blk("tl", i, 16) for i in range(4)]
+        ly, x1, x0, ab = [blk("tl", i, 16) for i in range(4)]
         cl = blk("CL", t, 16)
         tt(ly, PF, blk("HX", par, 16), A.max)
-        cp(blk("LU", 2 * t, 16), ly)
+        if t == 0:
+            cp(blk("LU", 0, 16), ly)
         ts(x0, PF, 256.0, None, A.is_lt if par else A.is_ge)
         tt(cl, x0, blk("HL", 2 + par, 16), A.mult)
         ts(ab, cl, 0.0, None, A.is_lt)
         tt(x1, PF, il, A.subtract)
         tt(x1, x1, ab, A.mult)
         tt(x1, x1, il, A.add)
-        cp(blk("LU", 2 * t + 1, 16), x1)
+        cp(*((blk("LU", t, 32), blk("tl", 0, 32)) if t else (blk("LU", 1, 16), x1)))
         aw = "AW3" if t == 3 else "AW%d" % par
         act(blk(aw, par, 256), ind(r("NAT" if t == 3 else "IC"), blk("LU", 2 * t + 1, 16)), F.Copy)
         act(r("PN" if t == 3 else "PR%d" % (t + 1)), ind(r(aw), blk("PU", t, 32)), F.Copy)
 
     def code(t):
         ts(blk("CU", t, 16), blk("CL", t, 16), -1.0, 1.0, A.mult, A.add)
-        act(blk("CD", t, 256), ind(r("C3"), blk("CU", t, 16)), F.Copy)
+        act(blk("CD", t, 256), ind(r("IC", 256, 272), blk("CU", t, 16)), F.Copy)
 
     def parents_out():
         mm([(B(7, 0, 32), r("B0b", 15 - w, 143 - w), r("PN", 256 * (w & 1) + (w >> 1), 256 * (w & 1) + 256, 8), w == 0, w == 15)
@@ -313,20 +321,29 @@ def build(g, T, send):
         act(r("OP"), B(7, 0, 32), F.Identity, bias=256.0)
 
     def hop(t):
-        lo = 16 * t
-        a, b = r("PF", 32 * t + lo, 32 * t + 32), r("PF", 32 * t + 32 + lo, 32 * t + 64)
-        x, u = r("tl", 64 + lo, 96), r("LU", 128 + 32 * t, 160 + 16 * t)
+        if t == 0:
+            x = blk("tl", 4, 16)
+            ts(x, blk("CL", 0, 16), 1.0, 512.0, A.add, A.mult)
+            tt(x, x, blk("IL", 0, 16), A.max)
+            ts(blk("LU", 8, 16), x, 512.0, None, A.min)
+            act(blk("TT", 0, 256), ind(r("WF"), blk("LU", 8, 16)), F.Copy)
+            act(r("TH", 0, 512), ind(r("TT"), blk("PU", 0, 32)), F.Copy)
+            return
+        a, b, x = blk("PF", 3, 16), blk("PF", 5, 16), blk("tl", 5, 16)
         tt(x, a, b, A.is_equal)
         act(x, x, F.Copy, scale=512.0)
         tt(x, x, a, A.max)
-        cp(u, x)
-        act(r("TH", 512 * t, 512 + 256 * t), ind(r("WF"), u), F.Copy)
+        cp(blk("LU", 10, 16), x)
+        act(blk("TH", 2, 256), ind(r("WF"), blk("LU", 10, 16)), F.Copy)
 
     def bit(o, src):
         n = cols(o)
         return acc(o, [(r("PK32"), r("ONE", 0, n)), (r("PK"), src), (Ib, r("RT", 0, n)), (In, r("RT", 0, n)), (r("PKn"), src)])
 
     def frames():
+        mm([(B(2, 128 * k, 128 * k + 128), blk("PR1", k), OBb, True, True) for k in range(4)])
+        for par in range(2):
+            act(blk("TG", par, 512), B(2), F.Relu, scale=(1.0, -1.0)[par], bias=(8.0, -8.0)[par])
         for h in range(2):
             o = B(4 + h, 0, 256)
             mm(bit(o, blk("WF", h, 256)))
@@ -337,23 +354,21 @@ def build(g, T, send):
                 c, rt = blk("cw", 2 * h + k), r("RT", 0, 128)
                 its += acc(B(4 + h, 256 + 128 * k, 384 + 128 * k), [(ONb, r("PK32")), (c, r("PK")), (Ib, rt), (In, rt), (c, r("PKn"))])
             mm(its)
-            ts(blk("MT", h, 256), B(4 + h, 256, 512), 0.0, None, A.is_gt)
+            for par in range(2):
+                tt(blk("MT", 2 * par + h, 256), B(4 + h, 256, 512), blk("TG", 2 * par + h, 256), A.is_gt)
 
     def onehot():
         mm([(B(7, 8 * k, 8 * k + 8), blk("PR1", k), r("B0b", 15, 143, 16), True, True) for k in range(4)])
-        a, b, c, d = [blk("ti", i, 32) for i in range(4)]
+        a, b, d = [blk("ti", i, 32) for i in range(3)]
         ts(a, B(7, 0, 32), 256.0, None, A.add)
         ts(b, a, 128, None, A.bitwise_and)
-        ts(c, a, 1, 128, A.arith_shift_right, A.bitwise_and)
         ts(d, a, 127, None, A.bitwise_and)
-        tt(blk("PW", 0, 32), c, d, A.add)
+        cp(blk("PW", 0, 32), d)
         ts(blk("PW", 1, 32), b, 1023.0 / 128, 1.0, A.mult, A.add)
-
-    def hot(par):
         for q in range(8):
             for k in range(4):
                 i = 8 * k + q
-                ts(blk("OH", 2 * i + par), blk("I256", par), r("PW", i, i + 1), r("PW", 32 + i, 33 + i), A.is_equal, A.mult)
+                ts(blk("OH", i), blk("IC", 2), r("PW", i, i + 1), r("PW", 32 + i, 33 + i), A.is_equal, A.mult)
 
     def head(t):
         XL = "XL%d" % t
@@ -361,7 +376,7 @@ def build(g, T, send):
         for h in range(2):
             ts(blk("QU", h), ind(NW, r("PU", p0 + 8 * h, p0 + 8 * h + 8)), -1.0, 4095.0, A.mult, A.add)
         ts(r("YH"), ind(r("NX"), blk("LU", 2 * t, 16)), -1.0, 2047.0, A.mult, A.add)
-        mm([(B(6, 0, 16), r("B0h", 15 - w, 143 - w), r("YH", w, 256, 16), w == 0, w == 15) for w in range(16)])
+        mm([(B(6, 0, 16), r("B0b", 15 - w, 143 - w), r("YH", w, 256, 16), w == 0, w == 15) for w in range(16)])
         ts(r("YU"), B(6, 0, 16), 2048.0, None, A.add)
         ts(r("QH"), r("QU"), -2048.0, None, A.add)
         mm([(B(5, 0, 256), blk("BT", 0), r("YH"), True, True)] + acc(B(5, 256, 512), [(r("L1"), r("YH")), (r("L2"), r("QH"))]))
@@ -373,15 +388,18 @@ def build(g, T, send):
         mm([(B(6, 128 * h, 128 * h + 128), blk("XY", h), In, True, True) for h in range(2)])
         act(r("XT"), B(6, 0, 256), F.Copy)
 
-    def scores(t, lo, hi):
+    def scores(t):
         XL = "XL%d" % t
-        for n in range(lo, hi):
-            xq, bk, ad = blk("XQ", n, 512), B(n % 2), blk("AD", n % 4, 512)
+        for n in range(8):
+            xq, bk, ad = blk("XQ", n, 512), B((0, 5, 1)[n % 3]), blk("AD", n, 512)
+            rows = (32 * (n % 4), 32 * (n % 4) + 32)
             if n in VQ[t]:
                 cp(xq, ind(r(XL, 0, 4096), blk("QU", n, 32)))
-            else:
+            elif n in XM:
+                act(r("XQ", 512 * n, 512 * n + 1024), ind(r(XL, 0, 4096), r("QU", 32 * n, 32 * n + 64)), F.Copy)
+            elif n - 1 not in XM:
                 act(xq, ind(r(XL, 0, 4096), blk("QU", n, 32)), F.Copy)
-            mm(acc(bk, [(Ib, xq), (blk("XT", n // 4), blk("EX", n % 4, 512))]))
+            mm(acc(bk, [(Ib, xq), (r("XT", 128 * (n // 4), 128 * (n // 4) + 128, p=rows), r("EX", p=rows))]))
             act(ad, bk, F.Abs)
             tt(blk("CM", n, 512), ind(r(XL, 4096, 8192), blk("HU", n, 32)), ad, A.is_ge)
 
@@ -390,24 +408,28 @@ def build(g, T, send):
         ne, o = blk("ne", par, 256), B(7, 0, 256)
         if t > 1:
             act(ne, blk("NX", par, 256), F.Sign)
-        mm([(o, r("FST"), ne, True, True)])
-        act(blk("first", par, 256), o, F.Identity, bias=kn)
+        mm(acc(o, [(DG(14), r("ONE", 0, 256)), (r("N8k"), blk("CD", t, 256))]))
+        tt(blk("Nx", par, 256), o, blk("NX", par, 256), A.min)
+        count(t, 2 * par)
+        count(t, 2 * par + 1)
+
+    def count(t, k):
+        par = t & 1
+        its = [(B(1, 0, 128), r("ZR"), Ib, True, False)] if k == 2 * par else []
+        mm(its + [(B(1, 16 * q, 16 * q + 16), blk("OH", 8 * k + q), blk("MT", 32 * par + 8 * k + q, 16), False,
+                   k == 3 - 2 * par and q == 7) for q in range(8)])
 
     def masks(t):
         par = t & 1
         XL = "XL%d" % t
-        one, cd = r("ONE", 0, 256), blk("CD", t, 256)
-        W = blk("WF", par, 256)
+        cd, W = blk("CD", t, 256), blk("WF", par, 256)
         ts(r("q"), r("QU"), 4095.0, None, A.is_lt)
         act(r("Ns"), ind(NW, blk("LU", 2 * t + 1, 16)), F.Copy)
-        mm(acc(B(3, 256, 512), [(DG(14), one), (r("N8k"), cd)]))
-        tt(r("Nx"), B(3, 256, 512), blk("NX", par, 256), A.min)
-        mm([(B(3, 0, 256), r("Ihn"), r("QH"), True, True)])
-        for q in range(8):
-            mm(acc(B(7, 16 * q, 16 * q + 16), [(r("OH", 256 * (8 * k + q) + 128 * par, 256 * (8 * k + q) + 128 * par + 128),
-                                               r("MT", 128 * k + 16 * q, 128 * k + 16 * q + 16)) for k in range(4)]))
-        ts(r("ki"), B(7, 0, 128), 1024.0 * RND, -1024.0 * RND, A.add, A.add)
-        tt(blk("nh", 0), B(7, 0, 128), r("ki"), A.not_equal)
+        mm([(B(3, 0, 256), In, r("QH"), True, True)])
+        count(t, 2 - 2 * par)
+        count(t, 3 - 2 * par)
+        ts(r("ki"), B(1, 0, 128), 1024.0 * RND, -1024.0 * RND, A.add, A.add)
+        tt(blk("nh", 0), B(1, 0, 128), r("ki"), A.not_equal)
         act(blk("nh", 1), r("ki"), F.Sign)
         o = B(7, 256, 512)
         its = []
@@ -421,72 +443,81 @@ def build(g, T, send):
             ts(o, o, 0.0, None, A.is_gt)
             tt(cw, o, th, A.mult)
         mm(bit(o, cw))
-        ts(r("cb"), o, 0.0, -1.0, A.is_gt, A.mult)
+        act(r("cb"), o, F.Sign, scale=-1.0, bias=2.0 ** -18)
         o = B(4, 0, 256)
         if t == 3:
-            mm([(B(4, 128 * f, 128 * f + 128), blk("MT", 2 * par + f), Ib, True, True) for f in range(2)])
+            mm([it for f in range(2) for it in acc(B(4, 128 * f, 128 * f + 128), [(blk("MT", 2 + f), Ib), (blk("MT", 6 + f), Ib)])])
             tt(r("cw", 256, 512), o, blk("TH", 2, 256), A.mult)
             mm(bit(o, r("cw", 256, 512)))
             ts(r("b3"), o, 0.0, None, A.is_gt)
         its = []
         for f in range(2):
-            held = (r("N16"), blk("b3", f)) if t == 3 else (blk("MT", 2 * par + f), r("N16"))
+            held = (r("N16"), blk("b3", f)) if t == 3 else (blk("MT", 4 - 2 * par + f), r("N16"))
             its += acc(B(4, 128 * f, 128 * f + 128),
                        [held, (DG(4), blk("q", f)), (r("OBm"), blk("ne", 2 * par + f)), (r("N16"), blk("CD", 2 * t + f))])
         mm(its)
         act(r("pj"), o, F.Sign, bias=-0.5)
         o = B(4, 256, 512)
-        mm(acc(o, [(DG(8), cd), (DG(8), r("q")), (DG(5), r("cb"))]))
-        act(r("sc", 0, 1), r(XL, 8193, 8194), F.Identity, bias=-768.0 - 16.0)
-        act(r("thr"), o, F.Identity, bias=r("sc", 0, 1))
-        act(r("sc", 1, 2), r(XL, 8192, 8193), F.Identity, scale=-KL, bias=-16.0 * KL - 48 * LN2)
+        mm(acc(o, [(DG(6), cd), (DG(6), r("q")), (DG(4), r("cb"))]))
+        act(r("thr"), o, F.Identity, bias=r(XL, 8193, 8194))
+        th1 = r(XL, 8192, 8193)
         if t:
-            act(r("cn", 0, 2), B(2, 384, 386), F.Copy)
-            cn, rt = [r("cn", f, f + 1) for f in range(2)], r("RT", 0, 1)
-            mm(acc(B(2, 386, 387), [(Ib, r("cn", 2, 3))] + [(r("NEG", 0, 128), x) for x in cn]
-                   + [(DG(1), rt), (In, rt), (In, rt)] + [(ONb, x) for x in cn]))
-            act(r("sc", 2, 3), B(2, 386, 387), F.Identity, scale=-KL, bias=r("sc", 1, 2))
+            act(r("cn", 0, 1), B(2, 384, 385), F.Copy)
+            cn, rt = [r("cn", 0, 1)], r("RT", 0, 1)
+            mm(acc(B(2, 386, 387), [(Ib, r("cn", 2, 3))] + [(r("NEG"), x) for x in cn]
+                   + [(DG(1), rt), (In, rt), (In, rt)] + [(ONb, x) for x in cn] + [(Ib, th1)]))
+            th1 = B(2, 386, 387)
+        act(r("sc", 2, 3), th1, F.Identity, scale=-KL, bias=-32.0 * KL - 48 * LN2)
 
     def piece(t, f):
         par = t & 1
-        X, Z1, Z2 = ((2, 4, 5), (6, 0, 1))[f]
-        d = 2 * par + f
-        v, ta, tb = B(X, 0, 128), B(X, 128, 256), B(X, 256, 384)
-        wA, wB, KP, cb = [blk(n, f) for n in ("wA", "wB", "KP", "cb")]
-        HA, HB, pA, pB = blk("H", 2 * f), blk("H", 2 * f + 1), blk("p", 2 * f), blk("p", 2 * f + 1)
-        cd, first = blk("CD", 2 * t + f), blk("first", d)
-        for k in range(2):
-            o, e = B(X, 64 * k, 64 * k + 64), 1024 * (2 * f + k)
-            mm(acc(o, [(DG(4), blk("pj", 2 * f + k, 64)), (DG(5), blk("cb", 2 * f + k, 64))]
-                   + [(r("BM", 15 - j, 143 - j), r("CM", e + j, e + 1024, 16)) for j in range(16)]))
-        act(wA, v, F.Exp, scale=KL, bias=r("sc", 2, 3) if t else r("sc", 1, 2))
-        act(wB, v, F.Exp, scale=-KL, bias=48 * LN2 - 48 * KL)
-        mm([(ta, r("TRI"), wA, True, True)] + acc(tb, [(r("D60"), cd), (r("TRI"), wB)]))
-        ts(blk("H", f, 256), B(X, 128, 384), -2.0 ** -50, None, A.is_lt)
-        tt(pA, B(3, 128 * f, 128 * f + 128), HA, A.mult)
-        tt(pB, B(3, 128 * f, 128 * f + 128), HB, A.mult)
-        tt(KP, v, blk("thr", f), A.is_le)
-        z, y = B(Z1, 0, 128), B(Z2, 0, 128)
-        mm(acc(z, [(r("Ifn"), blk("Nx", f))], stop=False))
-        mm(acc(y, [(DG(12), first)], stop=False))
-        mm(acc(z, [(r("O8k"), HA), (r("O2k"), HB)], start=False, stop=False) + acc(y, [(r("O2k"), HA)], start=False, stop=False))
-        mm(acc(y, [(r("OBh"), pA)], start=False) + acc(z, [(r("OBh"), pB), (In, KP)], start=False))
-        act(blk("AB", f), z, F.Abs, scale=4096.0)
-        tt(y, y, blk("Ns", f), A.max)
+        lo, hi = (0, CUT) if f == 0 else (CUT, 256)
+        n, d = hi - lo, 256 * par
+        v, ta, tb, z, y = [B(k, c, c + n) for k, c in (((2, 0), (2, 192), (5, 256), (4, 0), (5, 0)),
+                                                       ((6, 0), (6, 128), (6, 256), (0, 0), (6, 384)))[f]]
+        wA, wB, KP, cb, HA, HB, pA, pB, AB = [r(x, lo, hi) for x in ("wA", "wB", "KP", "cb", "HA", "HB", "pA", "pB", "AB")]
+        cd, Q = r("CD", 256 * t + lo, 256 * t + hi), B(3, lo, hi)
+        sums = [acc(r(v[0], 64 * k - lo, 64 * k + 64 - lo), [(r("BM", 15 - j, 143 - j), r("CM", 1024 * k + j, 1024 * k + 1024, 16))
+                                                             for j in range(16)], False, f == 1 and k == 3)
+                for k in range(lo // 64, hi // 64)]
+        sums.insert(len(sums) - f, [(v, DG(4), cb, False, f == 0)])
+        mm([(v, DG(4), r("pj", lo, hi), True, False)])
+        for its in sums:
+            mm(its)
+        act(wA, v, F.Exp, scale=KL, bias=r("sc", 2, 3))
+        act(wB, v, F.Exp, scale=-KL, bias=48 * LN2 - 32 * KL)
+        tt(KP, v, r("thr", lo, hi), A.is_le)
+        mm([(ta, r("TRI"), wA, True, True)])
+        mm(acc(tb, [(r("D60"), cd), (r("TRI"), wB)]))
+        ts(HA, ta, -2.0 ** -50, None, A.is_lt)
+        tt(pA, Q, HA, A.mult)
+        ts(HB, tb, -2.0 ** -50, None, A.is_lt)
+        tt(pB, Q, HB, A.mult)
+        mm(acc(y, [(r("F16"), r("ne", d + lo, d + hi)), (r("K16"), r("ONE", 0, n)), (r("O2k"), HA), (OBb, pA)]))
+        mm(acc(z, [(In, KP), (r("O8k"), HA), (r("O2k"), HB)], stop=False))
+        mm(acc(z, [(OBb, pB)], start=False))
+        tt(AB, y, r("Ns", lo, hi), A.max)
+        tt(z, z, r("Nx", d + lo, d + hi), A.not_equal)
         if t < 3:
-            tt(blk("NX", d), y, blk("AB", f), A.min)
-            o = B(7, 128 * f, 128 * f + 128)
-            mm(acc(o, [(DG(6), blk("MT", d)), (cb, DG(4)), (cd, r("N16"))] + ([(blk("CD", f), r("N10"))] if t == 2 else [])
-                   + [(KP, DG(7)), (HA, r("MJ")), (HB, r("N35"))]))
-            ts(blk("MT", d), o, 14.0 if t == 2 else 24.0, None, A.is_gt)
-            mm([(B(2, 384 + f, 385 + f), HA, r("o16", 0, 1), True, True)])
+            tt(r("NX", d + lo, d + hi), z, AB, A.mult)
         else:
-            tt(y, y, blk("AB", f), A.min)
-            ts(r("OC", 256 * f + 1, 256 * f + 256, 2), y, -1.0, 4095.0, A.mult, A.add)
-        if t < 2:
-            o = B(Z2, 128, 256)
-            mm(acc(o, [(DG(16), first), (r("PW2"), HA)]))
-            tt(blk("WF", d), o, blk("WF", d), A.max)
+            tt(z, z, AB, A.mult)
+            act(r("OC", 2 * lo + 1, 2 * hi, 2), z, F.Identity, scale=-1.0, bias=4095.0)
+
+    def after(t):
+        par = t & 1
+        for f in range(2):
+            mm(acc(B(7, 128 * f, 128 * f + 128),
+                   [(DG(6), blk("MT", 4 - 2 * par + f)), (blk("cb", f), DG(3)), (blk("CD", 2 * t + f), r("N16"))]
+                   + ([(blk("CD", f), r("N10"))] if t == 2 else [])
+                   + [(blk("KP", f), DG(7)), (blk("HA", f), r("MJ")), (blk("HB", f), r("N35"))]))
+        ts(blk("MT", 2 - par, 256), B(7, 0, 256), 22.0 if t == 2 else 32.0, None, A.is_gt)
+        mm(acc(B(2, 384, 385), [(blk("HA", f), r("ONE", 0, 1)) for f in range(2)]))
+
+    def weights(t):
+        o = B(7, 256, 512)
+        mm(acc(o, [(r("F16"), blk("ne", t, 256)), (r("K16"), r("ONE", 0, 256)), (r("PW2"), r("HA"))]))
+        tt(blk("WF", t, 256), o, blk("WF", t, 256), A.max)
 
     lists(0)
     compare(0)
@@ -496,23 +527,22 @@ def build(g, T, send):
     head(0)
     lists(1)
     onehot()
-    hot(0)
     tops(1)
     hop(0)
     frames()
     code(0)
     early(0)
     for t in range(4):
+        if t == 3:
+            parents_out()
         if t > 0:
             head(t)
         masks(t)
-        scores(t, 0, 8)
-        if t == 0:
-            hot(1)
+        scores(t)
+        if t in (1, 2):
+            weights(t - 1)
         if t == 2:
             hop(1)
-        if t == 3:
-            parents_out()
         if t < 3:
             if t:
                 lists(t + 1)
@@ -521,14 +551,17 @@ def build(g, T, send):
             early(t + 1)
         piece(t, 0)
         piece(t, 1)
+        if t < 3:
+            after(t)
         if t == 2:
             act(r("OC", 0, 512, 2), blk("NX", 0, 256), F.Identity, bias=4095.0, scale=-1.0)
     return ops
 
 
-EXT = {"dcq": 2600, "dpt": 2300, "dth": 2400, "dxs": 7000, "dlim": 11000}
-SEND = 16000.0
-SENDS = ((1, 0, 4096), (1, 4096, XW), (2, 0, 4096), (2, 4096, XW), (3, 0, 4096), (3, 4096, XW))
+EXT = {"dcq": 2600, "dpt": 2300, "dth": 2400, "dxs": 10500, "dlim": 13000}
+SEND = 13000.0
+PARTS = ((0, 4096), (4096, XW))
+SENDS = [(t, lo, hi) for t in (1, 2, 3) for lo, hi in PARTS]
 
 
 def outside(x):
@@ -559,7 +592,7 @@ def schedule(ops):
                     d.add(j)
         for x, w in use:
             seen.setdefault(x[0], []).append((i, x, w))
-        if "late" in o and d:
+        if "late" in o:
             d.update(j for j in range(i) if ops[j]["e"] == "G")
         d.discard(i)
         keep, cover = [], 0
@@ -574,12 +607,20 @@ def schedule(ops):
         for d in deps[i]:
             succ[d].append(i)
     start = arrange(ops, deps, succ)
+    second = [i for i in range(n) if "late" in ops[i]][1]
+    for i in range(n):
+        if ops[i]["e"] == "G" and ops[i]["w"][0][0] in ("NAT", "AW1", "AW3"):
+            start[i] = min([start[second] + 1.0] + [start[s] - 1.0 for s in succ[i] if "late" not in ops[s]])
     return sorted(range(n), key=lambda i: (start[i], i)), deps, start
 
 
 CACHE = {}
 LAT = 200.0
-ROUNDS = 6000
+CASES = ((1.56, 220.0, 1.0), (1.25, 170.0, 1.1), (1.95, 190.0, 1.0))
+ROUNDS = 9500
+MIX = 500
+STEPS = 1000
+HEAT = 150.0
 
 
 def place(seq, pre, eng, cost, rel):
@@ -608,24 +649,29 @@ def place(seq, pre, eng, cost, rel):
 
 def arrange(ops, deps, succ):
     n = len(ops)
-    eng, cost = [o["e"] for o in ops], [o["c"] for o in ops]
+    eng = [o["e"] for o in ops]
+    num = ["VSPG".index(e) for e in eng]
     rel = [max([EXT.get(outside(x), 0.0) for x in o["r"]] + [0.0]) for o in ops]
 
-    def gap(a, b):
-        return ops[a].get("late", 0.0) + (0.0 if eng[a] == eng[b] == "P" else (0.5 * LAT if eng[a] == eng[b] else LAT))
-    fore = [[(d, cost[d] + gap(d, i)) for d in deps[i]] for i in range(n)]
-    aft = [[(s, cost[s] + gap(i, s)) for s in succ[i]] for i in range(n)]
+    def gap(a, b, lat):
+        return ops[a].get("late", 0.0) + (0.0 if eng[a] == eng[b] == "P" else (0.5 * lat if eng[a] == eng[b] else lat))
+    cases = []
+    for ga, lat, pe in CASES:
+        cost = [(o["c"] + o["g"] * (ga - GA)) * (pe if o["e"] == "P" else 1.0) for o in ops]
+        cases.append(([[(d, cost[d] + gap(d, i, lat)) for d in deps[i]] for i in range(n)], num, cost, rel))
+    fore, cost = cases[0][0], cases[0][2]
+    aft = [[(s, cost[s] + gap(i, s, CASES[0][1])) for s in succ[i]] for i in range(n)]
     way = [0.0] * n
     for i in range(n - 1, -1, -1):
-        way[i] = cost[i] + max([way[s] + gap(i, s) for s in succ[i]] + [0.0])
-    best, span, rnd = None, 1e18, 12345
+        way[i] = cost[i] + max([way[s] + gap(i, s, CASES[0][1]) for s in succ[i]] + [0.0])
+    best, total, rnd = None, 1e18, 12345
     for k in range(ROUNDS):
         if best is None:
             seq = sorted(range(n), key=lambda i: (-way[i], i))
         else:
             key = list(best)
             rnd = (rnd * 1103515245 + 12345) % 2147483648
-            t0, amp = rnd / 2147483648.0 * span, (500.0, 1500.0, 4000.0)[k % 3]
+            t0, amp = rnd / 2147483648.0 * max(best), (500.0, 1500.0, 4000.0)[k % 3]
             for i in range(n):
                 if abs(best[i] - t0) < 7000:
                     rnd = (rnd * 1103515245 + 12345) % 2147483648
@@ -637,21 +683,141 @@ def arrange(ops, deps, succ):
         for _r in range(6 if best is None else 1):
             back = place(sorted(range(n), key=lambda i: (-st[i] - cost[i], -i)), aft, eng, cost, [0.0] * n)
             st = place(sorted(range(n), key=lambda i: (-back[i] - cost[i], i)), fore, eng, cost, rel)
-            sp = max(st[i] + cost[i] for i in range(n))
-            if sp <= span:
-                best, span = st, sp
+            seq = sorted(range(n), key=lambda i: (st[i], i))
+            sp = worth([run(seq, 0, st, st, *c) for c in cases])
+            if sp <= total:
+                best, total = st, sp
+        if k % MIX == MIX - 1:
+            best, total = anneal(best, aft, cases)
     return best
+
+
+def run(seq, a, st, by, fore, eng, cost, rel):
+    free, last = [0.0] * 4, [-1] * 4
+    p = a - 1
+    while p >= 0 and min(last) < 0:
+        i = seq[p]
+        if last[eng[i]] < 0:
+            last[eng[i]], free[eng[i]] = i, st[i] + cost[i]
+        p -= 1
+    st, by = list(st), list(by)
+    for i in seq[a:]:
+        e, t, b = eng[i], rel[i], -1
+        for d, w in fore[i]:
+            if st[d] + w > t:
+                t, b = st[d] + w, d
+        if free[e] > t:
+            t, b = free[e], -2 - last[e]
+        st[i], by[i] = t, b
+        free[e], last[e] = t + cost[i], i
+    e = free.index(max(free[:3]))
+    return free[e], st, by, last[e]
+
+
+def worth(runs):
+    return sum(x[0] + 1.5 * sum(x[1]) / len(x[1]) for x in runs)
+
+
+def anneal(st, aft, cases):
+    n = len(st)
+    fore, eng = cases[0][:2]
+    rnd = int(sum(st)) % 99991
+    for part in range(6):
+        seq = sorted(range(n), key=lambda i: (st[i], i))
+        now = [run(seq, 0, st, st, *c) for c in cases]
+        best, keep = worth(now), now[0][1]
+        end = best
+        for k in range(STEPS):
+            span, at, by, j = now[k % len(now)]
+            lo, hi = (part - 0.3) * span / 6, (part + 1.3) * span / 6
+            pairs = []
+            while j >= 0 and at[j] >= lo:
+                b = by[j]
+                if b <= -2:
+                    b = -2 - b
+                    if at[j] < hi:
+                        pairs.append((b, j))
+                j = b
+            if not pairs:
+                continue
+            rnd = (rnd * 1103515245 + 12345) % 2147483648
+            u, v = pairs[(rnd >> 8) % len(pairs)]
+            a, b = seq.index(u), seq.index(v)
+            rnd = (rnd * 1103515245 + 12345) % 2147483648
+            far = (0, 0, 1, 2, 4)[(rnd >> 8) % 5]
+            if rnd >> 20 & 1:
+                while far and a > 0:
+                    a -= 1
+                    far -= eng[seq[a]] == eng[v]
+                go = {v}
+                for x in reversed(seq[a:b]):
+                    if any(s in go for s, w in aft[x]):
+                        go.add(x)
+                new = seq[:a] + [x for x in seq[a:b + 1] if x in go] + [x for x in seq[a:b + 1] if x not in go] + seq[b + 1:]
+            else:
+                while far and b < n - 1:
+                    b += 1
+                    far -= eng[seq[b]] == eng[u]
+                go = {u}
+                for x in seq[a + 1:b + 1]:
+                    if any(s in go for s, w in fore[x]):
+                        go.add(x)
+                new = seq[:a] + [x for x in seq[a:b + 1] if x not in go] + [x for x in seq[a:b + 1] if x in go] + seq[b + 1:]
+            then = [run(new, a, x[1], x[2], *c) for x, c in zip(now, cases)]
+            e2 = worth(then)
+            rnd = (rnd * 1103515245 + 12345) % 2147483648
+            if e2 <= end or (rnd >> 8) / 8388608.0 < math.exp((end - e2) / (HEAT * (1.0 - k / STEPS) + 1.0)):
+                end, now, seq = e2, then, new
+                if end < best:
+                    best, keep = end, now[0][1]
+        st = keep
+    return st, best
+
+
+def routes(T, topo):
+    n = len(T.cores)
+    free = [c for c in topo.cores_of(T.cores[0]) if c not in T.cores]
+    plan = {}
+    for a, src in enumerate(T.cores):
+        need = [(T.cores[(a - t) % n], t) for t in range(1, n)]
+        far = [x for x in need if topo.die(x[0]) != topo.die(src)]
+        help_ = [c for c in free if len(far) > 1 and c not in plan and topo.die(c) == topo.die(far[0][0])]
+        plan[src] = need
+        if help_:
+            plan[help_[0]] = far
+            plan[src] = [(help_[0], 0) if x == far[0] else x for x in need if x not in far[1:]]
+    return plan
 
 
 def rank_program(g, core, T, topo):
     rank = T.rank_of(core)
-    if rank is None:
-        return
     n = len(T.cores)
     sem = T.sem
+    plan = routes(T, topo)
+
+    def write(dst, t, lo, hi):
+        rid, pid, _ = topo.addr(dst)
+        g.remote_dma(T["XL%d" % t][:, lo:hi], T.XL0[:, lo:hi], sem["arr%d%s" % (max(t, 1), "ab"[lo > 0])], sem.sent, pid, rid,
+                     topo.mask(core, dst))
+        return len(topo.engines(core, dst))
+
+    if rank is None:
+        gone = 0
+        for k, (dst, t) in enumerate(plan.get(core, [])):
+            if k:
+                g.wait_ge(sem.sent, gone)
+            for lo, hi in PARTS:
+                if k == 0:
+                    src = [c for c in T.cores if (core, 0) in plan[c]][0]
+                    g.wait_ge(sem["arr1" + "ab"[lo > 0]], len(topo.engines(src, core)))
+                gone += write(dst, t, lo, hi)
+        if gone:
+            g.wait_ge(sem.sent, gone)
+        return
     g.sync.dma_start(T.cqs[:], T.cq[:]).then_inc(sem.dcq, 16)
     g.scalar.dma_start(T.pts[:], T.pt[:]).then_inc(sem.dpt, 16)
     g.scalar.dma_start(T.ths[0:8, 0:2], T.th[:]).then_inc(sem.dth, 16)
+    g.sync.wait_ge(sem.dcq, 16)
     g.sync.dma_start(T.XL0[:, 0:4096], T.xs[:]).then_inc(sem.dxs, 16)
     g.sync.dma_start(T.XL0[:, 4096:8192], T.lim[:]).then_inc(sem.dlim, 16)
 
@@ -659,13 +825,10 @@ def rank_program(g, core, T, topo):
 
     def send(k):
         t, lo, hi = SENDS[k]
-        if k:
-            g.wait_ge(sem.sent, left[0])
-        dst = T.cores[(rank - t) % n]
-        rid, pid, _ = topo.addr(dst)
-        x = r("XL%d" % t, lo, hi)
-        g.remote_dma(T[x[0]][:, lo:hi], T.XL0[:, lo:hi], sem[outside(x)], sem.sent, pid, rid, topo.mask(core, dst))
-        left[0] += len(topo.engines(core, dst))
+        if t <= len(plan[core]):
+            if k and lo == 0:
+                g.wait_ge(sem.sent, left[0])
+            left[0] += write(*plan[core][t - 1], lo, hi)
 
     ops = build(g, T, send)
     if "plan" not in CACHE:
@@ -675,7 +838,8 @@ def rank_program(g, core, T, topo):
     SM = {"V": sem.sV, "S": sem.sS, "P": sem.sP, "G": sem.sG}
     arrive = {}
     for t in range(1, n):
-        arrive["arr%da" % t] = arrive["arr%db" % t] = len(topo.engines(T.cores[(rank + t) % n], core))
+        src = [c for c in plan if (core, t) in plan[c]][0]
+        arrive["arr%da" % t] = arrive["arr%db" % t] = len(topo.engines(src, core))
     count = {"V": 0, "S": 0, "P": 0, "G": 0}
     mark = {}
     wrote = []
@@ -708,7 +872,7 @@ def rank_program(g, core, T, topo):
         need = {}
         for d in deps[i]:
             de = ops[d]["e"]
-            if "late" in ops[d] or de == "P" and e == "P":
+            if "late" in ops[d] or de == "P" and e == "P" or de == "G" and "late" in o:
                 continue
             need[de] = max(need.get(de, 0), mark[d])
         for de in sorted(need, key=lambda x: x == e):
@@ -721,15 +885,15 @@ def rank_program(g, core, T, topo):
         mark[i] = count[e]
         after[(e, count[e])] = dict(known[e])
         for x in o["w"]:
-            if x[0] in ("OP", "OC", "XL0"):
+            if x[0] in ("OP", "OC"):
                 wrote.append((x, e, count[e]))
 
     g.wait_ge(sem.sent, left[0])
     ready(g.sync, r("OP"))
     g.sync.dma_start(T.yp[:], T.OP[:]).then_inc(sem.dout, 16)
-    for f in range(2):
-        ready(g.sync, r("OC", 256 * f, 256 * f + 256))
-        g.sync.dma_start(T.yc[:, 256 * f:256 * f + 256], T.OC[:, 256 * f:256 * f + 256]).then_inc(sem.dout, 16)
+    for q, lo, hi in ((g.sync, 0, 2 * CUT), (g.scalar, 2 * CUT, 512)):
+        ready(q, r("OC", lo, hi))
+        q.dma_start(T.yc[:, lo:hi], T.OC[:, lo:hi]).then_inc(sem.dout, 16)
     g.sync.wait_ge(sem.dout, 48)
     for e in count:
         g.sync.wait_ge(SM[e], count[e])

@@ -18,32 +18,30 @@ def _sb(name, cols, dtype):
 
 for _i in range(4):
     _sb("XL%d" % _i, XW, "bfloat16")
-    _sb("PR%d" % _i, 512, "bfloat16")
+_sb("PR1", 512, "bfloat16")
 for _i in range(8):
     SCRATCH["B%d" % _i] = ("psum", [128, 512], "float32")
 for _n, _c, _d in [
     ("cqs", 512, "int32"), ("pts", 32, "int32"), ("ths", 8, "int32"), ("thb", 8, "bfloat16"),
-    ("LU", 192, "uint16"), ("PU", 160, "uint16"), ("PF", 128, "float32"), ("PW", 64, "bfloat16"),
-    ("NX", 1024, "float32"), ("WF", 528, "bfloat16"), ("TH", 768, "bfloat16"), ("TT", 512, "bfloat16"),
-    ("IC", 512, "bfloat16"), ("NAT", 512, "bfloat16"), ("PERM", 512, "bfloat16"),
+    ("LU", 256, "uint16"), ("PU", 128, "uint16"), ("PF", 128, "float32"), ("PW", 64, "bfloat16"),
+    ("NX", 1024, "float32"), ("WF", 528, "bfloat16"), ("TH", 768, "bfloat16"), ("PL", 64, "float16"),
+    ("IC", 512, "bfloat16"), ("NAT", 512, "bfloat16"), ("Z", 272, "bfloat16"), ("T5", 16, "bfloat16"),
     ("AW0", 512, "bfloat16"), ("AW1", 512, "bfloat16"), ("AW3", 512, "bfloat16"),
-    ("pci", 8, "int32"), ("pcf", 16, "float32"), ("IG", 128, "float32"), ("IJ", 128, "float32"),
-    ("I144", 144, "float32"), ("IL", 32, "float32"),
-    ("B0b", 144, "bfloat16"), ("CE", 1024, "float16"), ("HX", 32, "float32"),
-    ("OBb", 128, "bfloat16"),
+    ("pci", 8, "int32"), ("pcf", 16, "float32"), ("IG", 128, "float32"),
+    ("I144", 144, "float32"), ("IL", 64, "float32"),
+    ("B0b", 144, "bfloat16"), ("CE", 1024, "float16"), ("HX", 32, "float32"), ("OBb", 128, "bfloat16"),
     ("ONE", 512, "bfloat16"), ("NEG", 128, "bfloat16"), ("RT", 256, "bfloat16"), ("ZR", 128, "bfloat16"),
-    ("In", 128, "bfloat16"), ("DG", 17 * 128, "bfloat16"),
-    ("N35", 128, "bfloat16"), ("N10", 128, "bfloat16"), ("N16", 128, "bfloat16"), ("D60", 128, "bfloat16"),
-    ("N8k", 128, "bfloat16"), ("MJ", 128, "bfloat16"), ("O2k", 128, "float16"), ("OBm", 128, "bfloat16"),
-    ("O8k", 128, "bfloat16"), ("PW2", 128, "bfloat16"), ("D32", 128, "bfloat16"), ("CU", 64, "uint16"),
+    ("In", 128, "bfloat16"), ("DG", 16 * 128, "bfloat16"), ("N16", 128, "bfloat16"), ("N8", 128, "bfloat16"), ("sT", 128, "bfloat16"),
+    ("O8k", 128, "bfloat16"), ("O2k", 128, "float16"), ("OBm", 128, "bfloat16"), ("PW2", 128, "bfloat16"),
+    ("D25", 128, "bfloat16"), ("N35", 128, "bfloat16"), ("MJ", 128, "bfloat16"),
     ("L1", 128, "float16"), ("L2", 128, "float16"), ("BT", 2048, "bfloat16"), ("BM", 144, "bfloat16"),
     ("EX", 512, "bfloat16"), ("FST", 128, "bfloat16"), ("TRI", 128, "bfloat16"),
     ("PK", 128, "bfloat16"), ("PKn", 128, "bfloat16"), ("PK32", 128, "bfloat16"), ("c1", 128, "bfloat16"),
-    ("S8", 128, "bfloat16"), ("QN", 512, "float16"), ("E", 4096, "bfloat16"),
+    ("S8", 128, "bfloat16"), ("QN", 256, "float16"), ("E", 4096, "bfloat16"),
     ("ne", 512, "bfloat16"), ("t5", 512, "bfloat16"), ("f5", 512, "float16"),
-    ("HL", 64, "float32"), ("tl", 192, "float32"), ("ti", 128, "int32"), ("PN", 512, "bfloat16"),
-    ("CL", 64, "float16"), ("CD", 1024, "bfloat16"), ("F16", 128, "bfloat16"), ("K16", 128, "bfloat16"),
-    ("QU", 256, "uint16"), ("QH", 256, "float16"), ("YH", 256, "float16"), ("YU", 16, "uint16"),
+    ("HL", 64, "float32"), ("tl", 64, "int32"), ("tf", 32, "float32"), ("ti", 128, "int32"), ("PN", 512, "bfloat16"),
+    ("CD", 1024, "bfloat16"), ("F16", 128, "bfloat16"), ("K16", 128, "bfloat16"),
+    ("QU", 256, "uint16"), ("QH", 256, "float16"), ("YH", 768, "float16"), ("YU", 16, "uint16"),
     ("XY", 256, "bfloat16"), ("XT", 256, "bfloat16"), ("hm", 256, "float32"), ("hi", 256, "int32"),
     ("HU", 256, "uint16"), ("XQ", 4096, "bfloat16"), ("AD", 4096, "float32"), ("CM", 4096, "bfloat16"),
     ("Ns", 256, "float32"), ("Nx", 512, "float32"), ("thr", 256, "float32"),
@@ -62,10 +60,12 @@ SEMAPHORES = ["sV", "sS", "sP", "sG", "dcq", "dpt", "dth", "dxs", "dlim", "dout"
 CY = 0.83
 PCY = 0.42
 GA = 1.56
-ES = ((), ())
-CUT = 192
-VQ = ((), (1, 3), (1, 3), (1, 3))
-XM = (6,)
+TWO = ((0, 192, (2, 0), (1, 0), (1, 256), (4, 0), (4, 256)), (192, 256, (6, 0), (5, 0), (5, 128), (0, 0), (0, 128)))
+THREE = ((0, 128, (2, 0), (4, 0), (4, 128), (4, 256), (4, 384)), (128, 192, (6, 0), (1, 0), (1, 128), (1, 256), (1, 384)),
+         (192, 256, (7, 0), (5, 0), (5, 128), (0, 0), (0, 128)))
+PIECES = (TWO, TWO, TWO, THREE)
+XM = (2, 4, 6)
+CJ = (0,)
 
 
 def r(name, lo=0, hi=None, st=1, p=None):
@@ -135,6 +135,26 @@ def build(g, T, send):
         op("S", 65 + max(64.0, cols(out) * (GA if in_[5] else 1)) * CY, [in_, bias, scale], [out],
            lambda: S.activation(ap(out), ap(in_), func, **{k: ap(v) for k, v in kw.items()}))
 
+    def either(first="V"):
+        s, v = ops.pop(), ops.pop()
+        a, b = (v, s) if first == "V" else (s, v)
+        a["alt"] = (b["e"], b["c"], b["f"])
+        ops.append(a)
+
+    def aff(out, in_, scale=None, bias=None, relu=False, first="S"):
+        steps = [x for x in ((scale, A.mult), (bias, A.add), (0.0 if relu else None, A.max)) if x[0] is not None]
+        if steps:
+            ts(out, in_, steps[0][0], steps[1][0] if steps[1:] else None, steps[0][1], steps[1][1] if steps[1:] else None)
+        else:
+            cp(out, in_)
+        act(out, in_, F.Relu if relu else (F.Copy if bias is None else F.Identity), bias, scale)
+        either(first)
+
+    def pos(out, in_):
+        ts(out, in_, 0.0, None, A.is_gt)
+        act(out, in_, F.Sign)
+        either("S")
+
     def mm(items):
         c = 40 + sum(max(64, cols(it[2])) * (1 if narrow(it[2]) else 4) for it in items) * PCY
 
@@ -144,6 +164,7 @@ def build(g, T, send):
                 last = P.matmul(ap(it[0]), ap(it[1]), ap(it[2]), it[3], it[4])
             return last
         op("P", c, [it[1] for it in items] + [it[2] for it in items], [it[0] for it in items], fn)
+        ops[-1]["s"] = (items[0][0][0], items[0][3], items[-1][4])
 
     def acc(out, terms, start=True, stop=True):
         return [(out, a, b, start and i == 0, stop and i == len(terms) - 1) for i, (a, b) in enumerate(terms)]
@@ -157,6 +178,9 @@ def build(g, T, send):
     def sel(out, in_, pat, cmp, fill, base, ch):
         op("G", 170 + 2 * cols(out) * CY, [in_], [out], lambda: g.affine_select(ap(out), ap(in_), pat, cmp, fill, base, ch))
 
+    def diag(name, v, off="ZR"):
+        sel(r(name), r(off), [[1, 128]], A.not_equal, v, 0, -1)
+
     def B(k, lo=0, hi=512, st=1):
         return r("B%d" % k, lo, hi, st)
 
@@ -166,329 +190,330 @@ def build(g, T, send):
     def DG(j):
         return blk("DG", j)
 
-    pcol, gcol, kcol, g16, k1, k0, kln, kn = [r("pcf", i, i + 1) for i in range(8)]
+    pcol, gcol, kcol, p32, g16, k0, kln, kn, kz, kh = [r("pcf", i, i + 1) for i in range(10)]
     Ib, In, OBb, ONb = DG(0), r("In"), r("OBb"), r("ONE", 0, 128)
 
     io(r("pci", 0, 1), [[0, 1]], 0, 1, False)
     io(r("IG"), [[1, 8], [0, 16]], 0, 0)
     io(r("I144"), [[1, 144]], -15, 0)
-    io(r("IJ"), [[0, 8], [1, 16]], 0, 0)
-    io(r("PERM"), [[1, 256], [256, 2]], -256, 0)
-    io(r("IC"), [[1, 512]], -256, 0)
-    io(r("IL"), [[16, 32]], 0, 0)
-    io(r("NAT"), [[1, 2], [2, 256]], -256, 0)
+    io(r("IC", 0, 272), [[1, 272]], -256, 0)
+    io(r("IC", 272, 512), [[1, 240]], 16, 0)
+    io(r("IL"), [[XO, 2], [16, 32]], 0, 0)
     io(blk("AW0", 1, 256), [[1, 256]], 0, 0)
-    io(blk("AW1", 0, 256), [[1, 256]], -256, 0)
-    io(blk("AW3", 0, 256), [[2, 256]], -256, 0)
     io(blk("NX", 3, 256), [[0, 256]], 0, 0)
+    io(r("T5", 0, 3), [[4, 3]], 0, 0)
+    io(r("T5", 3, 16), [[-4, 13]], 4, 0)
     ms(r("XL0", 8192, XW), 0.0)
     ms(r("ONE"), 1.0)
     ms(r("NEG"), -1.0)
     ms(r("RT"), RND)
-    act(r("ZR"), r("RT", 0, 128), F.Copy, scale=0.0)
-    ms(r("cn", 2, 3), 0.5)
+    ms(r("ZR"), 0.0)
+    ms(r("cn", 2, 3), 0.25)
     io(r("EX"), [[1, 32], [0, 16]], 0, 0)
     ts(r("pci", 1, 2), r("pci", 0, 1), 4, None, A.arith_shift_right)
     ts(r("pci", 2, 3), r("pci", 0, 1), 15, None, A.bitwise_and)
-    cp(r("pcf", 0, 3), r("pci", 0, 3))
     ts(r("pci", 3, 4), r("pci", 0, 1), 31, None, A.bitwise_and)
-    cp(r("pcf", 8, 9), r("pci", 3, 4))
-    ts(r("EX"), r("EX"), r("pcf", 8, 9), None, A.is_equal)
-    act(g16, gcol, F.Copy, scale=16.0)
-    act(k1, kcol, F.Identity, scale=-1.0, bias=1.0)
-    act(k0, k1, F.Relu)
-    act(kn, kcol, F.Copy, scale=-65536.0)
-    act(kln, kcol, F.Copy, scale=LN2)
-    I128f = r("I144", 15, 143)
+    cp(r("pcf", 0, 4), r("pci", 0, 4))
+    ts(r("EX"), r("EX"), p32, None, A.is_equal)
+    aff(g16, gcol, 16.0)
+    act(k0, kcol, F.Relu, scale=-1.0, bias=1.0)
+    aff(kn, kcol, -65536.0)
+    aff(kln, kcol, LN2)
+    ts(kz, pcol, g16, -240.0, A.add, A.add)
     ts(OBb, r("IG"), gcol, None, A.is_equal)
-    ts(Ib, I128f, pcol, None, A.is_equal)
+    ts(Ib, r("I144", 15, 143), pcol, None, A.is_equal)
     for q in range(4):
         sel(blk("BT", q, 512), r("ONE"), [[-1, 4], [-16, 8], [0, 16]], A.is_equal, 0.0, -4 * q, 1)
-    for j in range(1, 16):
-        act(DG(j), Ib, F.Copy, scale=2.0 ** j)
-    for nm, v in (("In", -1.0), ("N10", -10.0), ("N16", -16.0), ("N35", -35.0), ("D60", 2.0 ** 60), ("N8k", -8192.0),
-                  ("D32", 1.0 / 32)):
-        act(r(nm), Ib, F.Copy, scale=v)
-    for nm, v in (("OBm", -1.0), ("PKn", 12.0), ("O8k", 8192.0)):
-        act(r(nm), OBb, F.Copy, scale=v)
-    mm(acc(B(6, 0, 128), [(Ib, r("PKn")), (Ib, DG(6))]))
-    act(r("MJ"), B(6, 0, 128), F.Copy)
-    ts(r("O2k"), OBb, 2047.0, None, A.mult)
-    ts(r("L1"), blk("BT", 0), 2080.0, None, A.mult)
-    ts(r("L2"), Ib, 3232.0, None, A.mult)
+    for j in (1, 2, 4, 8):
+        aff(r("DG", 128 * j, 256 * j), r("DG", 0, 128 * j), 2.0 ** j)
+    for nm, v in (("In", -1.0), ("K16", kn), ("L2", 3232.0)):
+        aff(r(nm), Ib, v)
+    diag("N16", -16.0)
+    diag("N8", -8.0)
+    for nm, v in (("OBm", -1.0), ("O2k", 2047.0), ("O8k", 8192.0), ("MJ", 12.0)):
+        aff(r(nm), OBb, v)
+    aff(r("L1"), blk("BT", 0), 2080.0)
     ts(r("BM"), r("I144"), g16, None, A.is_equal)
     ts(r("B0b"), r("I144"), pcol, k0, A.is_equal, A.mult)
+    for v in range(2):
+        ts(blk("Z", v, 136), r("IC", v, 272, 2), kz, None, A.is_equal)
     sel(r("c1"), OBb, [[1, 128]], A.is_gt, 0.0, 0, -1)
-    sel(r("FST"), r("c1"), [[1, 128]], A.not_equal, -16.0, 0, -1)
-    act(r("F16"), r("FST"), F.Copy, scale=65536.0)
-    act(r("K16"), Ib, F.Copy, scale=kn)
-    mm(acc(B(6, 128, 256), [(DG(1), r("c1")), (r("c1"), r("D32")), (Ib, In)]))
-    act(r("TRI"), B(6, 128, 256), F.Copy)
-    act(r("PK"), r("IJ"), F.Exp, scale=-LN2, bias=-LN2)
+    diag("FST", -16.0, "c1")
+    aff(r("F16"), r("FST"), 65536.0)
+    mm(acc(B(5, 128, 256), [(DG(6), r("c1")), (r("c1"), Ib), (DG(1), r("N16"))]))
+    aff(r("TRI"), B(5, 128, 256), 1.0 / 32)
+    act(r("WF", 512, 528), r("ZR", 0, 16), F.Exp, bias=kln)
     ops[-1]["c"] += 1300
-    act(r("WF", 512, 528), r("IJ", 0, 16), F.Exp, scale=0.0, bias=kln)
-    tt(r("PK"), r("PK"), OBb, A.mult)
-    act(r("PK32"), r("PK"), F.Copy, scale=1.0 / 32)
-    act(r("PKn"), r("PK"), F.Copy, scale=-1.0)
-    act(blk("TT", 1, 256), r("RT"), F.Exp, scale=0.0, bias=kln)
+    act(kh, kln, F.Exp, scale=-1.0, bias=-LN2)
+    ops[-1]["r"].append(r("WF", 512, 528))
+    aff(r("PKn"), Ib, kh)
+    mm([(B(5, 256, 384), OBb, r("PKn"), True, True)])
+    aff(r("PK"), B(5, 256, 384))
+    aff(r("PK32"), r("PK"), 1.0 / 32)
+    aff(r("PKn"), r("PK"), -1.0)
     ts(r("PW2"), OBb, r("WF", 512, 513), None, A.mult)
-    act(r("IL"), r("IL"), F.Identity, bias=kcol)
+    aff(r("IL"), r("IL"), None, kcol)
     ts(r("S8", p=(0, 8)), r("IG", p=(0, 8)), r("pcf", 0, 1, p=(0, 8)), None, A.is_equal)
     cp(r("thb", 0, 2, p=(0, 8)), r("ths", 0, 2, p=(0, 8)))
     mm([(B(7, 0, 2), r("S8", p=(0, 8)), r("thb", 0, 2, p=(0, 8)), True, True)])
-    act(r("XL0", 8192, 8193), B(7, 0, 1), F.Copy)
-    act(r("XL0", 8193, 8194), B(7, 1, 2), F.Identity, bias=-208.0)
+    aff(r("XL0", 8192, 8193), B(7, 0, 1), 0.5)
+    aff(r("XL0", 8193, 8194), B(7, 1, 2), None, -128.0)
 
     for k, (t, lo, hi) in enumerate(SENDS):
-        op("G", 300, [r("XL0", 0, 4096), r("XL0", 4096, 8192), r("XL0", 8192, XW)],
+        op("G", 300 if k else 3000, [r("XL0", 0, 4096), r("XL0", 4096, 8192), r("XL0", 8192, XW)],
            [r("XL%d" % t, lo, hi), r("ths", 4, 5)], lambda k=k: send(k))
-        ops[-1]["late"] = SEND * (hi - lo) / XW * (1 if k else 2)
+        ops[-1]["late"] = SEND * (0.75, 1.25, 0.5)[min(k, 2)]
+        ops[-1]["pair"] = k == 1
+        if k == 1:
+            io(blk("AW1", 0, 256), [[1, 256]], -256, 0)
+            diag("MJ", 76.0, "MJ")
+            diag("N35", -35.0)
+            diag("D25", 2.5)
+            io(r("NAT"), [[1, 2], [2, 256]], -256, 0)
+            io(blk("AW3", 0, 256), [[2, 256]], -256, 0)
 
     NW = r("NX", 0, 512)
-    PUn = r("PU", 128, 160)
-    cp(PUn, r("pts"))
-    ts(r("QN"), ind(r("cqs"), PUn), -2048.0, None, A.add)
     for h in range(2):
-        ts(blk("CE", 2 * h, 256), r("cqs", h, 512, 2), -2048.0, None, A.add)
-        cp(blk("CE", 2 * h + 1, 256), blk("CE", 2 * h, 256))
-        ts(blk("NX", h, 256), blk("CE", 2 * h, 256), -1.0, 2047.0, A.mult, A.add)
-        act(blk("ne", h, 256), blk("NX", h, 256), F.Sign)
-    act(r("PN"), ind(r("PERM"), PUn), F.Copy)
-    for h in range(2):
-        act(blk("PR0", h, 256), r("PN", h, 512, 2), F.Copy)
+        aff(blk("CE", 2 * h, 256), r("cqs", h, 512, 2), None, -2048.0, first="V")
+        aff(blk("CE", 2 * h + 1, 256), blk("CE", 2 * h, 256))
+        aff(blk("NX", h, 256), r("cqs", h, 512, 2), -1.0, 4095.0, first="V")
+        pos(blk("ne", h, 256), blk("NX", h, 256))
 
     def lists(t):
-        bk = (6, 3, 7, 7)[t]
-        mm([(B(bk, 0, 32), r("B0b", 15 - w, 143 - w), r("PR%d" % t, w, 512, 16), w == 0, w == 15) for w in range(16)])
-        ts(blk("PU", t, 32), B(bk, 0, 32), 256.0, None, A.add)
-        act(blk("PF", t, 32), B(bk, 0, 32), F.Identity, bias=256.0)
+        o = B((6, 3)[t], 0, 32)
+        if t == 0:
+            aff(r("PL", 32, 64), r("pts"))
+            mm([(B(7, 16, 32), r("Z", 8 - 8 * u, 136 - 8 * u), r("PL", 32 + u, 64, 2), u == 0, u == 1) for u in range(2)])
+            aff(r("YU"), B(7, 16, 32), first="V")
+            a = blk("ti", 0, 32)
+            ts(a, r("pts"), 1, None, A.bitwise_and)
+            ts(a, a, 511.0, None, A.mult)
+            tt(r("PL", 0, 32), a, r("pts"), A.add)
+            mm([(blk(o[0], v, 16), r("Z", 136 * v + 8 - 8 * u, 136 * v + 136 - 8 * u), r("PL", u, 32, 2), u == 0, u == 1)
+                for v in range(2) for u in range(2)])
+        else:
+            mm([(o, r("B0b", 15 - w, 143 - w), r("PR1", w, 512, 16), w == 0, w == 15) for w in range(16)])
+        aff(blk("PU", t, 32), o, *((None, 256.0) if t else (0.5, None)), first="V")
+        aff(blk("PF", t, 32), o, *((None, 256.0) if t else (0.5, None)))
 
     def compare(h):
         sb = 3 + 2 * h
+        qn = r("QN") if h else r("QH")
+        if h:
+            aff(qn, ind(NW, blk("PU", h, 16)), -1.0, 2047.0)
+        else:
+            aff(qn, ind(r("cqs"), r("YU")), None, -2048.0, first="V")
         for n in range(8):
             bk, eb = (0, 1, 2, 4)[n % 4], 4 * h + n % 4
-            if n in ES[h]:
-                mm([it for i in range(2) for it in acc(B(bk, 256 * i, 256 * i + 256),
-                                                       [(In, blk("CE", 2 * h, 256)), (blk("BT", 2 * n + i), r("QN", h, 512, 2))])])
-                act(B(bk), B(bk), F.Abs)
-                act(blk("E", eb, 512), B(bk), F.Relu, scale=-1.0, bias=1.0)
-            else:
-                mm([(B(bk, 256 * i, 256 * i + 256), blk("BT", 2 * n + i), r("QN", h, 512, 2), True, True) for i in range(2)])
-                tt(blk("E", eb, 512), B(bk), blk("CE", h, 512), A.is_equal)
+            mm([(B(bk, 256 * i, 256 * i + 256), blk("BT", 2 * n + i), qn, True, True) for i in range(2)])
+            tt(blk("E", eb, 512), B(bk), blk("CE", h, 512), A.is_equal)
             mm([(B(sb, 0, 256), DG(2 * n + i), blk("E", 2 * eb + i, 256), n + i == 0, n + i == 8) for i in range(2)])
         tt(blk("t5", h, 256), B(sb, 0, 256), blk("ne", h, 256), A.is_lt)
         tt(blk("WF", h, 256), B(sb, 0, 256), blk("ne", h, 256), A.mult)
 
     def tops(h):
         mm([(B(6, 0, 16), r("BM", 15 - w, 143 - w), r("t5", 256 * h + w, 256 * h + 256, 16), w == 0, w == 15) for w in range(16)])
-        act(blk("HL", h, 16), B(6, 0, 16), F.Sign)
-        act(blk("HL", 2 + h, 16), B(6, 0, 16), F.Sign, bias=-0.5)
-        act(blk("HX", h, 16), blk("IL", h, 16), F.Identity, bias=float(XO))
-        tt(blk("HX", h, 16), blk("HX", h, 16), blk("HL", h, 16), A.mult)
+        pos(blk("HL", h, 16), B(6, 0, 16))
+        aff(blk("HL", 2 + h, 16), blk("HL", h, 16), (-512.0, 512.0)[h], (768.0, 0.0)[h])
+        tt(blk("HX", h, 16), blk("IL", 2 + h, 16), blk("HL", h, 16), A.mult)
         o = B(7, 0, 256)
         mm([(o, r("FST"), blk("t5", h, 256), True, True)])
+        ts(o, o, -15.5, None, A.is_lt)
         act(o, o, F.Relu, bias=-15.0, scale=-1.0)
+        either("S")
         tt(blk("f5", h, 256), o, blk("CE", 2 * h, 256), A.mult)
         mm([(o, OBb, blk("f5", h, 256), True, True)])
-        act(r("NX", XO + 256 * h, XO + 256 * h + 256), o, F.Identity, scale=-1.0, bias=2047.0)
+        aff(r("NX", XO + 256 * h, XO + 256 * h + 256), o, -1.0, 2047.0)
 
     def chain(t):
         par = t & 1
         PF, il = blk("PF", 2 * t + par, 16), blk("IL", par, 16)
-        ly, x1, x0, ab = [blk("tl", i, 16) for i in range(4)]
-        cl = blk("CL", t, 16)
+        ly, x1, kind, e = [blk("tl", i, 16) for i in range(4)]
+        tt(e, PF, blk("HL", 2 + par, 16), A.add)
+        aff(x1, e, 1024.0, (-1023.5, -255.5)[par] * 1024, first="V")
+        tt(x1, x1, PF, (A.min, A.max)[par])
+        tt(x1, x1, il, (A.max, A.min)[par])
         tt(ly, PF, blk("HX", par, 16), A.max)
-        if t == 0:
-            cp(blk("LU", 0, 16), ly)
-        ts(x0, PF, 256.0, None, A.is_lt if par else A.is_ge)
-        tt(cl, x0, blk("HL", 2 + par, 16), A.mult)
-        ts(ab, cl, 0.0, None, A.is_lt)
-        tt(x1, PF, il, A.subtract)
-        tt(x1, x1, ab, A.mult)
-        tt(x1, x1, il, A.add)
-        cp(*((blk("LU", t, 32), blk("tl", 0, 32)) if t else (blk("LU", 1, 16), x1)))
+        ts(kind, e, 8, None, A.arith_shift_right)
+        aff(blk("LU", t, 48), blk("tl", 0, 48), first="V")
         aw = "AW3" if t == 3 else "AW%d" % par
-        act(blk(aw, par, 256), ind(r("NAT" if t == 3 else "IC"), blk("LU", 2 * t + 1, 16)), F.Copy)
-        act(r("PN" if t == 3 else "PR%d" % (t + 1)), ind(r(aw), blk("PU", t, 32)), F.Copy)
-
-    def code(t):
-        ts(blk("CU", t, 16), blk("CL", t, 16), -1.0, 1.0, A.mult, A.add)
-        act(blk("CD", t, 256), ind(r("IC", 256, 272), blk("CU", t, 16)), F.Copy)
+        aff(blk(aw, par, 256), ind(r("NAT" if t == 3 else "IC"), blk("LU", 3 * t + 1, 16)))
+        aff((r("PR1"), r("YH", 256), r("YH", 256), r("PN"))[t], ind(r(aw), blk("PU", t, 32)))
+        aff(blk("CD", t, 256), ind(r("T5"), blk("LU", 3 * t + 2, 16)))
 
     def parents_out():
-        mm([(B(7, 0, 32), r("B0b", 15 - w, 143 - w), r("PN", 256 * (w & 1) + (w >> 1), 256 * (w & 1) + 256, 8), w == 0, w == 15)
+        mm([(B(6, 64, 96), r("B0b", 15 - w, 143 - w), r("PN", 256 * (w & 1) + (w >> 1), 256 * (w & 1) + 256, 8), w == 0, w == 15)
             for w in range(16)])
-        act(r("OP"), B(7, 0, 32), F.Identity, bias=256.0)
+        aff(r("OP"), B(6, 64, 96), None, 256.0)
 
     def hop(t):
-        if t == 0:
-            x = blk("tl", 4, 16)
-            ts(x, blk("CL", 0, 16), 1.0, 512.0, A.add, A.mult)
-            tt(x, x, blk("IL", 0, 16), A.max)
-            ts(blk("LU", 8, 16), x, 512.0, None, A.min)
-            act(blk("TT", 0, 256), ind(r("WF"), blk("LU", 8, 16)), F.Copy)
-            act(r("TH", 0, 512), ind(r("TT"), blk("PU", 0, 32)), F.Copy)
-            return
-        a, b, x = blk("PF", 3, 16), blk("PF", 5, 16), blk("tl", 5, 16)
+        n = 16 if t else 32
+        a, b, x, u = [r(nm, lo, lo + n) for nm, lo in (("PF", 48 * t), ("PF", 32 + 48 * t), ("tf", 0), ("LU", 192 + 32 * t))]
         tt(x, a, b, A.is_equal)
-        act(x, x, F.Copy, scale=512.0)
+        aff(x, x, 512.0)
         tt(x, x, a, A.max)
-        cp(blk("LU", 10, 16), x)
-        act(blk("TH", 2, 256), ind(r("WF"), blk("LU", 10, 16)), F.Copy)
+        aff(u, x, first="V")
+        aff(r("TH", 512 * t, 512 * t + 16 * n), ind(r("WF"), u))
 
     def bit(o, src):
         n = cols(o)
         return acc(o, [(r("PK32"), r("ONE", 0, n)), (r("PK"), src), (Ib, r("RT", 0, n)), (In, r("RT", 0, n)), (r("PKn"), src)])
 
+    def carry(out, o, src, th, first):
+        mm(bit(o, src))
+        aff(o, o, 2.0 ** 34, None, True, first)
+        tt(out, o, th, A.min)
+
     def frames():
         mm([(B(2, 128 * k, 128 * k + 128), blk("PR1", k), OBb, True, True) for k in range(4)])
-        for par in range(2):
-            act(blk("TG", par, 512), B(2), F.Relu, scale=(1.0, -1.0)[par], bias=(8.0, -8.0)[par])
+        aff(blk("TG", 0, 512), B(2), None, 8.0, True)
+        ts(blk("TG", 1, 512), blk("TG", 0, 512), 0.0, 8.0, A.is_equal, A.mult)
+        act(blk("TG", 1, 512), blk("TG", 0, 512), F.Relu, scale=-1.0, bias=8.0)
+        either()
         for h in range(2):
-            o = B(4 + h, 0, 256)
-            mm(bit(o, blk("WF", h, 256)))
-            ts(o, o, 0.0, None, A.is_gt)
-            tt(blk("cw", h, 256), o, blk("TH", h, 256), A.mult)
+            bk = 4 + 3 * h
+            carry(blk("cw", h, 256), B(bk, 0, 256), blk("WF", h, 256), blk("TH", h, 256), "S")
             its = []
             for k in range(2):
                 c, rt = blk("cw", 2 * h + k), r("RT", 0, 128)
-                its += acc(B(4 + h, 256 + 128 * k, 384 + 128 * k), [(ONb, r("PK32")), (c, r("PK")), (Ib, rt), (In, rt), (c, r("PKn"))])
+                its += acc(B(bk, 256 + 128 * k, 384 + 128 * k), [(ONb, r("PK32")), (c, r("PK")), (Ib, rt), (In, rt), (c, r("PKn"))])
             mm(its)
             for par in range(2):
-                tt(blk("MT", 2 * par + h, 256), B(4 + h, 256, 512), blk("TG", 2 * par + h, 256), A.is_gt)
+                tt(blk("MT", 2 * par + h, 256), B(bk, 256, 512), blk("TG", 2 * par + h, 256), A.is_gt)
 
     def onehot():
         mm([(B(7, 8 * k, 8 * k + 8), blk("PR1", k), r("B0b", 15, 143, 16), True, True) for k in range(4)])
         a, b, d = [blk("ti", i, 32) for i in range(3)]
-        ts(a, B(7, 0, 32), 256.0, None, A.add)
+        aff(a, B(7, 0, 32), None, 256.0, first="V")
         ts(b, a, 128, None, A.bitwise_and)
         ts(d, a, 127, None, A.bitwise_and)
-        cp(blk("PW", 0, 32), d)
-        ts(blk("PW", 1, 32), b, 1023.0 / 128, 1.0, A.mult, A.add)
+        aff(blk("PW", 0, 32), d)
+        aff(blk("PW", 1, 32), b, 1023.0 / 128, 1.0)
         for q in range(8):
             for k in range(4):
                 i = 8 * k + q
                 ts(blk("OH", i), blk("IC", 2), r("PW", i, i + 1), r("PW", 32 + i, 33 + i), A.is_equal, A.mult)
 
     def head(t):
-        XL = "XL%d" % t
-        p0 = 32 * t + 16 * (t & 1)
-        for h in range(2):
-            ts(blk("QU", h), ind(NW, r("PU", p0 + 8 * h, p0 + 8 * h + 8)), -1.0, 4095.0, A.mult, A.add)
-        ts(r("YH"), ind(r("NX"), blk("LU", 2 * t, 16)), -1.0, 2047.0, A.mult, A.add)
-        mm([(B(6, 0, 16), r("B0b", 15 - w, 143 - w), r("YH", w, 256, 16), w == 0, w == 15) for w in range(16)])
-        ts(r("YU"), B(6, 0, 16), 2048.0, None, A.add)
-        ts(r("QH"), r("QU"), -2048.0, None, A.add)
-        mm([(B(5, 0, 256), blk("BT", 0), r("YH"), True, True)] + acc(B(5, 256, 512), [(r("L1"), r("YH")), (r("L2"), r("QH"))]))
+        if t:
+            aff(r("QU"), ind(NW, blk("PU", 2 * t + (t & 1), 16)), -1.0, 4095.0, first="V")
+        else:
+            aff(r("QU"), r("QH"), None, 2048.0, first="V")
+        YH = r("YH", 0, 256)
+        aff(YH, ind(r("NX"), blk("LU", 3 * t, 16)), -1.0, 2047.0, first="V")
+        n = 48 if t in (1, 2) else 16
+        mm([(B(6, 0, n), r("B0b", 15 - w, 143 - w), r("YH", w, 16 * n, 16), w == 0, w == 15) for w in range(16)])
+        aff(r("YU"), B(6, 0, 16), None, 2048.0, first="V")
+        if n > 16:
+            aff(blk("PU", t + 1, 32), B(6, 16, 48), None, 256.0, first="V")
+            aff(blk("PF", t + 1, 32), B(6, 16, 48), None, 256.0)
+        if t:
+            aff(r("QH"), r("QU"), None, -2048.0, first="V")
+        mm([(B(5, 0, 256), blk("BT", 0), YH, True, True)] + acc(B(5, 256, 512), [(r("L1"), YH), (r("L2"), r("QH"))]))
         tt(r("hm"), B(5, 0, 256), r("QH"), A.mult)
         tt(r("hi"), B(5, 256, 512), r("hm"), A.add)
         ts(r("hi"), r("hi"), 5, 4095, A.arith_shift_right, A.bitwise_and)
-        cp(r("HU"), r("hi"))
-        act(r("XY"), ind(r(XL, 0, 4096), r("YU")), F.Copy)
-        mm([(B(6, 128 * h, 128 * h + 128), blk("XY", h), In, True, True) for h in range(2)])
-        act(r("XT"), B(6, 0, 256), F.Copy)
+        aff(r("HU"), r("hi"), first="V")
+        aff(r("XY"), ind(r("XL%d" % t, 0, 4096), r("YU")))
+        mm([(B(6, 256 + 128 * h, 384 + 128 * h), blk("XY", h), In, True, True) for h in range(2)])
+        aff(r("XT"), B(6, 256, 512))
 
     def scores(t):
         XL = "XL%d" % t
         for n in range(8):
-            xq, bk, ad = blk("XQ", n, 512), B((0, 5, 1)[n % 3]), blk("AD", n, 512)
+            xq, bk = blk("XQ", n, 512), B((0, 5, 1)[n % 3])
             rows = (32 * (n % 4), 32 * (n % 4) + 32)
-            if n in VQ[t]:
-                cp(xq, ind(r(XL, 0, 4096), blk("QU", n, 32)))
-            elif n in XM:
-                act(r("XQ", 512 * n, 512 * n + 1024), ind(r(XL, 0, 4096), r("QU", 32 * n, 32 * n + 64)), F.Copy)
-            elif n - 1 not in XM:
-                act(xq, ind(r(XL, 0, 4096), blk("QU", n, 32)), F.Copy)
+            if n - 1 not in XM:
+                m = n + 1 + (n in XM)
+                aff(r("XQ", 512 * n, 512 * m), ind(r(XL, 0, 4096), r("QU", 32 * n, 32 * m)), first="V" if t and n == 1 else "S")
             mm(acc(bk, [(Ib, xq), (r("XT", 128 * (n // 4), 128 * (n // 4) + 128, p=rows), r("EX", p=rows))]))
-            act(ad, bk, F.Abs)
-            tt(blk("CM", n, 512), ind(r(XL, 4096, 8192), blk("HU", n, 32)), ad, A.is_ge)
+            act(blk("AD", n, 512), bk, F.Abs)
+            if n not in CJ:
+                m = n - (n - 1 in CJ)
+                tt(r("CM", 512 * m, 512 * n + 512), ind(r(XL, 4096, 8192), r("HU", 32 * m, 32 * n + 32)),
+                   r("AD", 512 * m, 512 * n + 512), A.is_ge)
 
-    def early(t):
+    def own(t):
         par = t & 1
-        ne, o = blk("ne", par, 256), B(7, 0, 256)
+        o = B(2, 192, 448)
         if t > 1:
-            act(ne, blk("NX", par, 256), F.Sign)
-        mm(acc(o, [(DG(14), r("ONE", 0, 256)), (r("N8k"), blk("CD", t, 256))]))
+            pos(blk("ne", par, 256), blk("NX", par, 256))
+        mm([(o, DG(11), blk("CD", t, 256), True, True)])
         tt(blk("Nx", par, 256), o, blk("NX", par, 256), A.min)
-        count(t, 2 * par)
-        count(t, 2 * par + 1)
 
-    def count(t, k):
-        par = t & 1
-        its = [(B(1, 0, 128), r("ZR"), Ib, True, False)] if k == 2 * par else []
-        mm(its + [(B(1, 16 * q, 16 * q + 16), blk("OH", 8 * k + q), blk("MT", 32 * par + 8 * k + q, 16), False,
-                   k == 3 - 2 * par and q == 7) for q in range(8)])
+    def members():
+        o = B(7, 0, 256)
+        mm([it for f in range(2) for it in acc(B(7, 128 * f, 128 * f + 128), [(blk("MT", 2 + f), Ib), (blk("MT", 6 + f), Ib)])])
+        tt(r("cw", 256, 512), o, blk("TH", 2, 256), A.mult)
+        mm(bit(o, r("cw", 256, 512)))
+        ts(r("b3"), o, 0.0, None, A.is_gt)
 
     def masks(t):
         par = t & 1
         XL = "XL%d" % t
         cd, W = blk("CD", t, 256), blk("WF", par, 256)
         ts(r("q"), r("QU"), 4095.0, None, A.is_lt)
-        act(r("Ns"), ind(NW, blk("LU", 2 * t + 1, 16)), F.Copy)
+        act(r("q"), r("QU"), F.Sign, scale=-1.0, bias=4095.0)
+        either()
+        aff(r("Ns"), ind(NW, blk("LU", 3 * t + 1, 16)))
+        for i, k in enumerate((0, 1, 2, 3) if par == 0 else (2, 3, 0, 1)):
+            mm([(B(3, 256 + 16 * q, 272 + 16 * q), blk("OH", 8 * k + q), blk("MT", 32 * par + 8 * k + q, 16), i + q == 0, i + q == 10)
+                for q in range(8)])
+        ts(r("ki"), B(3, 256, 384), 1024.0 * RND, -1024.0 * RND, A.add, A.add)
+        tt(blk("nh", 0), B(3, 256, 384), r("ki"), A.not_equal)
+        pos(blk("nh", 1), r("ki"))
         mm([(B(3, 0, 256), In, r("QH"), True, True)])
-        count(t, 2 - 2 * par)
-        count(t, 3 - 2 * par)
-        ts(r("ki"), B(1, 0, 128), 1024.0 * RND, -1024.0 * RND, A.add, A.add)
-        tt(blk("nh", 0), B(1, 0, 128), r("ki"), A.not_equal)
-        act(blk("nh", 1), r("ki"), F.Sign)
         o = B(7, 256, 512)
-        its = []
-        for f in range(2):
-            its += acc(B(7, 256 + 128 * f, 384 + 128 * f), [(Ib, blk("ne", 2 * par + f)), (blk("nh", f), In)])
-        mm(its)
+        mm([it for f in range(2)
+            for it in acc(B(7, 256 + 128 * f, 384 + 128 * f), [(Ib, blk("ne", 2 * par + f)), (blk("nh", f), In)])])
         cw = r("cw", 0, 256)
         tt(cw, o, W, A.mult)
-        for th in ([], [], [blk("TH", 0, 256)], [blk("TH", 1, 256), blk("TH", 2, 256)])[t]:
-            mm(bit(o, cw))
-            ts(o, o, 0.0, None, A.is_gt)
-            tt(cw, o, th, A.mult)
+        for th in ((), (), (0,), (1, 2))[t]:
+            carry(cw, o, cw, blk("TH", th, 256), "V")
         mm(bit(o, cw))
         act(r("cb"), o, F.Sign, scale=-1.0, bias=2.0 ** -18)
         o = B(4, 0, 256)
-        if t == 3:
-            mm([it for f in range(2) for it in acc(B(4, 128 * f, 128 * f + 128), [(blk("MT", 2 + f), Ib), (blk("MT", 6 + f), Ib)])])
-            tt(r("cw", 256, 512), o, blk("TH", 2, 256), A.mult)
-            mm(bit(o, r("cw", 256, 512)))
-            ts(r("b3"), o, 0.0, None, A.is_gt)
         its = []
         for f in range(2):
             held = (r("N16"), blk("b3", f)) if t == 3 else (blk("MT", 4 - 2 * par + f), r("N16"))
             its += acc(B(4, 128 * f, 128 * f + 128),
-                       [held, (DG(4), blk("q", f)), (r("OBm"), blk("ne", 2 * par + f)), (r("N16"), blk("CD", 2 * t + f))])
+                       [held, (DG(4), blk("q", f)), (r("OBm"), blk("ne", 2 * par + f)), (DG(2), blk("CD", 2 * t + f))])
         mm(its)
-        act(r("pj"), o, F.Sign, bias=-0.5)
+        act(r("pj"), o, F.Sign, bias=-32.5)
         o = B(4, 256, 512)
-        mm(acc(o, [(DG(6), cd), (DG(6), r("q")), (DG(4), r("cb"))]))
-        act(r("thr"), o, F.Identity, bias=r(XL, 8193, 8194))
+        mm(acc(o, [(r("N16"), cd), (DG(6), r("q")), (DG(4), r("cb"))]))
+        aff(r("thr"), o, None, r(XL, 8193, 8194))
         th1 = r(XL, 8192, 8193)
         if t:
-            act(r("cn", 0, 1), B(2, 384, 385), F.Copy)
-            cn, rt = [r("cn", 0, 1)], r("RT", 0, 1)
-            mm(acc(B(2, 386, 387), [(Ib, r("cn", 2, 3))] + [(r("NEG"), x) for x in cn]
-                   + [(DG(1), rt), (In, rt), (In, rt)] + [(ONb, x) for x in cn] + [(Ib, th1)]))
+            cn, rt = r("cn", 0, 1), r("RT", 0, 1)
+            aff(cn, B(2, 384, 385), 0.5)
+            mm(acc(B(2, 386, 387), [(Ib, r("cn", 2, 3)), (r("NEG"), cn), (Ib, rt), (In, rt), (ONb, cn), (Ib, th1)]))
             th1 = B(2, 386, 387)
-        act(r("sc", 2, 3), th1, F.Identity, scale=-KL, bias=-32.0 * KL - 48 * LN2)
+        aff(r("sc", 2, 3), th1, -2 * KL, -16.0 * KL - 48 * LN2)
 
     def piece(t, f):
         par = t & 1
-        lo, hi = (0, CUT) if f == 0 else (CUT, 256)
+        lo, hi = PIECES[t][f][:2]
         n, d = hi - lo, 256 * par
-        v, ta, tb, z, y = [B(k, c, c + n) for k, c in (((2, 0), (2, 192), (5, 256), (4, 0), (5, 0)),
-                                                       ((6, 0), (6, 128), (6, 256), (0, 0), (6, 384)))[f]]
+        v, ta, tb, z, y = [B(k, c, c + n) for k, c in PIECES[t][f][2:]]
         wA, wB, KP, cb, HA, HB, pA, pB, AB = [r(x, lo, hi) for x in ("wA", "wB", "KP", "cb", "HA", "HB", "pA", "pB", "AB")]
         cd, Q = r("CD", 256 * t + lo, 256 * t + hi), B(3, lo, hi)
         sums = [acc(r(v[0], 64 * k - lo, 64 * k + 64 - lo), [(r("BM", 15 - j, 143 - j), r("CM", 1024 * k + j, 1024 * k + 1024, 16))
-                                                             for j in range(16)], False, f == 1 and k == 3)
+                                                             for j in range(16)], False, f > 0 and k == hi // 64 - 1)
                 for k in range(lo // 64, hi // 64)]
-        sums.insert(len(sums) - f, [(v, DG(4), cb, False, f == 0)])
-        mm([(v, DG(4), r("pj", lo, hi), True, False)])
+        if f == 0:
+            mm([(B(6, 128 + j, 256, 16), r("CM", j, 2048, 16), r("BM", 15, 143, 16), j == 0, j == 15) for j in range(16)])
+            aff(r("sT"), B(6, 128, 256))
+            sums[:2] = [[(r(v[0], 0, 128), r("sT"), Ib, False, False)]]
+        sums.insert(len(sums) - (f > 0), [(v, DG(4), cb, False, f == 0)])
+        mm(acc(v, [(DG(6), r("pj", lo, hi)), (r("N8"), cd)], stop=False))
         for its in sums:
             mm(its)
         act(wA, v, F.Exp, scale=KL, bias=r("sc", 2, 3))
-        act(wB, v, F.Exp, scale=-KL, bias=48 * LN2 - 32 * KL)
+        act(wB, v, F.Exp, scale=-KL, bias=48 * LN2 - 144 * KL)
         tt(KP, v, r("thr", lo, hi), A.is_le)
         mm([(ta, r("TRI"), wA, True, True)])
-        mm(acc(tb, [(r("D60"), cd), (r("TRI"), wB)]))
+        mm([(tb, r("TRI"), wB, True, True)])
         ts(HA, ta, -2.0 ** -50, None, A.is_lt)
         tt(pA, Q, HA, A.mult)
         ts(HB, tb, -2.0 ** -50, None, A.is_lt)
@@ -502,20 +527,20 @@ def build(g, T, send):
             tt(r("NX", d + lo, d + hi), z, AB, A.mult)
         else:
             tt(z, z, AB, A.mult)
-            act(r("OC", 2 * lo + 1, 2 * hi, 2), z, F.Identity, scale=-1.0, bias=4095.0)
+            aff(r("OC", 2 * lo + 1, 2 * hi, 2), z, -1.0, 4095.0)
 
     def after(t):
         par = t & 1
         for f in range(2):
             mm(acc(B(7, 128 * f, 128 * f + 128),
-                   [(DG(6), blk("MT", 4 - 2 * par + f)), (blk("cb", f), DG(3)), (blk("CD", 2 * t + f), r("N16"))]
-                   + ([(blk("CD", f), r("N10"))] if t == 2 else [])
+                   [(DG(6), blk("MT", 4 - 2 * par + f)), (blk("cb", f), DG(3)), (blk("CD", 2 * t + f), DG(2))]
+                   + ([(blk("CD", f), r("D25"))] if t == 2 else [])
                    + [(blk("KP", f), DG(7)), (blk("HA", f), r("MJ")), (blk("HB", f), r("N35"))]))
-        ts(blk("MT", 2 - par, 256), B(7, 0, 256), 22.0 if t == 2 else 32.0, None, A.is_gt)
+        ts(blk("MT", 2 - par, 256), B(7, 0, 256), 74.0 if t == 2 else 64.0, None, A.is_gt)
         mm(acc(B(2, 384, 385), [(blk("HA", f), r("ONE", 0, 1)) for f in range(2)]))
 
     def weights(t):
-        o = B(7, 256, 512)
+        o = B(1, 256, 512)
         mm(acc(o, [(r("F16"), blk("ne", t, 256)), (r("K16"), r("ONE", 0, 256)), (r("PW2"), r("HA"))]))
         tt(blk("WF", t, 256), o, blk("WF", t, 256), A.max)
 
@@ -530,35 +555,32 @@ def build(g, T, send):
     tops(1)
     hop(0)
     frames()
-    code(0)
-    early(0)
+    own(0)
     for t in range(4):
-        if t == 3:
-            parents_out()
         if t > 0:
             head(t)
         masks(t)
         scores(t)
-        if t in (1, 2):
-            weights(t - 1)
         if t == 2:
             hop(1)
+            members()
         if t < 3:
-            if t:
-                lists(t + 1)
             chain(t + 1)
-            code(t + 1)
-            early(t + 1)
-        piece(t, 0)
-        piece(t, 1)
+        for f in range(len(PIECES[t])):
+            piece(t, f)
+            if f == 0 and t < 3:
+                own(t + 1)
         if t < 3:
             after(t)
+        if t < 2:
+            weights(t)
         if t == 2:
-            act(r("OC", 0, 512, 2), blk("NX", 0, 256), F.Identity, bias=4095.0, scale=-1.0)
+            parents_out()
+            aff(r("OC", 0, 512, 2), blk("NX", 0, 256), -1.0, 4095.0)
     return ops
 
 
-EXT = {"dcq": 2600, "dpt": 2300, "dth": 2400, "dxs": 10500, "dlim": 13000}
+EXT = {"dcq": 2600, "dpt": 2300, "dth": 2400, "dxs": 14000, "dlim": 18000}
 SEND = 13000.0
 PARTS = ((0, 4096), (4096, XW))
 SENDS = [(t, lo, hi) for t in (1, 2, 3) for lo, hi in PARTS]
@@ -579,8 +601,7 @@ def meet(a, b):
     return not (a[3] == b[3] > 1 and (a[1] - b[1]) % a[3])
 
 
-def schedule(ops):
-    n = len(ops)
+def links(ops, banks):
     seen = {}
     deps, below = [], []
     for i, o in enumerate(ops):
@@ -588,12 +609,12 @@ def schedule(ops):
         use = [(x, False) for x in o["r"]] + [(x, True) for x in o["w"]]
         for x, w in use:
             for j, y, v in seen.get(x[0], []):
-                if psum(x) and (ops[j]["e"] != o["e"] or o["e"] == "P") or (w or v) and meet(x, y):
+                if (w or v) and meet(x, y) or banks and psum(x):
                     d.add(j)
         for x, w in use:
             seen.setdefault(x[0], []).append((i, x, w))
-        if "late" in o:
-            d.update(j for j in range(i) if ops[j]["e"] == "G")
+        if o["e"] == "G":
+            d.update(j for j in range(i) if ops[j]["e"] == "G" and ("late" in o or "late" in ops[j]))
         d.discard(i)
         keep, cover = [], 0
         for j in sorted(d, reverse=True):
@@ -602,218 +623,263 @@ def schedule(ops):
                 cover |= below[j] if "late" not in ops[j] else 0
         deps.append(keep)
         below.append(cover | 1 << i)
-    succ = [[] for _ in range(n)]
-    for i in range(n):
-        for d in deps[i]:
-            succ[d].append(i)
-    start = arrange(ops, deps, succ)
-    second = [i for i in range(n) if "late" in ops[i]][1]
-    for i in range(n):
-        if ops[i]["e"] == "G" and ops[i]["w"][0][0] in ("NAT", "AW1", "AW3"):
-            start[i] = min([start[second] + 1.0] + [start[s] - 1.0 for s in succ[i] if "late" not in ops[s]])
-    return sorted(range(n), key=lambda i: (start[i], i)), deps, start
+    return deps
+
+
+def schedule(ops):
+    deps = links(ops, False)
+    banks = [sorted(set(int(x[0][1]) for x in o["r"] + o["w"] if psum(x))) for o in ops]
+    seq, eng = arrange(ops, deps, banks)
+    last = {}
+    for i in seq:
+        for b in banks[i]:
+            if b in last and eng[last[b]] != eng[i] and last[b] not in deps[i]:
+                deps[i].append(last[b])
+            last[b] = i
+    return seq, deps, ["VSPG"[e] for e in eng]
 
 
 CACHE = {}
-LAT = 200.0
-CASES = ((1.56, 220.0, 1.0), (1.25, 170.0, 1.1), (1.95, 190.0, 1.0))
-ROUNDS = 9500
-MIX = 500
-STEPS = 1000
-HEAT = 150.0
+CASES = ((1.56, 220.0, 1.0), (1.9, 100.0, 1.0), (1.1, 150.0, 1.1))
+SWEEPS = 20
+WIDE = 150
+STEPS = 2700
+HEAT = 300.0
+EARLY = 0.002
+SEED = 1
 
 
-def place(seq, pre, eng, cost, rel):
-    line = {"V": [], "S": [], "P": [], "G": []}
-    st = [0.0] * len(seq)
-    for i in seq:
-        e, c, t = eng[i], cost[i], rel[i]
-        for d, w in pre[i]:
-            if st[d] + w > t:
-                t = st[d] + w
-        ln = line[e]
-        lo, hi = 0, len(ln)
-        while lo < hi:
-            m = (lo + hi) // 2
-            if ln[m][1] <= t:
-                lo = m + 1
-            else:
-                hi = m
-        while lo < len(ln) and ln[lo][0] < t + c:
-            t = max(t, ln[lo][1])
-            lo += 1
-        ln.insert(lo, (t, t + c))
-        st[i] = t
-    return st
-
-
-def arrange(ops, deps, succ):
+def arrange(ops, deps, banks):
     n = len(ops)
-    eng = [o["e"] for o in ops]
-    num = ["VSPG".index(e) for e in eng]
-    rel = [max([EXT.get(outside(x), 0.0) for x in o["r"]] + [0.0]) for o in ops]
+    eng = ["VSPG".index(o["e"]) for o in ops]
+    rel = [min(max([EXT.get(outside(x), 0.0) for x in o["r"]] + [0.0]), SEND if o["e"] == "G" else 1e9) for o in ops]
 
-    def gap(a, b, lat):
-        return ops[a].get("late", 0.0) + (0.0 if eng[a] == eng[b] == "P" else (0.5 * lat if eng[a] == eng[b] else lat))
+    def edges(deps):
+        fore = [[(d, ops[d].get("late", 0.0) if o["e"] != "G" or not o.get("pair", True) else 0.0) for d in deps[i]]
+                for i, o in enumerate(ops)]
+        aft = [[] for _ in ops]
+        for i in range(n):
+            for d, w in fore[i]:
+                aft[d].append((i, w))
+        return fore, aft
     cases = []
     for ga, lat, pe in CASES:
-        cost = [(o["c"] + o["g"] * (ga - GA)) * (pe if o["e"] == "P" else 1.0) for o in ops]
-        cases.append(([[(d, cost[d] + gap(d, i, lat)) for d in deps[i]] for i in range(n)], num, cost, rel))
-    fore, cost = cases[0][0], cases[0][2]
-    aft = [[(s, cost[s] + gap(i, s, CASES[0][1])) for s in succ[i]] for i in range(n)]
+        cost = []
+        for o in ops:
+            c = [(o["c"] + o["g"] * (ga - GA)) * (pe if o["e"] == "P" else 1.0)] * 4
+            if "alt" in o:
+                c["VSPG".index(o["alt"][0])] = o["alt"][1] + o["g"] * (ga - GA)
+            cost.append(c)
+        cases.append((cost, [[0.0 if a == b == 2 else (0.5 * lat if a == b else lat) for a in range(4)] for b in range(4)], lat))
+    cost, gap = cases[0][:2]
+    fore, aft = edges(links(ops, True))
     way = [0.0] * n
     for i in range(n - 1, -1, -1):
-        way[i] = cost[i] + max([way[s] + gap(i, s, CASES[0][1]) for s in succ[i]] + [0.0])
-    best, total, rnd = None, 1e18, 12345
-    for k in range(ROUNDS):
-        if best is None:
-            seq = sorted(range(n), key=lambda i: (-way[i], i))
-        else:
-            key = list(best)
-            rnd = (rnd * 1103515245 + 12345) % 2147483648
-            t0, amp = rnd / 2147483648.0 * max(best), (500.0, 1500.0, 4000.0)[k % 3]
-            for i in range(n):
-                if abs(best[i] - t0) < 7000:
-                    rnd = (rnd * 1103515245 + 12345) % 2147483648
-                    key[i] += rnd / 2147483648.0 * amp
-                for d in deps[i]:
-                    key[i] = max(key[i], key[d] + 1e-3)
-            seq = sorted(range(n), key=lambda i: (key[i], i))
-        st = place(seq, fore, eng, cost, rel)
-        for _r in range(6 if best is None else 1):
-            back = place(sorted(range(n), key=lambda i: (-st[i] - cost[i], -i)), aft, eng, cost, [0.0] * n)
-            st = place(sorted(range(n), key=lambda i: (-back[i] - cost[i], i)), fore, eng, cost, rel)
-            seq = sorted(range(n), key=lambda i: (st[i], i))
-            sp = worth([run(seq, 0, st, st, *c) for c in cases])
-            if sp <= total:
-                best, total = st, sp
-        if k % MIX == MIX - 1:
-            best, total = anneal(best, aft, cases)
-    return best
+        way[i] = cost[i][eng[i]] + max([way[s] + w + gap[eng[s]][eng[i]] for s, w in aft[i]] + [0.0])
+    seq = justify(sorted(range(n), key=lambda i: (-way[i], i)), fore, aft, eng, cost, gap, rel)
+    fore, aft = edges(deps)
+
+    def run(part, end, by, last, case):
+        cost, gap, lat = case
+        for i in part:
+            e, t, u = eng[i], rel[i], -1
+            ge = gap[e]
+            for d, w in fore[i]:
+                x = end[d] + w + ge[eng[d]]
+                if x > t:
+                    t, u = x, d
+            d = last[e]
+            if end[d] > t:
+                t, u = end[d], -2 - d
+            for b in banks[i]:
+                d = last[4 + b]
+                if end[d] + lat > t and eng[d] != e:
+                    t, u = end[d] + lat, -2 - d
+                last[4 + b] = i
+            end[i] = t + cost[i][e]
+            by[i], last[e] = u, i
+
+    def rest(part, case):
+        cost, gap, lat = case
+        way, nxt = [0.0] * n + [0.0, -1e9], [n, n, n] + [n + 1] * 9
+        for i in reversed(part):
+            e = eng[i]
+            t = way[nxt[e]]
+            for s, w in aft[i]:
+                t = max(t, w + gap[eng[s]][e] + way[s])
+            for b in banks[i]:
+                if eng[nxt[4 + b]] != e:
+                    t = max(t, lat + way[nxt[4 + b]])
+                nxt[4 + b] = i
+            way[i], nxt[e] = t + cost[i][e], i
+        return way, nxt
+
+    def clash(part, held):
+        for i in part:
+            if eng[i] == 2:
+                b, start, stop = ops[i]["s"]
+                if start and b in held:
+                    return True
+                (held.discard if stop else held.add)(b)
+        return False
+
+    bounds = set(i for i in range(n) if eng[i] == 2 and ops[i]["s"][1] != ops[i]["s"][2])
+    eng += [-1, -1]
+    rnd = SEED
+    for sweep in range(SWEEPS):
+        for lo in range(-(sweep * 37 % (WIDE // 2)), n - WIDE // 2, WIDE // 2):
+            lo, hi = max(lo, 0), min(lo + WIDE, n)
+            end = [0.0] * n + [-1e9]
+            run(seq, end, [-1] * n, [n] * 12, cases[0])
+            at = {i: p for p, i in enumerate(seq)}
+            seq.sort(key=lambda i: (end[i] - cost[i][eng[i]], at[i]))
+            inside, held = set(seq[lo:hi]), set()
+            clash(seq[:lo], held)
+            now, out = [], []
+            for c in cases:
+                end, by, last = [0.0] * n + [-1e9], [-1] * n, [n] * 12
+                run(seq[:lo], end, by, last, c)
+                way, nxt = rest(seq[hi:], c)
+                far = [(i, [max(w + c[1][eng[s]][e] + way[s] for s, w in aft[i] if s not in inside) for e in range(4)])
+                       for i in seq[lo:hi] if any(s not in inside for s, w in aft[i])]
+                now.append((end, by, 0.0))
+                out.append((last, [(way[s], eng[s]) for s in nxt], far))
+
+            def judge(new, a, old, room=1e18):
+                res, total = [], 0.0
+                last0 = list(out[0][0])
+                for i in new[lo:a]:
+                    last0[eng[i]] = i
+                    for b in banks[i]:
+                        last0[4 + b] = i
+                part = new[a:hi]
+                for c, x, (last, nxt, far) in zip(cases, old, out):
+                    end, by, last = list(x[0]), list(x[1]), list(last0)
+                    run(part, end, by, last, c)
+                    t, j = max((end[i] + w + (c[2] if k > 3 and eng[i] != e else 0.0), i) for k, (i, (w, e)) in enumerate(zip(last, nxt)))
+                    for i, y in far:
+                        if end[i] + y[eng[i]] > t:
+                            t, j = end[i] + y[eng[i]], i
+                    t += EARLY * sum([end[i] for i in inside])
+                    if t - room > x[-1]:
+                        return None, 1e18
+                    res.append((end, by, j, t))
+                    total += t
+                return res, total
+            now, total = judge(seq, lo, now)
+            best, keep = total, (seq, list(eng))
+            for k in range(STEPS):
+                end, by, j = now[k % len(now)][:3]
+                pairs = []
+                while j in inside:
+                    b = by[j]
+                    if b <= -2:
+                        b = -2 - b
+                        if b in inside:
+                            pairs.append((b, j))
+                    j = b
+                if not pairs:
+                    continue
+                rnd = (rnd * 1103515245 + 12345) % 2147483648
+                u, v = pairs[(rnd >> 8) % len(pairs)]
+                a, b = seq.index(u, lo), seq.index(v, lo)
+                rnd = (rnd * 1103515245 + 12345) % 2147483648
+                step, kind, flip = (0, 0, 1, 2, 4, 8, 16)[(rnd >> 8) % 7], rnd >> 20 & 7, -1
+                if kind < 2 and "alt" in ops[(u, v)[kind]]:
+                    flip, a = (u, v)[kind], (a, b)[kind]
+                    p = q = a
+                    while rnd >> 23 & 1 and p > lo and all(seq[p - 1] != d for d, w in fore[flip]):
+                        p -= 1
+                    while rnd >> 23 & 1 and q < hi - 1 and all(seq[q + 1] != s for s, w in aft[flip]):
+                        q += 1
+                    p += (rnd >> 4) % (q - p + 1)
+                    new = seq[:a] + seq[a + 1:]
+                    new.insert(p, flip)
+                    a = min(a, p)
+                    eng[flip] = 1 - eng[flip]
+                else:
+                    if kind & 1:
+                        while step and a > lo:
+                            a -= 1
+                            step -= eng[seq[a]] == eng[v]
+                        go = {v}
+                        for x in reversed(seq[a:b]):
+                            if any(s in go for s, w in aft[x]):
+                                go.add(x)
+                    else:
+                        while step and b < hi - 1:
+                            b += 1
+                            step -= eng[seq[b]] == eng[u]
+                        go = {u}
+                        for x in seq[a + 1:b + 1]:
+                            if any(s in go for s, w in fore[x]):
+                                go.add(x)
+                        go = set(seq[a:b + 1]) - go
+                    new = seq[:a] + [x for x in seq[a:b + 1] if x in go] + [x for x in seq[a:b + 1] if x not in go] + seq[b + 1:]
+                    if not bounds.isdisjoint(seq[a:b + 1]) and clash(new[lo:b + 1], set(held)):
+                        continue
+                rnd = (rnd * 1103515245 + 12345) % 2147483648
+                room = -(HEAT * (1.0 - k / STEPS) + 5.0) * math.log(((rnd >> 8) + 1) / 8388608.0)
+                then, t = judge(new, a, now, room + 300.0)
+                if t <= total + room:
+                    total, now, seq = t, then, new
+                    if t < best:
+                        best, keep = t, (seq, list(eng))
+                elif flip >= 0:
+                    eng[flip] = 1 - eng[flip]
+            seq = list(keep[0])
+            eng[:] = keep[1]
+    ends = []
+    for c in cases:
+        end, last = [0.0] * n + [-1e9], [n] * 12
+        run(seq, end, [-1] * n, last, c)
+        ends.append((max(end[i] for i in last[:3]), [end[i] - c[0][i][eng[i]] for i in range(n)]))
+    CACHE["ends"] = ends
+    return seq, eng[:n]
 
 
-def run(seq, a, st, by, fore, eng, cost, rel):
-    free, last = [0.0] * 4, [-1] * 4
-    p = a - 1
-    while p >= 0 and min(last) < 0:
-        i = seq[p]
-        if last[eng[i]] < 0:
-            last[eng[i]], free[eng[i]] = i, st[i] + cost[i]
-        p -= 1
-    st, by = list(st), list(by)
-    for i in seq[a:]:
-        e, t, b = eng[i], rel[i], -1
-        for d, w in fore[i]:
-            if st[d] + w > t:
-                t, b = st[d] + w, d
-        if free[e] > t:
-            t, b = free[e], -2 - last[e]
-        st[i], by[i] = t, b
-        free[e], last[e] = t + cost[i], i
-    e = free.index(max(free[:3]))
-    return free[e], st, by, last[e]
-
-
-def worth(runs):
-    return sum(x[0] + 1.5 * sum(x[1]) / len(x[1]) for x in runs)
-
-
-def anneal(st, aft, cases):
-    n = len(st)
-    fore, eng = cases[0][:2]
-    rnd = int(sum(st)) % 99991
-    for part in range(6):
-        seq = sorted(range(n), key=lambda i: (st[i], i))
-        now = [run(seq, 0, st, st, *c) for c in cases]
-        best, keep = worth(now), now[0][1]
-        end = best
-        for k in range(STEPS):
-            span, at, by, j = now[k % len(now)]
-            lo, hi = (part - 0.3) * span / 6, (part + 1.3) * span / 6
-            pairs = []
-            while j >= 0 and at[j] >= lo:
-                b = by[j]
-                if b <= -2:
-                    b = -2 - b
-                    if at[j] < hi:
-                        pairs.append((b, j))
-                j = b
-            if not pairs:
-                continue
-            rnd = (rnd * 1103515245 + 12345) % 2147483648
-            u, v = pairs[(rnd >> 8) % len(pairs)]
-            a, b = seq.index(u), seq.index(v)
-            rnd = (rnd * 1103515245 + 12345) % 2147483648
-            far = (0, 0, 1, 2, 4)[(rnd >> 8) % 5]
-            if rnd >> 20 & 1:
-                while far and a > 0:
-                    a -= 1
-                    far -= eng[seq[a]] == eng[v]
-                go = {v}
-                for x in reversed(seq[a:b]):
-                    if any(s in go for s, w in aft[x]):
-                        go.add(x)
-                new = seq[:a] + [x for x in seq[a:b + 1] if x in go] + [x for x in seq[a:b + 1] if x not in go] + seq[b + 1:]
-            else:
-                while far and b < n - 1:
-                    b += 1
-                    far -= eng[seq[b]] == eng[u]
-                go = {u}
-                for x in seq[a + 1:b + 1]:
-                    if any(s in go for s, w in fore[x]):
-                        go.add(x)
-                new = seq[:a] + [x for x in seq[a:b + 1] if x not in go] + [x for x in seq[a:b + 1] if x in go] + seq[b + 1:]
-            then = [run(new, a, x[1], x[2], *c) for x, c in zip(now, cases)]
-            e2 = worth(then)
-            rnd = (rnd * 1103515245 + 12345) % 2147483648
-            if e2 <= end or (rnd >> 8) / 8388608.0 < math.exp((end - e2) / (HEAT * (1.0 - k / STEPS) + 1.0)):
-                end, now, seq = e2, then, new
-                if end < best:
-                    best, keep = end, now[0][1]
-        st = keep
-    return st, best
+def justify(seq, fore, aft, eng, cost, gap, rel):
+    n = len(seq)
+    for k in range(13):
+        pre = aft if k & 1 else fore
+        line = [[], [], [], []]
+        end = [0.0] * n
+        for i in seq:
+            e, t = eng[i], 0.0 if k & 1 else rel[i]
+            c = cost[i][e]
+            for d, w in pre[i]:
+                t = max(t, end[d] + w + gap[e][eng[d]])
+            ln, p = line[e], 0
+            while p < len(ln) and ln[p][0] < t + c:
+                t = max(t, ln[p][1])
+                p += 1
+            ln.insert(p, (t, t + c))
+            end[i] = t + c
+        seq = sorted(seq, key=lambda i: -end[i])
+    return sorted(range(n), key=lambda i: (end[i] - cost[i][eng[i]], i))
 
 
 def routes(T, topo):
     n = len(T.cores)
-    free = [c for c in topo.cores_of(T.cores[0]) if c not in T.cores]
-    plan = {}
+    plan = {c: [] for c in T.cores}
     for a, src in enumerate(T.cores):
         need = [(T.cores[(a - t) % n], t) for t in range(1, n)]
         far = [x for x in need if topo.die(x[0]) != topo.die(src)]
-        help_ = [c for c in free if len(far) > 1 and c not in plan and topo.die(c) == topo.die(far[0][0])]
-        plan[src] = need
-        if help_:
-            plan[help_[0]] = far
-            plan[src] = [(help_[0], 0) if x == far[0] else x for x in need if x not in far[1:]]
-    return plan
+        for dst, t in need:
+            for part in range(2):
+                if (dst, t) in far[1:] and (part or t > 2):
+                    plan[far[0][0]].append((t, far[0][1], part, dst))
+                else:
+                    plan[src].append((t, 0, part, dst))
+    return {c: sorted(plan[c]) for c in plan}
 
 
 def rank_program(g, core, T, topo):
-    rank = T.rank_of(core)
-    n = len(T.cores)
+    if T.rank_of(core) is None:
+        return
     sem = T.sem
     plan = routes(T, topo)
-
-    def write(dst, t, lo, hi):
-        rid, pid, _ = topo.addr(dst)
-        g.remote_dma(T["XL%d" % t][:, lo:hi], T.XL0[:, lo:hi], sem["arr%d%s" % (max(t, 1), "ab"[lo > 0])], sem.sent, pid, rid,
-                     topo.mask(core, dst))
-        return len(topo.engines(core, dst))
-
-    if rank is None:
-        gone = 0
-        for k, (dst, t) in enumerate(plan.get(core, [])):
-            if k:
-                g.wait_ge(sem.sent, gone)
-            for lo, hi in PARTS:
-                if k == 0:
-                    src = [c for c in T.cores if (core, 0) in plan[c]][0]
-                    g.wait_ge(sem["arr1" + "ab"[lo > 0]], len(topo.engines(src, core)))
-                gone += write(dst, t, lo, hi)
-        if gone:
-            g.wait_ge(sem.sent, gone)
-        return
+    arrive = {"arr%d%s" % (t, "ab"[part]): len(topo.engines(c, core)) for c in plan for t, s, part, dst in plan[c] if dst == core}
     g.sync.dma_start(T.cqs[:], T.cq[:]).then_inc(sem.dcq, 16)
     g.scalar.dma_start(T.pts[:], T.pt[:]).then_inc(sem.dpt, 16)
     g.scalar.dma_start(T.ths[0:8, 0:2], T.th[:]).then_inc(sem.dth, 16)
@@ -824,22 +890,23 @@ def rank_program(g, core, T, topo):
     left = [0]
 
     def send(k):
-        t, lo, hi = SENDS[k]
-        if t <= len(plan[core]):
-            if k and lo == 0:
+        for j in ([k], range(2, len(plan[core])), [])[max(0, min(k - 1, 2))]:
+            t, s, part, dst = plan[core][j]
+            if j and plan[core][j - 1][:2] != (t, s):
                 g.wait_ge(sem.sent, left[0])
-            left[0] += write(*plan[core][t - 1], lo, hi)
+            if s:
+                g.wait_ge(sem["arr%d%s" % (s, "ab"[part])], arrive["arr%d%s" % (s, "ab"[part])])
+            (lo, hi), (rid, pid, _) = PARTS[part], topo.addr(dst)
+            g.remote_dma(T["XL%d" % t][:, lo:hi], T["XL%d" % s][:, lo:hi], sem["arr%d%s" % (t, "ab"[part])], sem.sent, pid, rid,
+                         topo.mask(core, dst))
+            left[0] += len(topo.engines(core, dst))
 
     ops = build(g, T, send)
     if "plan" not in CACHE:
         CACHE["plan"] = schedule(ops)
-    order, deps, start = CACHE["plan"]
+    order, deps, eng = CACHE["plan"]
     Q = {"V": g.vector, "S": g.scalar, "P": g.tensor, "G": g}
     SM = {"V": sem.sV, "S": sem.sS, "P": sem.sP, "G": sem.sG}
-    arrive = {}
-    for t in range(1, n):
-        src = [c for c in plan if (core, t) in plan[c]][0]
-        arrive["arr%da" % t] = arrive["arr%db" % t] = len(topo.engines(src, core))
     count = {"V": 0, "S": 0, "P": 0, "G": 0}
     mark = {}
     wrote = []
@@ -864,20 +931,20 @@ def rank_program(g, core, T, topo):
 
     for i in order:
         o = ops[i]
-        e = o["e"]
+        e = eng[i]
         for x in o["r"]:
             s = outside(x)
             if s:
                 wait(e, s, sem[s], arrive.get(s, 16))
         need = {}
         for d in deps[i]:
-            de = ops[d]["e"]
+            de = eng[d]
             if "late" in ops[d] or de == "P" and e == "P" or de == "G" and "late" in o:
                 continue
             need[de] = max(need.get(de, 0), mark[d])
         for de in sorted(need, key=lambda x: x == e):
             wait(e, de, SM[de], need[de])
-        ins = o["f"]()
+        ins = (o["f"] if e == o["e"] else o["alt"][2])()
         if "late" in o:
             continue
         count[e] += 1
@@ -891,7 +958,8 @@ def rank_program(g, core, T, topo):
     g.wait_ge(sem.sent, left[0])
     ready(g.sync, r("OP"))
     g.sync.dma_start(T.yp[:], T.OP[:]).then_inc(sem.dout, 16)
-    for q, lo, hi in ((g.sync, 0, 2 * CUT), (g.scalar, 2 * CUT, 512)):
+    last = 2 * PIECES[3][-1][0]
+    for q, lo, hi in ((g.sync, 0, last), (g.scalar, last, 512)):
         ready(q, r("OC", lo, hi))
         q.dma_start(T.yc[:, lo:hi], T.OC[:, lo:hi]).then_inc(sem.dout, 16)
     g.sync.wait_ge(sem.dout, 48)

import math
from concourse.mybir import AluOpType, ActivationFunctionType

A = AluOpType
F = ActivationFunctionType
LN2 = math.log(2.0)
XW = 8208
XO = 512
KL = 6 * LN2
RND = 1.5 * 2.0 ** 23

SCRATCH = {}


def _sb(name, cols, dtype):
    SCRATCH[name] = ("sbuf", [128, cols], dtype)


for _i in range(4):
    _sb("XL%d" % _i, XW, "bfloat16")
_sb("PR1", 512, "bfloat16")
for _i in range(8):
    SCRATCH["B%d" % _i] = ("psum", [128, 512], "float32")
for _n, _c, _d in [
    ("cqs", 512, "int32"), ("pts", 32, "int32"), ("ths", 8, "int32"), ("thb", 8, "bfloat16"),
    ("LU", 256, "uint16"), ("PU", 128, "uint16"), ("PF", 128, "float32"), ("PW", 64, "bfloat16"),
    ("NX", 1024, "float32"), ("WF", 528, "bfloat16"), ("TH", 768, "bfloat16"), ("PL", 64, "float16"),
    ("IC", 512, "bfloat16"), ("NAT", 512, "bfloat16"), ("Z", 272, "bfloat16"), ("T5", 16, "bfloat16"),
    ("AW0", 512, "bfloat16"), ("AW1", 512, "bfloat16"), ("AW3", 512, "bfloat16"),
    ("pci", 8, "int32"), ("pcf", 16, "float32"), ("IG", 128, "float32"),
    ("I144", 144, "float32"), ("IL", 64, "float32"),
    ("B0b", 144, "bfloat16"), ("CE", 1024, "float16"), ("HX", 32, "float32"), ("OBb", 128, "bfloat16"),
    ("ONE", 512, "bfloat16"), ("NEG", 128, "bfloat16"), ("RT", 256, "bfloat16"), ("ZR", 128, "bfloat16"),
    ("In", 128, "bfloat16"), ("DG", 16 * 128, "bfloat16"), ("N16", 128, "bfloat16"), ("N8", 128, "bfloat16"), ("sT", 128, "bfloat16"),
    ("O8k", 128, "bfloat16"), ("O2k", 128, "float16"), ("OBm", 128, "bfloat16"), ("PW2", 128, "bfloat16"),
    ("D25", 128, "bfloat16"), ("N35", 128, "bfloat16"), ("MJ", 128, "bfloat16"),
    ("L1", 128, "float16"), ("L2", 128, "float16"), ("BT", 2048, "bfloat16"), ("BM", 144, "bfloat16"),
    ("EX", 512, "bfloat16"), ("FST", 128, "bfloat16"), ("TRI", 128, "bfloat16"),
    ("PK", 128, "bfloat16"), ("PKn", 128, "bfloat16"), ("PK32", 128, "bfloat16"), ("c1", 128, "bfloat16"),
    ("S8", 128, "bfloat16"), ("QN", 256, "float16"), ("E", 4096, "bfloat16"),
    ("ne", 512, "bfloat16"), ("t5", 512, "bfloat16"), ("f5", 512, "float16"),
    ("HL", 64, "float32"), ("tl", 64, "int32"), ("tf", 32, "float32"), ("ti", 128, "int32"), ("PN", 512, "bfloat16"),
    ("CD", 1024, "bfloat16"), ("F16", 128, "bfloat16"), ("K16", 128, "bfloat16"),
    ("QU", 256, "uint16"), ("QH", 256, "float16"), ("YH", 768, "float16"), ("YU", 16, "uint16"),
    ("XY", 256, "bfloat16"), ("XT", 256, "bfloat16"), ("hm", 256, "float32"), ("hi", 256, "int32"),
    ("HU", 256, "uint16"), ("XQ", 4096, "bfloat16"), ("AD", 4096, "float32"), ("CM", 4096, "bfloat16"),
    ("Ns", 256, "float32"), ("Nx", 512, "float32"), ("thr", 256, "float32"),
    ("MT", 1024, "bfloat16"), ("TG", 1024, "bfloat16"),
    ("OH", 4096, "bfloat16"), ("ki", 128, "float32"), ("nh", 256, "bfloat16"), ("cw", 512, "bfloat16"),
    ("cb", 256, "bfloat16"), ("b3", 256, "bfloat16"), ("q", 256, "bfloat16"), ("pj", 256, "bfloat16"),
    ("wA", 256, "bfloat16"), ("wB", 256, "bfloat16"), ("HA", 256, "float16"), ("HB", 256, "float16"),
    ("KP", 256, "bfloat16"), ("pA", 256, "float16"), ("pB", 256, "float16"), ("AB", 256, "float32"),
    ("sc", 16, "float32"), ("cn", 8, "bfloat16"), ("OC", 512, "float32"), ("OP", 32, "float32"),
]:
    _sb(_n, _c, _d)

SEMAPHORES = ["sV", "sS", "sP", "sG", "dcq", "dpt", "dth", "dxs", "dlim", "dout", "sent",
              "arr1a", "arr1b", "arr2a", "arr2b", "arr3a", "arr3b"]

CY = 0.83
PCY = 0.42
GA = 1.56
TWO = ((0, 192, (2, 0), (1, 0), (1, 256), (4, 0), (4, 256)), (192, 256, (6, 0), (5, 0), (5, 128), (0, 0), (0, 128)))
THREE = ((0, 128, (2, 0), (4, 0), (4, 128), (4, 256), (4, 384)), (128, 192, (6, 0), (1, 0), (1, 128), (1, 256), (1, 384)),
         (192, 256, (7, 0), (5, 0), (5, 128), (0, 0), (0, 128)))
PIECES = (TWO, TWO, TWO, THREE)
XM = (2, 4, 6)
CJ = (0,)


def r(name, lo=0, hi=None, st=1, p=None):
    return (name, lo, SCRATCH[name][1][1] if hi is None else hi, st, p, None)


def ind(win, off):
    return win[:5] + (off,)


def cols(x):
    return 16 * cols(x[5]) if x[5] else (x[2] - x[1] + x[3] - 1) // x[3]


def psum(x):
    return SCRATCH[x[0]][0] == "psum"


def narrow(x):
    return SCRATCH[x[0]][2] in ("bfloat16", "float16", "uint16")


def build(g, T, send):
    ops = []
    V, S, P = g.vector, g.scalar, g.tensor

    def ap(x):
        if not isinstance(x, tuple):
            return x
        c = slice(x[1], x[2], x[3]) if x[3] > 1 else slice(x[1], x[2])
        a = T[x[0]][slice(x[4][0], x[4][1]) if x[4] else slice(None), c]
        return a.indirect(ap(x[5])) if x[5] else a

    def op(eng, ns, rd, wr, fn):
        rd = [x for x in rd if isinstance(x, tuple)]
        ops.append({"e": eng, "c": ns, "r": rd + [x[5] for x in rd if x[5]], "w": wr, "f": fn,
                    "g": sum(cols(x) * CY for x in rd if x[5])})

    def vc(out, in0, f):
        if in0[5]:
            return 50 + cols(out) * GA * CY
        return 35 + max(64.0, cols(out) * f) * CY

    def ts(out, in0, s1, s2, o0, o1=None):
        c = vc(out, in0, 0.5 if narrow(out) and narrow(in0) else 1)
        if s2 is None:
            op("V", c, [in0, s1], [out], lambda: V.tensor_scalar(ap(out), ap(in0), ap(s1), None, o0))
        else:
            op("V", c, [in0, s1, s2], [out], lambda: V.tensor_scalar(ap(out), ap(in0), ap(s1), ap(s2), o0, o1))

    def tt(out, in0, in1, o):
        op("V", vc(out, in0, 1 if psum(in0) or psum(in1) else 2), [in0, in1], [out],
           lambda: V.tensor_tensor(ap(out), ap(in0), ap(in1), o))

    def cp(out, in_):
        op("V", vc(out, in_, 0.5 if narrow(out) and narrow(in_) else 1), [in_], [out], lambda: V.tensor_copy(ap(out), ap(in_)))

    def ms(out, val):
        op("V", vc(out, out, 0.5 if narrow(out) else 1), [], [out], lambda: V.memset(ap(out), val))

    def act(out, in_, func, bias=None, scale=None):
        kw = {}
        if bias is not None:
            kw["bias"] = bias
        if scale is not None:
            kw["scale"] = scale
        op("S", 65 + max(64.0, cols(out) * (GA if in_[5] else 1)) * CY, [in_, bias, scale], [out],
           lambda: S.activation(ap(out), ap(in_), func, **{k: ap(v) for k, v in kw.items()}))

    def either(first="V"):
        s, v = ops.pop(), ops.pop()
        a, b = (v, s) if first == "V" else (s, v)
        a["alt"] = (b["e"], b["c"], b["f"])
        ops.append(a)

    def aff(out, in_, scale=None, bias=None, relu=False, first="S"):
        steps = [x for x in ((scale, A.mult), (bias, A.add), (0.0 if relu else None, A.max)) if x[0] is not None]
        if steps:
            ts(out, in_, steps[0][0], steps[1][0] if steps[1:] else None, steps[0][1], steps[1][1] if steps[1:] else None)
        else:
            cp(out, in_)
        act(out, in_, F.Relu if relu else (F.Copy if bias is None else F.Identity), bias, scale)
        either(first)

    def pos(out, in_):
        ts(out, in_, 0.0, None, A.is_gt)
        act(out, in_, F.Sign)
        either("S")

    def mm(items):
        c = 40 + sum(max(64, cols(it[2])) * (1 if narrow(it[2]) else 4) for it in items) * PCY

        def fn():
            last = None
            for it in items:
                last = P.matmul(ap(it[0]), ap(it[1]), ap(it[2]), it[3], it[4])
            return last
        op("P", c, [it[1] for it in items] + [it[2] for it in items], [it[0] for it in items], fn)
        ops[-1]["s"] = (items[0][0][0], items[0][3], items[-1][4])

    def acc(out, terms, start=True, stop=True):
        return [(out, a, b, start and i == 0, stop and i == len(terms) - 1) for i, (a, b) in enumerate(terms)]

    def io(out, pat, base, ch, flt=True):
        if flt:
            op("G", 130 + 2 * cols(out) * CY, [], [out], lambda: g.iota(ap(out), pat, base, ch, allow_small_or_imprecise_dtypes=True))
        else:
            op("G", 130 + 2 * cols(out) * CY, [], [out], lambda: g.iota(ap(out), pat, base, ch))

    def sel(out, in_, pat, cmp, fill, base, ch):
        op("G", 170 + 2 * cols(out) * CY, [in_], [out], lambda: g.affine_select(ap(out), ap(in_), pat, cmp, fill, base, ch))

    def diag(name, v, off="ZR"):
        sel(r(name), r(off), [[1, 128]], A.not_equal, v, 0, -1)

    def B(k, lo=0, hi=512, st=1):
        return r("B%d" % k, lo, hi, st)

    def blk(name, i, w=128):
        return r(name, w * i, w * i + w)

    def DG(j):
        return blk("DG", j)

    pcol, gcol, kcol, p32, g16, k0, kln, kn, kz, kh = [r("pcf", i, i + 1) for i in range(10)]
    Ib, In, OBb, ONb = DG(0), r("In"), r("OBb"), r("ONE", 0, 128)

    io(r("pci", 0, 1), [[0, 1]], 0, 1, False)
    io(r("IG"), [[1, 8], [0, 16]], 0, 0)
    io(r("I144"), [[1, 144]], -15, 0)
    io(r("IC", 0, 272), [[1, 272]], -256, 0)
    io(r("IC", 272, 512), [[1, 240]], 16, 0)
    io(r("IL"), [[XO, 2], [16, 32]], 0, 0)
    io(blk("AW0", 1, 256), [[1, 256]], 0, 0)
    io(blk("NX", 3, 256), [[0, 256]], 0, 0)
    io(r("T5", 0, 3), [[4, 3]], 0, 0)
    io(r("T5", 3, 16), [[-4, 13]], 4, 0)
    ms(r("XL0", 8192, XW), 0.0)
    ms(r("ONE"), 1.0)
    ms(r("NEG"), -1.0)
    ms(r("RT"), RND)
    ms(r("ZR"), 0.0)
    ms(r("cn", 2, 3), 0.25)
    io(r("EX"), [[1, 32], [0, 16]], 0, 0)
    ts(r("pci", 1, 2), r("pci", 0, 1), 4, None, A.arith_shift_right)
    ts(r("pci", 2, 3), r("pci", 0, 1), 15, None, A.bitwise_and)
    ts(r("pci", 3, 4), r("pci", 0, 1), 31, None, A.bitwise_and)
    cp(r("pcf", 0, 4), r("pci", 0, 4))
    ts(r("EX"), r("EX"), p32, None, A.is_equal)
    aff(g16, gcol, 16.0)
    act(k0, kcol, F.Relu, scale=-1.0, bias=1.0)
    aff(kn, kcol, -65536.0)
    aff(kln, kcol, LN2)
    ts(kz, pcol, g16, -240.0, A.add, A.add)
    ts(OBb, r("IG"), gcol, None, A.is_equal)
    ts(Ib, r("I144", 15, 143), pcol, None, A.is_equal)
    for q in range(4):
        sel(blk("BT", q, 512), r("ONE"), [[-1, 4], [-16, 8], [0, 16]], A.is_equal, 0.0, -4 * q, 1)
    for j in (1, 2, 4, 8):
        aff(r("DG", 128 * j, 256 * j), r("DG", 0, 128 * j), 2.0 ** j)
    for nm, v in (("In", -1.0), ("K16", kn), ("L2", 3232.0)):
        aff(r(nm), Ib, v)
    diag("N16", -16.0)
    diag("N8", -8.0)
    for nm, v in (("OBm", -1.0), ("O2k", 2047.0), ("O8k", 8192.0), ("MJ", 12.0)):
        aff(r(nm), OBb, v)
    aff(r("L1"), blk("BT", 0), 2080.0)
    ts(r("BM"), r("I144"), g16, None, A.is_equal)
    ts(r("B0b"), r("I144"), pcol, k0, A.is_equal, A.mult)
    for v in range(2):
        ts(blk("Z", v, 136), r("IC", v, 272, 2), kz, None, A.is_equal)
    sel(r("c1"), OBb, [[1, 128]], A.is_gt, 0.0, 0, -1)
    diag("FST", -16.0, "c1")
    aff(r("F16"), r("FST"), 65536.0)
    mm(acc(B(5, 128, 256), [(DG(6), r("c1")), (r("c1"), Ib), (DG(1), r("N16"))]))
    aff(r("TRI"), B(5, 128, 256), 1.0 / 32)
    act(r("WF", 512, 528), r("ZR", 0, 16), F.Exp, bias=kln)
    ops[-1]["c"] += 1300
    act(kh, kln, F.Exp, scale=-1.0, bias=-LN2)
    ops[-1]["r"].append(r("WF", 512, 528))
    aff(r("PKn"), Ib, kh)
    mm([(B(5, 256, 384), OBb, r("PKn"), True, True)])
    aff(r("PK"), B(5, 256, 384))
    aff(r("PK32"), r("PK"), 1.0 / 32)
    aff(r("PKn"), r("PK"), -1.0)
    ts(r("PW2"), OBb, r("WF", 512, 513), None, A.mult)
    aff(r("IL"), r("IL"), None, kcol)
    ts(r("S8", p=(0, 8)), r("IG", p=(0, 8)), r("pcf", 0, 1, p=(0, 8)), None, A.is_equal)
    cp(r("thb", 0, 2, p=(0, 8)), r("ths", 0, 2, p=(0, 8)))
    mm([(B(7, 0, 2), r("S8", p=(0, 8)), r("thb", 0, 2, p=(0, 8)), True, True)])
    aff(r("XL0", 8192, 8193), B(7, 0, 1), 0.5)
    aff(r("XL0", 8193, 8194), B(7, 1, 2), None, -128.0)

    for k, (t, lo, hi) in enumerate(SENDS):
        op("G", 300 if k else 3000, [r("XL0", 0, 4096), r("XL0", 4096, 8192), r("XL0", 8192, XW)],
           [r("XL%d" % t, lo, hi), r("ths", 4, 5)], lambda k=k: send(k))
        ops[-1]["late"] = SEND * (0.75, 1.25, 0.5)[min(k, 2)]
        ops[-1]["pair"] = k == 1
        if k == 1:
            io(blk("AW1", 0, 256), [[1, 256]], -256, 0)
            diag("MJ", 76.0, "MJ")
            diag("N35", -35.0)
            diag("D25", 2.5)
            io(r("NAT"), [[1, 2], [2, 256]], -256, 0)
            io(blk("AW3", 0, 256), [[2, 256]], -256, 0)

    NW = r("NX", 0, 512)
    for h in range(2):
        aff(blk("CE", 2 * h, 256), r("cqs", h, 512, 2), None, -2048.0, first="V")
        aff(blk("CE", 2 * h + 1, 256), blk("CE", 2 * h, 256))
        aff(blk("NX", h, 256), r("cqs", h, 512, 2), -1.0, 4095.0, first="V")
        pos(blk("ne", h, 256), blk("NX", h, 256))

    def lists(t):
        o = B((6, 3)[t], 0, 32)
        if t == 0:
            aff(r("PL", 32, 64), r("pts"))
            mm([(B(7, 16, 32), r("Z", 8 - 8 * u, 136 - 8 * u), r("PL", 32 + u, 64, 2), u == 0, u == 1) for u in range(2)])
            aff(r("YU"), B(7, 16, 32), first="V")
            a = blk("ti", 0, 32)
            ts(a, r("pts"), 1, None, A.bitwise_and)
            ts(a, a, 511.0, None, A.mult)
            tt(r("PL", 0, 32), a, r("pts"), A.add)
            mm([(blk(o[0], v, 16), r("Z", 136 * v + 8 - 8 * u, 136 * v + 136 - 8 * u), r("PL", u, 32, 2), u == 0, u == 1)
                for v in range(2) for u in range(2)])
        else:
            mm([(o, r("B0b", 15 - w, 143 - w), r("PR1", w, 512, 16), w == 0, w == 15) for w in range(16)])
        aff(blk("PU", t, 32), o, *((None, 256.0) if t else (0.5, None)), first="V")
        aff(blk("PF", t, 32), o, *((None, 256.0) if t else (0.5, None)))

    def compare(h):
        sb = 3 + 2 * h
        qn = r("QN") if h else r("QH")
        if h:
            aff(qn, ind(NW, blk("PU", h, 16)), -1.0, 2047.0)
        else:
            aff(qn, ind(r("cqs"), r("YU")), None, -2048.0, first="V")
        for n in range(8):
            bk, eb = (0, 1, 2, 4)[n % 4], 4 * h + n % 4
            mm([(B(bk, 256 * i, 256 * i + 256), blk("BT", 2 * n + i), qn, True, True) for i in range(2)])
            tt(blk("E", eb, 512), B(bk), blk("CE", h, 512), A.is_equal)
            mm([(B(sb, 0, 256), DG(2 * n + i), blk("E", 2 * eb + i, 256), n + i == 0, n + i == 8) for i in range(2)])
        tt(blk("t5", h, 256), B(sb, 0, 256), blk("ne", h, 256), A.is_lt)
        tt(blk("WF", h, 256), B(sb, 0, 256), blk("ne", h, 256), A.mult)

    def tops(h):
        mm([(B(6, 0, 16), r("BM", 15 - w, 143 - w), r("t5", 256 * h + w, 256 * h + 256, 16), w == 0, w == 15) for w in range(16)])
        pos(blk("HL", h, 16), B(6, 0, 16))
        aff(blk("HL", 2 + h, 16), blk("HL", h, 16), (-512.0, 512.0)[h], (768.0, 0.0)[h])
        tt(blk("HX", h, 16), blk("IL", 2 + h, 16), blk("HL", h, 16), A.mult)
        o = B(7, 0, 256)
        mm([(o, r("FST"), blk("t5", h, 256), True, True)])
        ts(o, o, -15.5, None, A.is_lt)
        act(o, o, F.Relu, bias=-15.0, scale=-1.0)
        either("S")
        tt(blk("f5", h, 256), o, blk("CE", 2 * h, 256), A.mult)
        mm([(o, OBb, blk("f5", h, 256), True, True)])
        aff(r("NX", XO + 256 * h, XO + 256 * h + 256), o, -1.0, 2047.0)

    def chain(t):
        par = t & 1
        PF, il = blk("PF", 2 * t + par, 16), blk("IL", par, 16)
        ly, x1, kind, e = [blk("tl", i, 16) for i in range(4)]
        tt(e, PF, blk("HL", 2 + par, 16), A.add)
        aff(x1, e, 1024.0, (-1023.5, -255.5)[par] * 1024, first="V")
        tt(x1, x1, PF, (A.min, A.max)[par])
        tt(x1, x1, il, (A.max, A.min)[par])
        tt(ly, PF, blk("HX", par, 16), A.max)
        ts(kind, e, 8, None, A.arith_shift_right)
        aff(blk("LU", t, 48), blk("tl", 0, 48), first="V")
        aw = "AW3" if t == 3 else "AW%d" % par
        aff(blk(aw, par, 256), ind(r("NAT" if t == 3 else "IC"), blk("LU", 3 * t + 1, 16)))
        aff((r("PR1"), r("YH", 256), r("YH", 256), r("PN"))[t], ind(r(aw), blk("PU", t, 32)))
        aff(blk("CD", t, 256), ind(r("T5"), blk("LU", 3 * t + 2, 16)))

    def parents_out():
        mm([(B(6, 64, 96), r("B0b", 15 - w, 143 - w), r("PN", 256 * (w & 1) + (w >> 1), 256 * (w & 1) + 256, 8), w == 0, w == 15)
            for w in range(16)])
        aff(r("OP"), B(6, 64, 96), None, 256.0)

    def hop(t):
        n = 16 if t else 32
        a, b, x, u = [r(nm, lo, lo + n) for nm, lo in (("PF", 48 * t), ("PF", 32 + 48 * t), ("tf", 0), ("LU", 192 + 32 * t))]
        tt(x, a, b, A.is_equal)
        aff(x, x, 512.0)
        tt(x, x, a, A.max)
        aff(u, x, first="V")
        aff(r("TH", 512 * t, 512 * t + 16 * n), ind(r("WF"), u))

    def bit(o, src):
        n = cols(o)
        return acc(o, [(r("PK32"), r("ONE", 0, n)), (r("PK"), src), (Ib, r("RT", 0, n)), (In, r("RT", 0, n)), (r("PKn"), src)])

    def carry(out, o, src, th, first):
        mm(bit(o, src))
        aff(o, o, 2.0 ** 34, None, True, first)
        tt(out, o, th, A.min)

    def frames():
        mm([(B(2, 128 * k, 128 * k + 128), blk("PR1", k), OBb, True, True) for k in range(4)])
        aff(blk("TG", 0, 512), B(2), None, 8.0, True)
        ts(blk("TG", 1, 512), blk("TG", 0, 512), 0.0, 8.0, A.is_equal, A.mult)
        act(blk("TG", 1, 512), blk("TG", 0, 512), F.Relu, scale=-1.0, bias=8.0)
        either()
        for h in range(2):
            bk = 4 + 3 * h
            carry(blk("cw", h, 256), B(bk, 0, 256), blk("WF", h, 256), blk("TH", h, 256), "S")
            its = []
            for k in range(2):
                c, rt = blk("cw", 2 * h + k), r("RT", 0, 128)
                its += acc(B(bk, 256 + 128 * k, 384 + 128 * k), [(ONb, r("PK32")), (c, r("PK")), (Ib, rt), (In, rt), (c, r("PKn"))])
            mm(its)
            for par in range(2):
                tt(blk("MT", 2 * par + h, 256), B(bk, 256, 512), blk("TG", 2 * par + h, 256), A.is_gt)

    def onehot():
        mm([(B(7, 8 * k, 8 * k + 8), blk("PR1", k), r("B0b", 15, 143, 16), True, True) for k in range(4)])
        a, b, d = [blk("ti", i, 32) for i in range(3)]
        aff(a, B(7, 0, 32), None, 256.0, first="V")
        ts(b, a, 128, None, A.bitwise_and)
        ts(d, a, 127, None, A.bitwise_and)
        aff(blk("PW", 0, 32), d)
        aff(blk("PW", 1, 32), b, 1023.0 / 128, 1.0)
        for q in range(8):
            for k in range(4):
                i = 8 * k + q
                ts(blk("OH", i), blk("IC", 2), r("PW", i, i + 1), r("PW", 32 + i, 33 + i), A.is_equal, A.mult)

    def head(t):
        if t:
            aff(r("QU"), ind(NW, blk("PU", 2 * t + (t & 1), 16)), -1.0, 4095.0, first="V")
        else:
            aff(r("QU"), r("QH"), None, 2048.0, first="V")
        YH = r("YH", 0, 256)
        aff(YH, ind(r("NX"), blk("LU", 3 * t, 16)), -1.0, 2047.0, first="V")
        n = 48 if t in (1, 2) else 16
        mm([(B(6, 0, n), r("B0b", 15 - w, 143 - w), r("YH", w, 16 * n, 16), w == 0, w == 15) for w in range(16)])
        aff(r("YU"), B(6, 0, 16), None, 2048.0, first="V")
        if n > 16:
            aff(blk("PU", t + 1, 32), B(6, 16, 48), None, 256.0, first="V")
            aff(blk("PF", t + 1, 32), B(6, 16, 48), None, 256.0)
        if t:
            aff(r("QH"), r("QU"), None, -2048.0, first="V")
        mm([(B(5, 0, 256), blk("BT", 0), YH, True, True)] + acc(B(5, 256, 512), [(r("L1"), YH), (r("L2"), r("QH"))]))
        tt(r("hm"), B(5, 0, 256), r("QH"), A.mult)
        tt(r("hi"), B(5, 256, 512), r("hm"), A.add)
        ts(r("hi"), r("hi"), 5, 4095, A.arith_shift_right, A.bitwise_and)
        aff(r("HU"), r("hi"), first="V")
        aff(r("XY"), ind(r("XL%d" % t, 0, 4096), r("YU")))
        mm([(B(6, 256 + 128 * h, 384 + 128 * h), blk("XY", h), In, True, True) for h in range(2)])
        aff(r("XT"), B(6, 256, 512))

    def scores(t):
        XL = "XL%d" % t
        for n in range(8):
            xq, bk = blk("XQ", n, 512), B((0, 5, 1)[n % 3])
            rows = (32 * (n % 4), 32 * (n % 4) + 32)
            if n - 1 not in XM:
                m = n + 1 + (n in XM)
                aff(r("XQ", 512 * n, 512 * m), ind(r(XL, 0, 4096), r("QU", 32 * n, 32 * m)), first="V" if t and n == 1 else "S")
            mm(acc(bk, [(Ib, xq), (r("XT", 128 * (n // 4), 128 * (n // 4) + 128, p=rows), r("EX", p=rows))]))
            act(blk("AD", n, 512), bk, F.Abs)
            if n not in CJ:
                m = n - (n - 1 in CJ)
                tt(r("CM", 512 * m, 512 * n + 512), ind(r(XL, 4096, 8192), r("HU", 32 * m, 32 * n + 32)),
                   r("AD", 512 * m, 512 * n + 512), A.is_ge)

    def own(t):
        par = t & 1
        o = B(2, 192, 448)
        if t > 1:
            pos(blk("ne", par, 256), blk("NX", par, 256))
        mm([(o, DG(11), blk("CD", t, 256), True, True)])
        tt(blk("Nx", par, 256), o, blk("NX", par, 256), A.min)

    def members():
        o = B(7, 0, 256)
        mm([it for f in range(2) for it in acc(B(7, 128 * f, 128 * f + 128), [(blk("MT", 2 + f), Ib), (blk("MT", 6 + f), Ib)])])
        tt(r("cw", 256, 512), o, blk("TH", 2, 256), A.mult)
        mm(bit(o, r("cw", 256, 512)))
        ts(r("b3"), o, 0.0, None, A.is_gt)

    def masks(t):
        par = t & 1
        XL = "XL%d" % t
        cd, W = blk("CD", t, 256), blk("WF", par, 256)
        ts(r("q"), r("QU"), 4095.0, None, A.is_lt)
        act(r("q"), r("QU"), F.Sign, scale=-1.0, bias=4095.0)
        either()
        aff(r("Ns"), ind(NW, blk("LU", 3 * t + 1, 16)))
        for i, k in enumerate((0, 1, 2, 3) if par == 0 else (2, 3, 0, 1)):
            mm([(B(3, 256 + 16 * q, 272 + 16 * q), blk("OH", 8 * k + q), blk("MT", 32 * par + 8 * k + q, 16), i + q == 0, i + q == 10)
                for q in range(8)])
        ts(r("ki"), B(3, 256, 384), 1024.0 * RND, -1024.0 * RND, A.add, A.add)
        tt(blk("nh", 0), B(3, 256, 384), r("ki"), A.not_equal)
        pos(blk("nh", 1), r("ki"))
        mm([(B(3, 0, 256), In, r("QH"), True, True)])
        o = B(7, 256, 512)
        mm([it for f in range(2)
            for it in acc(B(7, 256 + 128 * f, 384 + 128 * f), [(Ib, blk("ne", 2 * par + f)), (blk("nh", f), In)])])
        cw = r("cw", 0, 256)
        tt(cw, o, W, A.mult)
        for th in ((), (), (0,), (1, 2))[t]:
            carry(cw, o, cw, blk("TH", th, 256), "V")
        mm(bit(o, cw))
        act(r("cb"), o, F.Sign, scale=-1.0, bias=2.0 ** -18)
        o = B(4, 0, 256)
        its = []
        for f in range(2):
            held = (r("N16"), blk("b3", f)) if t == 3 else (blk("MT", 4 - 2 * par + f), r("N16"))
            its += acc(B(4, 128 * f, 128 * f + 128),
                       [held, (DG(4), blk("q", f)), (r("OBm"), blk("ne", 2 * par + f)), (DG(2), blk("CD", 2 * t + f))])
        mm(its)
        act(r("pj"), o, F.Sign, bias=-32.5)
        o = B(4, 256, 512)
        mm(acc(o, [(r("N16"), cd), (DG(6), r("q")), (DG(4), r("cb"))]))
        aff(r("thr"), o, None, r(XL, 8193, 8194))
        th1 = r(XL, 8192, 8193)
        if t:
            cn, rt = r("cn", 0, 1), r("RT", 0, 1)
            aff(cn, B(2, 384, 385), 0.5)
            mm(acc(B(2, 386, 387), [(Ib, r("cn", 2, 3)), (r("NEG"), cn), (Ib, rt), (In, rt), (ONb, cn), (Ib, th1)]))
            th1 = B(2, 386, 387)
        aff(r("sc", 2, 3), th1, -2 * KL, -16.0 * KL - 48 * LN2)

    def piece(t, f):
        par = t & 1
        lo, hi = PIECES[t][f][:2]
        n, d = hi - lo, 256 * par
        v, ta, tb, z, y = [B(k, c, c + n) for k, c in PIECES[t][f][2:]]
        wA, wB, KP, cb, HA, HB, pA, pB, AB = [r(x, lo, hi) for x in ("wA", "wB", "KP", "cb", "HA", "HB", "pA", "pB", "AB")]
        cd, Q = r("CD", 256 * t + lo, 256 * t + hi), B(3, lo, hi)
        sums = [acc(r(v[0], 64 * k - lo, 64 * k + 64 - lo), [(r("BM", 15 - j, 143 - j), r("CM", 1024 * k + j, 1024 * k + 1024, 16))
                                                             for j in range(16)], False, f > 0 and k == hi // 64 - 1)
                for k in range(lo // 64, hi // 64)]
        if f == 0:
            mm([(B(6, 128 + j, 256, 16), r("CM", j, 2048, 16), r("BM", 15, 143, 16), j == 0, j == 15) for j in range(16)])
            aff(r("sT"), B(6, 128, 256))
            sums[:2] = [[(r(v[0], 0, 128), r("sT"), Ib, False, False)]]
        sums.insert(len(sums) - (f > 0), [(v, DG(4), cb, False, f == 0)])
        mm(acc(v, [(DG(6), r("pj", lo, hi)), (r("N8"), cd)], stop=False))
        for its in sums:
            mm(its)
        act(wA, v, F.Exp, scale=KL, bias=r("sc", 2, 3))
        act(wB, v, F.Exp, scale=-KL, bias=48 * LN2 - 144 * KL)
        tt(KP, v, r("thr", lo, hi), A.is_le)
        mm([(ta, r("TRI"), wA, True, True)])
        mm([(tb, r("TRI"), wB, True, True)])
        ts(HA, ta, -2.0 ** -50, None, A.is_lt)
        tt(pA, Q, HA, A.mult)
        ts(HB, tb, -2.0 ** -50, None, A.is_lt)
        tt(pB, Q, HB, A.mult)
        mm(acc(y, [(r("F16"), r("ne", d + lo, d + hi)), (r("K16"), r("ONE", 0, n)), (r("O2k"), HA), (OBb, pA)]))
        mm(acc(z, [(In, KP), (r("O8k"), HA), (r("O2k"), HB)], stop=False))
        mm(acc(z, [(OBb, pB)], start=False))
        tt(AB, y, r("Ns", lo, hi), A.max)
        tt(z, z, r("Nx", d + lo, d + hi), A.not_equal)
        if t < 3:
            tt(r("NX", d + lo, d + hi), z, AB, A.mult)
        else:
            tt(z, z, AB, A.mult)
            aff(r("OC", 2 * lo + 1, 2 * hi, 2), z, -1.0, 4095.0)

    def after(t):
        par = t & 1
        for f in range(2):
            mm(acc(B(7, 128 * f, 128 * f + 128),
                   [(DG(6), blk("MT", 4 - 2 * par + f)), (blk("cb", f), DG(3)), (blk("CD", 2 * t + f), DG(2))]
                   + ([(blk("CD", f), r("D25"))] if t == 2 else [])
                   + [(blk("KP", f), DG(7)), (blk("HA", f), r("MJ")), (blk("HB", f), r("N35"))]))
        ts(blk("MT", 2 - par, 256), B(7, 0, 256), 74.0 if t == 2 else 64.0, None, A.is_gt)
        mm(acc(B(2, 384, 385), [(blk("HA", f), r("ONE", 0, 1)) for f in range(2)]))

    def weights(t):
        o = B(1, 256, 512)
        mm(acc(o, [(r("F16"), blk("ne", t, 256)), (r("K16"), r("ONE", 0, 256)), (r("PW2"), r("HA"))]))
        tt(blk("WF", t, 256), o, blk("WF", t, 256), A.max)

    lists(0)
    compare(0)
    tops(0)
    chain(0)
    compare(1)
    head(0)
    lists(1)
    onehot()
    tops(1)
    hop(0)
    frames()
    own(0)
    for t in range(4):
        if t > 0:
            head(t)
        masks(t)
        scores(t)
        if t == 2:
            hop(1)
            members()
        if t < 3:
            chain(t + 1)
        for f in range(len(PIECES[t])):
            piece(t, f)
            if f == 0 and t < 3:
                own(t + 1)
        if t < 3:
            after(t)
        if t < 2:
            weights(t)
        if t == 2:
            parents_out()
            aff(r("OC", 0, 512, 2), blk("NX", 0, 256), -1.0, 4095.0)
    return ops


EXT = {"dcq": 2600, "dpt": 2300, "dth": 2400, "dxs": 14000, "dlim": 18000}
SEND = 13000.0
PARTS = ((0, 4096), (4096, XW))
SENDS = [(t, lo, hi) for t in (1, 2, 3) for lo, hi in PARTS]


def outside(x):
    n = x[0]
    if n in ("cqs", "pts", "ths"):
        return {"cqs": "dcq", "pts": "dpt", "ths": "dth"}[n]
    if n == "XL0":
        return "dxs" if x[1] < 4096 else ("dlim" if x[1] < 8192 else None)
    return "arr" + n[2] + "ab"[x[1] >= 4096] if n[:2] == "XL" else None


def meet(a, b):
    if a[2] <= b[1] or b[2] <= a[1]:
        return False
    return not (a[3] == b[3] > 1 and (a[1] - b[1]) % a[3])


def links(ops, banks):
    seen = {}
    deps, below = [], []
    for i, o in enumerate(ops):
        d = set()
        use = [(x, False) for x in o["r"]] + [(x, True) for x in o["w"]]
        for x, w in use:
            for j, y, v in seen.get(x[0], []):
                if (w or v) and meet(x, y) or banks and psum(x):
                    d.add(j)
        for x, w in use:
            seen.setdefault(x[0], []).append((i, x, w))
        if o["e"] == "G":
            d.update(j for j in range(i) if ops[j]["e"] == "G" and ("late" in o or "late" in ops[j]))
        d.discard(i)
        keep, cover = [], 0
        for j in sorted(d, reverse=True):
            if not cover >> j & 1:
                keep.append(j)
                cover |= below[j] if "late" not in ops[j] else 0
        deps.append(keep)
        below.append(cover | 1 << i)
    return deps


def schedule(ops):
    deps = links(ops, False)
    banks = [sorted(set(int(x[0][1]) for x in o["r"] + o["w"] if psum(x))) for o in ops]
    seq, eng = arrange(ops, deps, banks)
    last = {}
    for i in seq:
        for b in banks[i]:
            if b in last and eng[last[b]] != eng[i] and last[b] not in deps[i]:
                deps[i].append(last[b])
            last[b] = i
    return seq, deps, ["VSPG"[e] for e in eng]


CACHE = {}
CASES = ((1.56, 220.0, 1.0), (1.9, 100.0, 1.0), (1.1, 150.0, 1.1))
SWEEPS = 20
WIDE = 150
STEPS = 2700
HEAT = 300.0
EARLY = 0.002
SEED = 1


def arrange(ops, deps, banks):
    n = len(ops)
    eng = ["VSPG".index(o["e"]) for o in ops]
    rel = [min(max([EXT.get(outside(x), 0.0) for x in o["r"]] + [0.0]), SEND if o["e"] == "G" else 1e9) for o in ops]

    def edges(deps):
        fore = [[(d, ops[d].get("late", 0.0) if o["e"] != "G" or not o.get("pair", True) else 0.0) for d in deps[i]]
                for i, o in enumerate(ops)]
        aft = [[] for _ in ops]
        for i in range(n):
            for d, w in fore[i]:
                aft[d].append((i, w))
        return fore, aft
    cases = []
    for ga, lat, pe in CASES:
        cost = []
        for o in ops:
            c = [(o["c"] + o["g"] * (ga - GA)) * (pe if o["e"] == "P" else 1.0)] * 4
            if "alt" in o:
                c["VSPG".index(o["alt"][0])] = o["alt"][1] + o["g"] * (ga - GA)
            cost.append(c)
        cases.append((cost, [[0.0 if a == b == 2 else (0.5 * lat if a == b else lat) for a in range(4)] for b in range(4)], lat))
    cost, gap = cases[0][:2]
    fore, aft = edges(links(ops, True))
    way = [0.0] * n
    for i in range(n - 1, -1, -1):
        way[i] = cost[i][eng[i]] + max([way[s] + w + gap[eng[s]][eng[i]] for s, w in aft[i]] + [0.0])
    seq = justify(sorted(range(n), key=lambda i: (-way[i], i)), fore, aft, eng, cost, gap, rel)
    fore, aft = edges(deps)

    def run(part, end, by, last, case):
        cost, gap, lat = case
        for i in part:
            e, t, u = eng[i], rel[i], -1
            ge = gap[e]
            for d, w in fore[i]:
                x = end[d] + w + ge[eng[d]]
                if x > t:
                    t, u = x, d
            d = last[e]
            if end[d] > t:
                t, u = end[d], -2 - d
            for b in banks[i]:
                d = last[4 + b]
                if end[d] + lat > t and eng[d] != e:
                    t, u = end[d] + lat, -2 - d
                last[4 + b] = i
            end[i] = t + cost[i][e]
            by[i], last[e] = u, i

    def rest(part, case):
        cost, gap, lat = case
        way, nxt = [0.0] * n + [0.0, -1e9], [n, n, n] + [n + 1] * 9
        for i in reversed(part):
            e = eng[i]
            t = way[nxt[e]]
            for s, w in aft[i]:
                t = max(t, w + gap[eng[s]][e] + way[s])
            for b in banks[i]:
                if eng[nxt[4 + b]] != e:
                    t = max(t, lat + way[nxt[4 + b]])
                nxt[4 + b] = i
            way[i], nxt[e] = t + cost[i][e], i
        return way, nxt

    def clash(part, held):
        for i in part:
            if eng[i] == 2:
                b, start, stop = ops[i]["s"]
                if start and b in held:
                    return True
                (held.discard if stop else held.add)(b)
        return False

    bounds = set(i for i in range(n) if eng[i] == 2 and ops[i]["s"][1] != ops[i]["s"][2])
    eng += [-1, -1]
    rnd = SEED
    for sweep in range(SWEEPS):
        for lo in range(-(sweep * 37 % (WIDE // 2)), n - WIDE // 2, WIDE // 2):
            lo, hi = max(lo, 0), min(lo + WIDE, n)
            end = [0.0] * n + [-1e9]
            run(seq, end, [-1] * n, [n] * 12, cases[0])
            at = {i: p for p, i in enumerate(seq)}
            seq.sort(key=lambda i: (end[i] - cost[i][eng[i]], at[i]))
            inside, held = set(seq[lo:hi]), set()
            clash(seq[:lo], held)
            now, out = [], []
            for c in cases:
                end, by, last = [0.0] * n + [-1e9], [-1] * n, [n] * 12
                run(seq[:lo], end, by, last, c)
                way, nxt = rest(seq[hi:], c)
                far = [(i, [max(w + c[1][eng[s]][e] + way[s] for s, w in aft[i] if s not in inside) for e in range(4)])
                       for i in seq[lo:hi] if any(s not in inside for s, w in aft[i])]
                now.append((end, by, 0.0))
                out.append((last, [(way[s], eng[s]) for s in nxt], far))

            def judge(new, a, old, room=1e18):
                res, total = [], 0.0
                last0 = list(out[0][0])
                for i in new[lo:a]:
                    last0[eng[i]] = i
                    for b in banks[i]:
                        last0[4 + b] = i
                part = new[a:hi]
                for c, x, (last, nxt, far) in zip(cases, old, out):
                    end, by, last = list(x[0]), list(x[1]), list(last0)
                    run(part, end, by, last, c)
                    t, j = max((end[i] + w + (c[2] if k > 3 and eng[i] != e else 0.0), i) for k, (i, (w, e)) in enumerate(zip(last, nxt)))
                    for i, y in far:
                        if end[i] + y[eng[i]] > t:
                            t, j = end[i] + y[eng[i]], i
                    t += EARLY * sum([end[i] for i in inside])
                    if t - room > x[-1]:
                        return None, 1e18
                    res.append((end, by, j, t))
                    total += t
                return res, total
            now, total = judge(seq, lo, now)
            best, keep = total, (seq, list(eng))
            for k in range(STEPS):
                end, by, j = now[k % len(now)][:3]
                pairs = []
                while j in inside:
                    b = by[j]
                    if b <= -2:
                        b = -2 - b
                        if b in inside:
                            pairs.append((b, j))
                    j = b
                if not pairs:
                    continue
                rnd = (rnd * 1103515245 + 12345) % 2147483648
                u, v = pairs[(rnd >> 8) % len(pairs)]
                a, b = seq.index(u, lo), seq.index(v, lo)
                rnd = (rnd * 1103515245 + 12345) % 2147483648
                step, kind, flip = (0, 0, 1, 2, 4, 8, 16)[(rnd >> 8) % 7], rnd >> 20 & 7, -1
                if kind < 2 and "alt" in ops[(u, v)[kind]]:
                    flip, a = (u, v)[kind], (a, b)[kind]
                    p = q = a
                    while rnd >> 23 & 1 and p > lo and all(seq[p - 1] != d for d, w in fore[flip]):
                        p -= 1
                    while rnd >> 23 & 1 and q < hi - 1 and all(seq[q + 1] != s for s, w in aft[flip]):
                        q += 1
                    p += (rnd >> 4) % (q - p + 1)
                    new = seq[:a] + seq[a + 1:]
                    new.insert(p, flip)
                    a = min(a, p)
                    eng[flip] = 1 - eng[flip]
                else:
                    if kind & 1:
                        while step and a > lo:
                            a -= 1
                            step -= eng[seq[a]] == eng[v]
                        go = {v}
                        for x in reversed(seq[a:b]):
                            if any(s in go for s, w in aft[x]):
                                go.add(x)
                    else:
                        while step and b < hi - 1:
                            b += 1
                            step -= eng[seq[b]] == eng[u]
                        go = {u}
                        for x in seq[a + 1:b + 1]:
                            if any(s in go for s, w in fore[x]):
                                go.add(x)
                        go = set(seq[a:b + 1]) - go
                    new = seq[:a] + [x for x in seq[a:b + 1] if x in go] + [x for x in seq[a:b + 1] if x not in go] + seq[b + 1:]
                    if not bounds.isdisjoint(seq[a:b + 1]) and clash(new[lo:b + 1], set(held)):
                        continue
                rnd = (rnd * 1103515245 + 12345) % 2147483648
                room = -(HEAT * (1.0 - k / STEPS) + 5.0) * math.log(((rnd >> 8) + 1) / 8388608.0)
                then, t = judge(new, a, now, room + 300.0)
                if t <= total + room:
                    total, now, seq = t, then, new
                    if t < best:
                        best, keep = t, (seq, list(eng))
                elif flip >= 0:
                    eng[flip] = 1 - eng[flip]
            seq = list(keep[0])
            eng[:] = keep[1]
    ends = []
    for c in cases:
        end, last = [0.0] * n + [-1e9], [n] * 12
        run(seq, end, [-1] * n, last, c)
        ends.append((max(end[i] for i in last[:3]), [end[i] - c[0][i][eng[i]] for i in range(n)]))
    CACHE["ends"] = ends
    return seq, eng[:n]


def justify(seq, fore, aft, eng, cost, gap, rel):
    n = len(seq)
    for k in range(13):
        pre = aft if k & 1 else fore
        line = [[], [], [], []]
        end = [0.0] * n
        for i in seq:
            e, t = eng[i], 0.0 if k & 1 else rel[i]
            c = cost[i][e]
            for d, w in pre[i]:
                t = max(t, end[d] + w + gap[e][eng[d]])
            ln, p = line[e], 0
            while p < len(ln) and ln[p][0] < t + c:
                t = max(t, ln[p][1])
                p += 1
            ln.insert(p, (t, t + c))
            end[i] = t + c
        seq = sorted(seq, key=lambda i: -end[i])
    return sorted(range(n), key=lambda i: (end[i] - cost[i][eng[i]], i))


def routes(T, topo):
    n = len(T.cores)
    plan = {c: [] for c in T.cores}
    for a, src in enumerate(T.cores):
        need = [(T.cores[(a - t) % n], t) for t in range(1, n)]
        far = [x for x in need if topo.die(x[0]) != topo.die(src)]
        for dst, t in need:
            for part in range(2):
                if (dst, t) in far[1:] and (part or t > 2):
                    plan[far[0][0]].append((t, far[0][1], part, dst))
                else:
                    plan[src].append((t, 0, part, dst))
    return {c: sorted(plan[c]) for c in plan}


def rank_program(g, core, T, topo):
    if T.rank_of(core) is None:
        return
    sem = T.sem
    plan = routes(T, topo)
    arrive = {"arr%d%s" % (t, "ab"[part]): len(topo.engines(c, core)) for c in plan for t, s, part, dst in plan[c] if dst == core}
    g.sync.dma_start(T.cqs[:], T.cq[:]).then_inc(sem.dcq, 16)
    g.scalar.dma_start(T.pts[:], T.pt[:]).then_inc(sem.dpt, 16)
    g.scalar.dma_start(T.ths[0:8, 0:2], T.th[:]).then_inc(sem.dth, 16)
    g.sync.wait_ge(sem.dcq, 16)
    g.sync.dma_start(T.XL0[:, 0:4096], T.xs[:]).then_inc(sem.dxs, 16)
    g.sync.dma_start(T.XL0[:, 4096:8192], T.lim[:]).then_inc(sem.dlim, 16)

    left = [0]

    def send(k):
        for j in ([k], range(2, len(plan[core])), [])[max(0, min(k - 1, 2))]:
            t, s, part, dst = plan[core][j]
            if j and plan[core][j - 1][:2] != (t, s):
                g.wait_ge(sem.sent, left[0])
            if s:
                g.wait_ge(sem["arr%d%s" % (s, "ab"[part])], arrive["arr%d%s" % (s, "ab"[part])])
            (lo, hi), (rid, pid, _) = PARTS[part], topo.addr(dst)
            g.remote_dma(T["XL%d" % t][:, lo:hi], T["XL%d" % s][:, lo:hi], sem["arr%d%s" % (t, "ab"[part])], sem.sent, pid, rid,
                         topo.mask(core, dst))
            left[0] += len(topo.engines(core, dst))

    ops = build(g, T, send)
    if "plan" not in CACHE:
        CACHE["plan"] = schedule(ops)
    order, deps, eng = CACHE["plan"]
    Q = {"V": g.vector, "S": g.scalar, "P": g.tensor, "G": g}
    SM = {"V": sem.sV, "S": sem.sS, "P": sem.sP, "G": sem.sG}
    count = {"V": 0, "S": 0, "P": 0, "G": 0}
    mark = {}
    wrote = []

    known = {e: {} for e in Q}
    after = {}

    def wait(e, name, s, v):
        if known[e].get(name, 0) < v:
            Q[e].wait_ge(s, v)
            known[e][name] = v
            for k, x in after.get((name, v), {}).items():
                known[e][k] = max(known[e].get(k, 0), x)

    def ready(q, x):
        need = {}
        for y, e, c in wrote:
            if y[0] == x[0] and meet(x, y):
                need[e] = max(need.get(e, 0), c)
        for e in need:
            q.wait_ge(SM[e], need[e])

    for i in order:
        o = ops[i]
        e = eng[i]
        for x in o["r"]:
            s = outside(x)
            if s:
                wait(e, s, sem[s], arrive.get(s, 16))
        need = {}
        for d in deps[i]:
            de = eng[d]
            if "late" in ops[d] or de == "P" and e == "P" or de == "G" and "late" in o:
                continue
            need[de] = max(need.get(de, 0), mark[d])
        for de in sorted(need, key=lambda x: x == e):
            wait(e, de, SM[de], need[de])
        ins = (o["f"] if e == o["e"] else o["alt"][2])()
        if "late" in o:
            continue
        count[e] += 1
        ins.then_inc(SM[e], 1)
        mark[i] = count[e]
        after[(e, count[e])] = dict(known[e])
        for x in o["w"]:
            if x[0] in ("OP", "OC"):
                wrote.append((x, e, count[e]))

    g.wait_ge(sem.sent, left[0])
    ready(g.sync, r("OP"))
    g.sync.dma_start(T.yp[:], T.OP[:]).then_inc(sem.dout, 16)
    last = 2 * PIECES[3][-1][0]
    for q, lo, hi in ((g.sync, 0, last), (g.scalar, last, 512)):
        ready(q, r("OC", lo, hi))
        q.dma_start(T.yc[:, lo:hi], T.OC[:, lo:hi]).then_inc(sem.dout, 16)
    g.sync.wait_ge(sem.dout, 48)
    for e in count:
        g.sync.wait_ge(SM[e], count[e])
